import numpy as np
import ml_dtypes


def mxq(x, axis, fmt="e4m3"):
    dtype, down = {"e4m3": (ml_dtypes.float8_e4m3fn, 7), "e5m2": (ml_dtypes.float8_e5m2, 14)}[fmt]
    v = np.moveaxis(np.asarray(x, np.float32).astype(ml_dtypes.bfloat16).astype(np.float64), axis, -1)
    blocks = v.reshape(v.shape[:-1] + (-1, 32))
    amax = np.abs(blocks).max(-1, keepdims=True)
    byte = np.maximum(np.where(amax > 0, np.frexp(amax)[1] - 1 + 127, 0) - down, 1)
    scale = np.exp2(byte - 127.0)
    codes = (blocks / scale).astype(np.float32).astype(dtype).astype(np.float64)
    return np.moveaxis((codes * scale).reshape(v.shape), -1, axis)


WIDE = False


def mx_kscale(k):
    if not WIDE:
        return np.ones(k)
    levels = np.array([18, -18])
    if k % 512:
        return np.exp2(np.random.permutation(np.resize(levels, k // 32))).repeat(32)
    a = np.empty((k // 512, 16))
    for p in range(k // 512):
        a[p, :8] = np.random.permutation(np.resize(levels, 8))
        for g in range(8):
            far = levels[np.abs(levels - a[p, g]) >= 10]
            a[p, g + 8] = far[np.random.randint(len(far))]
    return np.exp2(a.ravel()).repeat(32)


def f64(x):
    return np.asarray(x).astype(np.float64)


def striped(idx):
    return np.tile(np.asarray(idx).reshape(-1, 16).T, (8, 1)).astype(np.uint16)


def unstriped(offs):
    return offs[:16].T.reshape(-1).astype(np.int64)


def setup_inputs():
    n = np.random.standard_normal
    uni = np.random.uniform
    idx = np.random.permutation(2048)[:1024]
    doc = np.random.permutation(np.repeat(np.arange(512), 2))
    slot = np.argsort(doc, kind="stable")
    f_d = mx_kscale(512)
    f_r = mx_kscale(512)
    return {
        "qT": (0.5 * n((512, 512)) * f_d[:, None] * f_r[None, :]).astype(np.float32),
        "wT": (n((512, 2048)) / np.sqrt(512) / f_d[:, None]).astype(np.float32),
        "us": (uni(0.75, 1.3, (512, 1)) / f_r[:, None]).astype(np.float32),
        "ts": np.tile(uni(0.75, 1.3, 2048), (128, 1)).astype(np.float32),
        "G": (n((512, 512))).astype(np.float32),
        "wt": (uni(0.75, 1.3, (512, 1)) / np.sqrt(512)).astype(np.float32),
        "offs": striped(idx),
        "docoffs": striped(doc),
        "slotoffs": striped(slot),
    }


def reference(qT, wT, us, ts, G, wt, offs, docoffs, slotoffs):
    idx = unstriped(offs)
    doc = unstriped(docoffs)
    slot = unstriped(slotoffs)
    wT_c = f64(wT)[:, idx]
    ts_c = f64(ts)[:1][:, idx]
    a = mxq(f64(qT), 0, "e4m3").T @ mxq(wT_c, 0, "e4m3")
    e = np.exp(f64(us) * ts_c * a)
    es = e[:, slot]
    s = es.reshape(512, 512, 2).sum(-1)
    h = f64(G) / s
    hc = h[:, doc]
    g = f64(wt) * f64(us) * ts_c * e * hc
    dw = mxq(f64(qT), 1, "e4m3") @ mxq(g, 0, "e5m2")
    out = np.zeros((512, 2048))
    out[:, idx] = dw
    return out

@@ -1,0 +1,275 @@
+from contextlib import ExitStack
+
+import concourse.mybir as mybir
+from concourse.masks import make_identity
+
+D, R, C, T, X = 512, 512, 1024, 2048, 512
+FLOPS = 2 * 2 * D * R * C
+
+F32 = mybir.dt.float32
+BF16 = mybir.dt.bfloat16
+U32 = mybir.dt.uint32
+U16 = mybir.dt.uint16
+U8 = mybir.dt.uint8
+I32 = mybir.dt.int32
+E4M3 = mybir.dt.float8_e4m3fn_x4
+E5M2 = mybir.dt.float8_e5m2_x4
+ACT = mybir.ActivationFunctionType
+MULT = mybir.AluOpType.mult
+
+P = 128
+PACK = 4
+HALF = 512
+LIST_COLS = HALF // 16
+W_CHUNK = 512
+H_COLS = X + P
+
+
+def tile_attend_gcolb_kernel(tc, qT, wT, us, ts, G, wt, offs, docoffs, slotoffs, out):
+    nc = tc.nc
+    halves = range(C // HALF)
+    r_tiles = range(R // P)
+
+    def half_list(tile, h):
+        return tile[:, h * LIST_COLS : (h + 1) * LIST_COLS]
+
+    with ExitStack() as ctx:
+        keep = ctx.enter_context(tc.tile_pool(name="keep", bufs=1))
+        stage = ctx.enter_context(tc.tile_pool(name="stage", bufs=1))
+        ring = ctx.enter_context(tc.tile_pool(name="ring", bufs=2))
+        psum = ctx.enter_context(tc.psum_pool(name="psum", bufs=1))
+
+        def bank_tile(n, shape, name):
+            return psum.tile(shape, F32, name=name, tag="bank%d" % n)
+
+        idx = keep.tile([P, C // 16], U16, name="idx")
+        nc.sync.dma_start(idx[:], offs)
+
+        ts_win = keep.tile([P, T], F32, name="ts_win")
+        nc.vector.memset(ts_win[:].bitcast(I32), 0)
+        nc.sync.dma_start(ts_win[0:1, :], ts[0:1, :])
+
+        ident = keep.tile([P, P], F32, name="ident")
+        make_identity(nc, ident[:])
+        uw_rows = keep.tile([P, P], F32, name="uw_rows")
+        nc.gpsimd.memset(uw_rows[:], 0.0)
+        nc.sync.dma_start(uw_rows[0:4, :], us.rearrange("(j p) o -> j (p o)", p=P))
+        nc.sync.dma_start(uw_rows[4:8, :], wt.rearrange("(j p) o -> j (p o)", p=P))
+
+        w_rows = wT.rearrange("(p j) t -> p j t", j=PACK)
+        w_win = []
+        n_chunks = T // W_CHUNK
+        for u in range(2):
+            win = keep.tile([P, T], U32, name="w_win%d" % u)
+            win_pairs = win[:].bitcast(BF16).rearrange("p (t e) -> p t e", e=2)
+            for n in range(n_chunks):
+                cols = slice(n * W_CHUNK, (n + 1) * W_CHUNK)
+                raw = stage.tile([P, 2, W_CHUNK], F32, name="w_raw", tag="stage%d" % (u * n_chunks + n))
+                nc.sync.dma_start(raw[:], w_rows[:, 2 * u : 2 * u + 2, cols])
+                src = raw[:].rearrange("p e t -> p t e")
+                if u == 1 and n == n_chunks - 1:
+                    nc.vector.tensor_copy(win_pairs[:, cols, :], src)
+                else:
+                    nc.scalar.activation(win_pairs[:, cols, :], src, ACT.Copy)
+            w_win.append(win)
+
+        q_rows = qT.rearrange("(p j) r -> p j r", j=PACK)
+        q_raw = keep.tile([P, PACK, R], F32, name="q_raw")
+        nc.sync.dma_start(q_raw[:, :, 0:P], q_rows[:, :, 0:P])
+        nc.sync.dma_start(q_raw[:, :, P:R], q_rows[:, :, P:R])
+        slot = keep.tile([P, C // 16], U16, name="slot")
+        nc.sync.dma_start(slot[:], slotoffs)
+        g_in = keep.tile([P, R // P, X], F32, name="g_in")
+        nc.sync.dma_start(g_in[:], G.rearrange("(j p) x -> p j x", p=P))
+        doc = keep.tile([P, C // 16], U16, name="doc")
+        nc.sync.dma_start(doc[:], docoffs)
+
+        w_codes = keep.tile([P, C], U32, name="w_codes", align_bytes=64)
+        w_scales = keep.tile([P, C], U8, name="w_scales", align_bytes=64)
+        w_grouped = [keep.tile([P, HALF * PACK], BF16, name="w_grouped%d" % h, align_bytes=64) for h in halves]
+
+        def gather_w(u, h):
+            words = w_grouped[h][:].bitcast(U32).rearrange("p (c u) -> p c u", u=2)
+            nc.vector.tensor_copy(words[:, :, u], w_win[u][:].indirect(half_list(idx, h)))
+
+        for h in halves:
+            gather_w(0, h)
+
+        ts_row = keep.tile([P, C], F32, name="ts_row")
+        nc.vector.tensor_copy(ts_row[:], ts_win[:].indirect(idx[:]))
+        ts_col = stage.tile([P, C // P], F32, name="ts_col", tag="stage6")
+        ts_all = keep.tile([P, C], F32, name="ts_all")
+        for h in halves:
+            bank = bank_tile(4 + h, [P, PACK, P], "ts_turned")
+            for b in range(PACK):
+                k = PACK * h + b
+                nc.tensor.transpose(bank[:, b, :], ts_row[:, k * P : (k + 1) * P], ident[:])
+            nc.scalar.copy(ts_col[:, PACK * h : PACK * (h + 1)], bank[:, :, 0])
+        for h in halves:
+            bank = bank_tile(6 + h, [P, PACK, P], "ts_spread")
+            for b in range(PACK):
+                k = PACK * h + b
+                nc.tensor.transpose(bank[:, b, :], ts_col[:, k : k + 1].to_broadcast([P, P]), ident[:])
+            nc.scalar.copy(ts_all[:, h * HALF : (h + 1) * HALF], bank[:].rearrange("p b c -> p (b c)"))
+
+        uw_bank = bank_tile(0, [P, PACK, P], "uw_bank")
+        nc.tensor.transpose(uw_bank[:, 0, :], uw_rows[:], ident[:])
+        uw = keep.tile([P, 8], F32, name="uw")
+        nc.vector.tensor_copy(uw[:], uw_bank[:, 0, 0:8])
+        wtus = keep.tile([P, 4], F32, name="wtus")
+        nc.vector.tensor_tensor(wtus[:], uw[:, 0:4], uw[:, 4:8], MULT)
+
+        qa_codes = keep.tile([P, R], U32, name="qa_codes", align_bytes=64)
+        qa_scales = keep.tile([P, R], U8, name="qa_scales", align_bytes=64)
+        qa = keep.tile([P, R * PACK], BF16, name="qa", align_bytes=64)
+
+        def group_qa(j):
+            nc.scalar.activation(
+                qa[:, j * P * PACK : (j + 1) * P * PACK].rearrange("p (r i t) -> p r t i", i=4, t=PACK),
+                q_raw[:, :, j * P : (j + 1) * P].rearrange("p t (r i) -> p r t i", i=4),
+                ACT.Copy,
+            )
+
+        def quantize_qa(j):
+            cols = slice(j * P, (j + 1) * P)
+            nc.vector.quantize_mx(qa_codes[:, cols].bitcast(E4M3), qa_scales[:, cols], qa[:, j * P * PACK : (j + 1) * P * PACK])
+
+        group_qa(0)
+        for h in halves:
+            cols = slice(h * HALF, (h + 1) * HALF)
+            gather_w(1, h)
+            if h == 0:
+                quantize_qa(0)
+            nc.vector.quantize_mx(w_codes[:, cols].bitcast(E4M3), w_scales[:, cols], w_grouped[h][:])
+        for j in r_tiles[1:]:
+            group_qa(j)
+            quantize_qa(j)
+
+        e = []
+        for j in r_tiles:
+            rows = slice(j * P, (j + 1) * P)
+            e_j = keep.tile([P, C], F32, name="e%d" % j)
+            for h in halves:
+                cols = slice(h * HALF, (h + 1) * HALF)
+                a = bank_tile((2 * j + h) % 4, [P, HALF], "a")
+                nc.tensor.matmul_mx(
+                    a[:],
+                    lhsT=qa_codes[:, rows].bitcast(E4M3),
+                    lhsT_scale=qa_scales[:, rows],
+                    rhs=w_codes[:, cols].bitcast(E4M3),
+                    rhs_scale=w_scales[:, cols],
+                    start=True,
+                    stop=True,
+                )
+                z = ring.tile([P, HALF], F32, name="z", tag="z", bufs=4)
+                nc.vector.tensor_tensor(z[:], a[:], ts_all[:, cols], MULT)
+                nc.scalar.activation(e_j[:, cols], z[:], ACT.Exp, scale=uw[:, j : j + 1])
+            e.append(e_j)
+
+        h_win = []
+        ew = []
+        for j in r_tiles:
+            es = ring.tile([P, C], F32, name="es", tag="es")
+            for h in halves:
+                nc.vector.tensor_copy(es[:, h * HALF : (h + 1) * HALF], e[j][:].indirect(half_list(slot, h)))
+            s_turned = bank_tile(4 + j % 2, [P, PACK, P], "s_turned")
+            for b in range(X // P):
+                for u in range(2):
+                    nc.tensor.matmul(
+                        s_turned[:, b, :],
+                        es[:, 2 * P * b + u : 2 * P * (b + 1) : 2],
+                        ident[:],
+                        start=(u == 0),
+                        stop=(u == 1),
+                        is_transpose=True,
+                    )
+            root = stage.tile([P, X], F32, name="root", tag="stage%d" % j)
+            nc.scalar.activation(root[:], s_turned[:].rearrange("p b r -> p (b r)"), ACT.Abs_reciprocal_sqrt)
+            inv_turned = ring.tile([P, X], F32, name="inv_turned", tag="inv_turned")
+            nc.scalar.activation(inv_turned[:], root[:], ACT.Square)
+            inv = bank_tile(6 + j % 2, [P, X], "inv")
+            for b in range(X // P):
+                nc.tensor.transpose(inv[:, b * P : (b + 1) * P], inv_turned[:, b * P : (b + 1) * P], ident[:])
+            h_j = keep.tile([P, H_COLS], F32, name="h%d" % j)
+            nc.gpsimd.memset(h_j[:, X:H_COLS], 0.0)
+            nc.vector.tensor_tensor(h_j[:, 0:X], inv[:], g_in[:, j, :], MULT)
+            h_win.append(h_j)
+            ew_j = stage.tile([P, C], F32, name="ew", tag="stage%d" % j)
+            nc.scalar.activation(ew_j[:], e[j][:], ACT.Copy, scale=wtus[:, j : j + 1])
+            ew.append(ew_j)
+
+        qb = keep.tile([P, D * PACK], BF16, name="qb", align_bytes=64)
+        for j in range(PACK):
+            bank = bank_tile(j, [P, PACK, P], "q_turned")
+            for t in range(PACK):
+                nc.tensor.transpose(bank[:, t, :], q_raw[:, j, t:R:PACK], ident[:])
+            nc.scalar.activation(
+                qb[:, j * P * PACK : (j + 1) * P * PACK].rearrange("p (d t) -> p d t", t=PACK),
+                bank[:].rearrange("p t d -> p d t"),
+                ACT.Copy,
+            )
+        qb_codes = keep.tile([P, D], U32, name="qb_codes", align_bytes=64)
+        qb_scales = keep.tile([P, D], U8, name="qb_scales", align_bytes=64)
+        nc.vector.quantize_mx(qb_codes[:].bitcast(E4M3), qb_scales[:], qb[:])
+
+        m_first = [ring.tile([P, HALF], F32, name="m_first", tag="m_first", bufs=4) for j in r_tiles]
+        m = [[tile[:] for tile in m_first], [ew[3][:, 0:HALF]] + [ew[j][:, HALF:C] for j in r_tiles[:-1]]]
+        for h in halves:
+            cols = slice(h * HALF, (h + 1) * HALF)
+            for j in r_tiles:
+                nc.vector.tensor_tensor(m[h][j], h_win[j][:].indirect(half_list(doc, h)), ew[j][:, cols], MULT)
+
+        out_win = []
+        for j in range(PACK):
+            win = keep.tile([P, T], F32, name="out_win%d" % j)
+            nc.vector.memset(win[:].bitcast(I32), 0)
+            out_win.append(win)
+        out_rows = out.rearrange("(p j) t -> p j t", j=PACK)
+
+        def quantize_g(h, turn_banks):
+            g_grouped = ring.tile([P, HALF * PACK], BF16, name="g_grouped", tag="g_grouped", align_bytes=64)
+            g_words = g_grouped[:].bitcast(F32).rearrange("p (b c u) -> p b c u", c=P, u=2)
+            for pair in range(2):
+                words_bank = bank_tile(4 + pair, [P, 2, 2, P], "words_bank")
+                for b in range(2):
+                    block = 2 * pair + b
+                    bank = bank_tile(turn_banks[block], [P, R], "m_turned")
+                    for j in r_tiles:
+                        nc.tensor.transpose(bank[:, j * P : (j + 1) * P], m[h][j][:, block * P : (block + 1) * P], ident[:])
+                    g_turned = ring.tile([P, R], BF16, name="g_turned", tag="g_turned", bufs=4)
+                    k = PACK * h + block
+                    nc.scalar.activation(g_turned[:], bank[:], ACT.Copy, scale=ts_col[:, k : k + 1])
+                    words = g_turned[:].bitcast(F32)
+                    for u in range(2):
+                        nc.tensor.transpose(words_bank[:, b, u, :], words[:, u : R // 2 : 2], ident[:])
+                nc.scalar.copy(g_words[:, 2 * pair : 2 * pair + 2], words_bank[:].rearrange("p b u c -> p b c u"))
+            g_codes = ring.tile([P, HALF], U32, name="g_codes", tag="g_codes", align_bytes=64)
+            g_scales = ring.tile([P, HALF], U8, name="g_scales", tag="g_scales", align_bytes=64)
+            nc.vector.quantize_mx(g_codes[:].bitcast(E5M2), g_scales[:], g_grouped[:])
+            return g_codes, g_scales
+
+        def put_dw(h, j, g_mx, n):
+            rows = slice(j * P, (j + 1) * P)
+            dw_bank = bank_tile(n, [P, HALF], "dw_bank")
+            nc.tensor.matmul_mx(
+                dw_bank[:],
+                lhsT=qb_codes[:, rows].bitcast(E4M3),
+                lhsT_scale=qb_scales[:, rows],
+                rhs=g_mx[0][:].bitcast(E5M2),
+                rhs_scale=g_mx[1][:],
+                start=True,
+                stop=True,
+            )
+            dw = ring.tile([P, HALF], F32, name="dw", tag="dw", bufs=4)
+            nc.scalar.copy(dw[:], dw_bank[:])
+            nc.vector.tensor_copy(out_win[j][:].indirect(half_list(idx, h)), dw[:])
+            if h == halves[-1]:
+                nc.sync.dma_start(out_rows[:, j, :], out_win[j][:])
+
+        g_first = quantize_g(0, [0, 1, 2, 3])
+        for j in range(3):
+            put_dw(0, j, g_first, j)
+        g_second = quantize_g(1, [0, 1, 2, 0])
+        put_dw(0, 3, g_first, 5)
+        for j in range(PACK):
+            put_dw(1, j, g_second, j)

@@ -11,11 +11,11 @@ BF16 = mybir.dt.bfloat16
 U32 = mybir.dt.uint32
 U16 = mybir.dt.uint16
 U8 = mybir.dt.uint8
-I32 = mybir.dt.int32
 E4M3 = mybir.dt.float8_e4m3fn_x4
 E5M2 = mybir.dt.float8_e5m2_x4
 ACT = mybir.ActivationFunctionType
 MULT = mybir.AluOpType.mult
+ADD = mybir.AluOpType.add
 
 P = 128
 PACK = 4
@@ -46,15 +46,13 @@ def tile_attend_gcolb_kernel(tc, qT, wT, us, ts, G, wt, offs, docoffs, slotoffs,
         nc.sync.dma_start(idx[:], offs)
 
         ts_win = keep.tile([P, T], F32, name="ts_win")
-        nc.vector.memset(ts_win[:].bitcast(I32), 0)
+        nc.gpsimd.memset(ts_win[:], 0.0)
         nc.sync.dma_start(ts_win[0:1, :], ts[0:1, :])
 
         ident = keep.tile([P, P], F32, name="ident")
         make_identity(nc, ident[:])
         uw_rows = keep.tile([P, P], F32, name="uw_rows")
         nc.gpsimd.memset(uw_rows[:], 0.0)
-        nc.sync.dma_start(uw_rows[0:4, :], us.rearrange("(j p) o -> j (p o)", p=P))
-        nc.sync.dma_start(uw_rows[4:8, :], wt.rearrange("(j p) o -> j (p o)", p=P))
 
         w_rows = wT.rearrange("(p j) t -> p j t", j=PACK)
         w_win = []
@@ -76,6 +74,8 @@ def tile_attend_gcolb_kernel(tc, qT, wT, us, ts, G, wt, offs, docoffs, slotoffs,
         q_rows = qT.rearrange("(p j) r -> p j r", j=PACK)
         q_raw = keep.tile([P, PACK, R], F32, name="q_raw")
         nc.sync.dma_start(q_raw[:, :, 0:P], q_rows[:, :, 0:P])
+        nc.sync.dma_start(uw_rows[0:4, :], us.rearrange("(j p) o -> j (p o)", p=P))
+        nc.sync.dma_start(uw_rows[4:8, :], wt.rearrange("(j p) o -> j (p o)", p=P))
         nc.sync.dma_start(q_raw[:, :, P:R], q_rows[:, :, P:R])
         slot = keep.tile([P, C // 16], U16, name="slot")
         nc.sync.dma_start(slot[:], slotoffs)
@@ -97,8 +97,8 @@ def tile_attend_gcolb_kernel(tc, qT, wT, us, ts, G, wt, offs, docoffs, slotoffs,
 
         ts_row = keep.tile([P, C], F32, name="ts_row")
         nc.vector.tensor_copy(ts_row[:], ts_win[:].indirect(idx[:]))
-        ts_col = stage.tile([P, C // P], F32, name="ts_col", tag="stage6")
-        ts_all = keep.tile([P, C], F32, name="ts_all")
+        ts_col = keep.tile([P, C // P], F32, name="ts_col")
+        ts_all = stage.tile([P, C], F32, name="ts_all", tag="stage6")
         for h in halves:
             bank = bank_tile(4 + h, [P, PACK, P], "ts_turned")
             for b in range(PACK):
@@ -146,6 +146,7 @@ def tile_attend_gcolb_kernel(tc, qT, wT, us, ts, G, wt, offs, docoffs, slotoffs,
             quantize_qa(j)
 
         e = []
+        ew = []
         for j in r_tiles:
             rows = slice(j * P, (j + 1) * P)
             e_j = keep.tile([P, C], F32, name="e%d" % j)
@@ -165,9 +166,11 @@ def tile_attend_gcolb_kernel(tc, qT, wT, us, ts, G, wt, offs, docoffs, slotoffs,
                 nc.vector.tensor_tensor(z[:], a[:], ts_all[:, cols], MULT)
                 nc.scalar.activation(e_j[:, cols], z[:], ACT.Exp, scale=uw[:, j : j + 1])
             e.append(e_j)
+            ew_j = stage.tile([P, C], F32, name="ew", tag="stage%d" % j)
+            nc.gpsimd.tensor_scalar(ew_j[:], e_j[:], wtus[:, j : j + 1], 0.0, MULT, ADD)
+            ew.append(ew_j)
 
         h_win = []
-        ew = []
         for j in r_tiles:
             es = ring.tile([P, C], F32, name="es", tag="es")
             for h in halves:
@@ -183,20 +186,18 @@ def tile_attend_gcolb_kernel(tc, qT, wT, us, ts, G, wt, offs, docoffs, slotoffs,
                         stop=(u == 1),
                         is_transpose=True,
                     )
-            root = stage.tile([P, X], F32, name="root", tag="stage%d" % j)
-            nc.scalar.activation(root[:], s_turned[:].rearrange("p b r -> p (b r)"), ACT.Abs_reciprocal_sqrt)
-            inv_turned = ring.tile([P, X], F32, name="inv_turned", tag="inv_turned")
-            nc.scalar.activation(inv_turned[:], root[:], ACT.Square)
-            inv = bank_tile(6 + j % 2, [P, X], "inv")
+            root_turned = ring.tile([P, X], F32, name="root_turned", tag="root_turned")
+            nc.scalar.activation(root_turned[:], s_turned[:].rearrange("p b r -> p (b r)"), ACT.Abs_reciprocal_sqrt)
+            root = bank_tile(6 + j % 2, [P, X], "root")
             for b in range(X // P):
-                nc.tensor.transpose(inv[:, b * P : (b + 1) * P], inv_turned[:, b * P : (b + 1) * P], ident[:])
+                nc.tensor.transpose(root[:, b * P : (b + 1) * P], root_turned[:, b * P : (b + 1) * P], ident[:])
+            inv = ring.tile([P, X], F32, name="inv", tag="inv")
+            nc.scalar.activation(inv[:], root[:], ACT.Square)
             h_j = keep.tile([P, H_COLS], F32, name="h%d" % j)
             nc.gpsimd.memset(h_j[:, X:H_COLS], 0.0)
-            nc.vector.tensor_tensor(h_j[:, 0:X], inv[:], g_in[:, j, :], MULT)
+            engine = nc.gpsimd if j < 2 else nc.vector
+            engine.tensor_tensor(h_j[:, 0:X], inv[:], g_in[:, j, :], MULT)
             h_win.append(h_j)
-            ew_j = stage.tile([P, C], F32, name="ew", tag="stage%d" % j)
-            nc.scalar.activation(ew_j[:], e[j][:], ACT.Copy, scale=wtus[:, j : j + 1])
-            ew.append(ew_j)
 
         qb = keep.tile([P, D * PACK], BF16, name="qb", align_bytes=64)
         for j in range(PACK):
@@ -213,21 +214,26 @@ def tile_attend_gcolb_kernel(tc, qT, wT, us, ts, G, wt, offs, docoffs, slotoffs,
         nc.vector.quantize_mx(qb_codes[:].bitcast(E4M3), qb_scales[:], qb[:])
 
         m_first = [ring.tile([P, HALF], F32, name="m_first", tag="m_first", bufs=4) for j in r_tiles]
-        m = [[tile[:] for tile in m_first], [ew[3][:, 0:HALF]] + [ew[j][:, HALF:C] for j in r_tiles[:-1]]]
-        for h in halves:
+        m = [[tile[:] for tile in m_first], [ew[3][:, 0:HALF], ew[0][:, HALF:C], ew[1][:, HALF:C]]]
+
+        def gather_h(h, j):
             cols = slice(h * HALF, (h + 1) * HALF)
-            for j in r_tiles:
-                nc.vector.tensor_tensor(m[h][j], h_win[j][:].indirect(half_list(doc, h)), ew[j][:, cols], MULT)
+            nc.vector.tensor_tensor(m[h][j], h_win[j][:].indirect(half_list(doc, h)), ew[j][:, cols], MULT)
+
+        for j in r_tiles:
+            gather_h(0, j)
+        for j in r_tiles[:-1]:
+            gather_h(1, j)
 
         out_win = []
         for j in range(PACK):
             win = keep.tile([P, T], F32, name="out_win%d" % j)
-            nc.vector.memset(win[:].bitcast(I32), 0)
+            nc.gpsimd.memset(win[:], 0.0)
             out_win.append(win)
         out_rows = out.rearrange("(p j) t -> p j t", j=PACK)
 
         def quantize_g(h, turn_banks):
-            g_grouped = ring.tile([P, HALF * PACK], BF16, name="g_grouped", tag="g_grouped", align_bytes=64)
+            g_grouped = keep.tile([P, HALF * PACK], BF16, name="g_grouped", tag="g_grouped%d" % h, align_bytes=64)
             g_words = g_grouped[:].bitcast(F32).rearrange("p (b c u) -> p b c u", c=P, u=2)
             for pair in range(2):
                 words_bank = bank_tile(4 + pair, [P, 2, 2, P], "words_bank")
@@ -267,6 +273,9 @@ def tile_attend_gcolb_kernel(tc, qT, wT, us, ts, G, wt, offs, docoffs, slotoffs,
                 nc.sync.dma_start(out_rows[:, j, :], out_win[j][:])
 
         g_first = quantize_g(0, [0, 1, 2, 3])
+        m_last = keep.tile([P, HALF], F32, name="m_last", tag="g_grouped0", align_bytes=64)
+        m[1].append(m_last[:])
+        gather_h(1, 3)
         for j in range(3):
             put_dw(0, j, g_first, j)
         g_second = quantize_g(1, [0, 1, 2, 0])

@@ -11,11 +11,11 @@ BF16 = mybir.dt.bfloat16
 U32 = mybir.dt.uint32
 U16 = mybir.dt.uint16
 U8 = mybir.dt.uint8
+I32 = mybir.dt.int32
 E4M3 = mybir.dt.float8_e4m3fn_x4
 E5M2 = mybir.dt.float8_e5m2_x4
 ACT = mybir.ActivationFunctionType
 MULT = mybir.AluOpType.mult
-ADD = mybir.AluOpType.add
 
 P = 128
 PACK = 4
@@ -46,8 +46,14 @@ def tile_attend_gcolb_kernel(tc, qT, wT, us, ts, G, wt, offs, docoffs, slotoffs,
         nc.sync.dma_start(idx[:], offs)
 
         ts_win = keep.tile([P, T], F32, name="ts_win")
-        nc.gpsimd.memset(ts_win[:], 0.0)
+        nc.vector.memset(ts_win[:].bitcast(I32), 0)
         nc.sync.dma_start(ts_win[0:1, :], ts[0:1, :])
+
+        out_win = []
+        for j in range(PACK):
+            win = keep.tile([P, T], F32, name="out_win%d" % j)
+            nc.vector.memset(win[:].bitcast(I32), 0)
+            out_win.append(win)
 
         ident = keep.tile([P, P], F32, name="ident")
         make_identity(nc, ident[:])
@@ -146,7 +152,6 @@ def tile_attend_gcolb_kernel(tc, qT, wT, us, ts, G, wt, offs, docoffs, slotoffs,
             quantize_qa(j)
 
         e = []
-        ew = []
         for j in r_tiles:
             rows = slice(j * P, (j + 1) * P)
             e_j = keep.tile([P, C], F32, name="e%d" % j)
@@ -162,17 +167,23 @@ def tile_attend_gcolb_kernel(tc, qT, wT, us, ts, G, wt, offs, docoffs, slotoffs,
                     start=True,
                     stop=True,
                 )
-                z = ring.tile([P, HALF], F32, name="z", tag="z", bufs=4)
+                z = keep.tile([P, HALF], F32, name="z", tag="z%d" % ((2 * j + h) % 4))
                 nc.vector.tensor_tensor(z[:], a[:], ts_all[:, cols], MULT)
                 nc.scalar.activation(e_j[:, cols], z[:], ACT.Exp, scale=uw[:, j : j + 1])
             e.append(e_j)
-            ew_j = stage.tile([P, C], F32, name="ew", tag="stage%d" % j)
-            nc.gpsimd.tensor_scalar(ew_j[:], e_j[:], wtus[:, j : j + 1], 0.0, MULT, ADD)
-            ew.append(ew_j)
+
+        q_pairs = keep.tile([P, PACK * R], BF16, name="q_pairs", tag="z3")
+        nc.scalar.activation(
+            q_pairs[:].rearrange("p (u s e) -> p s u e", u=2, e=2),
+            q_raw[:].rearrange("p j (s u e) -> p (j s) u e", u=2, e=2),
+            ACT.Copy,
+        )
+        q_words = q_pairs[:].bitcast(F32).rearrange("p (u j s) -> p u j s", u=2, j=PACK)
 
         h_win = []
+        ew = []
         for j in r_tiles:
-            es = ring.tile([P, C], F32, name="es", tag="es")
+            es = ring.tile([P, C], F32, name="es", tag="es", bufs=3)
             for h in halves:
                 nc.vector.tensor_copy(es[:, h * HALF : (h + 1) * HALF], e[j][:].indirect(half_list(slot, h)))
             s_turned = bank_tile(4 + j % 2, [P, PACK, P], "s_turned")
@@ -186,29 +197,29 @@ def tile_attend_gcolb_kernel(tc, qT, wT, us, ts, G, wt, offs, docoffs, slotoffs,
                         stop=(u == 1),
                         is_transpose=True,
                     )
-            root_turned = ring.tile([P, X], F32, name="root_turned", tag="root_turned")
-            nc.scalar.activation(root_turned[:], s_turned[:].rearrange("p b r -> p (b r)"), ACT.Abs_reciprocal_sqrt)
-            root = bank_tile(6 + j % 2, [P, X], "root")
+            root = stage.tile([P, X], F32, name="root", tag="stage%d" % j)
+            nc.scalar.activation(root[:], s_turned[:].rearrange("p b r -> p (b r)"), ACT.Abs_reciprocal_sqrt)
+            inv_turned = ring.tile([P, X], F32, name="inv_turned", tag="inv_turned")
+            nc.scalar.activation(inv_turned[:], root[:], ACT.Square)
+            inv = bank_tile(6 + j % 2, [P, X], "inv")
             for b in range(X // P):
-                nc.tensor.transpose(root[:, b * P : (b + 1) * P], root_turned[:, b * P : (b + 1) * P], ident[:])
-            inv = ring.tile([P, X], F32, name="inv", tag="inv")
-            nc.scalar.activation(inv[:], root[:], ACT.Square)
+                nc.tensor.transpose(inv[:, b * P : (b + 1) * P], inv_turned[:, b * P : (b + 1) * P], ident[:])
             h_j = keep.tile([P, H_COLS], F32, name="h%d" % j)
             nc.gpsimd.memset(h_j[:, X:H_COLS], 0.0)
-            engine = nc.gpsimd if j < 2 else nc.vector
-            engine.tensor_tensor(h_j[:, 0:X], inv[:], g_in[:, j, :], MULT)
+            nc.vector.tensor_tensor(h_j[:, 0:X], inv[:], g_in[:, j, :], MULT)
             h_win.append(h_j)
+            ew_j = stage.tile([P, C], F32, name="ew", tag="stage%d" % j)
+            nc.scalar.activation(ew_j[:], e[j][:], ACT.Copy, scale=wtus[:, j : j + 1])
+            ew.append(ew_j)
 
         qb = keep.tile([P, D * PACK], BF16, name="qb", align_bytes=64)
-        for j in range(PACK):
-            bank = bank_tile(j, [P, PACK, P], "q_turned")
-            for t in range(PACK):
-                nc.tensor.transpose(bank[:, t, :], q_raw[:, j, t:R:PACK], ident[:])
-            nc.scalar.activation(
-                qb[:, j * P * PACK : (j + 1) * P * PACK].rearrange("p (d t) -> p d t", t=PACK),
-                bank[:].rearrange("p t d -> p d t"),
-                ACT.Copy,
-            )
+        qb_words = qb[:].bitcast(F32).rearrange("s (j p u) -> s j p u", p=P, u=2)
+        for pair in range(2):
+            bank = bank_tile(pair, [P, 2, 2, P], "q_turned")
+            for b in range(2):
+                for u in range(2):
+                    nc.tensor.transpose(bank[:, b, u, :], q_words[:, u, 2 * pair + b, :], ident[:])
+            nc.scalar.copy(qb_words[:, 2 * pair : 2 * pair + 2], bank[:].rearrange("s b u p -> s b p u"))
         qb_codes = keep.tile([P, D], U32, name="qb_codes", align_bytes=64)
         qb_scales = keep.tile([P, D], U8, name="qb_scales", align_bytes=64)
         nc.vector.quantize_mx(qb_codes[:].bitcast(E4M3), qb_scales[:], qb[:])
@@ -225,11 +236,6 @@ def tile_attend_gcolb_kernel(tc, qT, wT, us, ts, G, wt, offs, docoffs, slotoffs,
         for j in r_tiles[:-1]:
             gather_h(1, j)
 
-        out_win = []
-        for j in range(PACK):
-            win = keep.tile([P, T], F32, name="out_win%d" % j)
-            nc.gpsimd.memset(win[:], 0.0)
-            out_win.append(win)
         out_rows = out.rearrange("(p j) t -> p j t", j=PACK)
 
         def quantize_g(h, turn_banks):
@@ -244,10 +250,15 @@ def tile_attend_gcolb_kernel(tc, qT, wT, us, ts, G, wt, offs, docoffs, slotoffs,
                         nc.tensor.transpose(bank[:, j * P : (j + 1) * P], m[h][j][:, block * P : (block + 1) * P], ident[:])
                     g_turned = ring.tile([P, R], BF16, name="g_turned", tag="g_turned", bufs=4)
                     k = PACK * h + block
-                    nc.scalar.activation(g_turned[:], bank[:], ACT.Copy, scale=ts_col[:, k : k + 1])
+                    nc.scalar.activation(
+                        g_turned[:].rearrange("c (u s e) -> c s u e", u=2, e=2),
+                        bank[:].rearrange("c (s u e) -> c s u e", u=2, e=2),
+                        ACT.Copy,
+                        scale=ts_col[:, k : k + 1],
+                    )
                     words = g_turned[:].bitcast(F32)
                     for u in range(2):
-                        nc.tensor.transpose(words_bank[:, b, u, :], words[:, u : R // 2 : 2], ident[:])
+                        nc.tensor.transpose(words_bank[:, b, u, :], words[:, u * P : (u + 1) * P], ident[:])
                 nc.scalar.copy(g_words[:, 2 * pair : 2 * pair + 2], words_bank[:].rearrange("p b u c -> p b c u"))
             g_codes = ring.tile([P, HALF], U32, name="g_codes", tag="g_codes", align_bytes=64)
             g_scales = ring.tile([P, HALF], U8, name="g_scales", tag="g_scales", align_bytes=64)

@@ -49,16 +49,17 @@ def tile_attend_gcolb_kernel(tc, qT, wT, us, ts, G, wt, offs, docoffs, slotoffs,
         nc.vector.memset(ts_win[:].bitcast(I32), 0)
         nc.sync.dma_start(ts_win[0:1, :], ts[0:1, :])
 
-        out_win = []
-        for j in range(PACK):
-            win = keep.tile([P, T], F32, name="out_win%d" % j)
-            nc.vector.memset(win[:].bitcast(I32), 0)
-            out_win.append(win)
+        uw_rows = keep.tile([P, P], F32, name="uw_rows")
+        nc.gpsimd.memset(uw_rows[:], 0.0)
+        nc.sync.dma_start(uw_rows[0:4, :], us.rearrange("(j p) o -> j (p o)", p=P))
+        nc.sync.dma_start(uw_rows[4:8, :], wt.rearrange("(j p) o -> j (p o)", p=P))
+        slot = keep.tile([P, C // 16], U16, name="slot")
+        nc.sync.dma_start(slot[:], slotoffs)
+        doc = keep.tile([P, C // 16], U16, name="doc")
+        nc.sync.dma_start(doc[:], docoffs)
 
         ident = keep.tile([P, P], F32, name="ident")
         make_identity(nc, ident[:])
-        uw_rows = keep.tile([P, P], F32, name="uw_rows")
-        nc.gpsimd.memset(uw_rows[:], 0.0)
 
         w_rows = wT.rearrange("(p j) t -> p j t", j=PACK)
         w_win = []
@@ -80,26 +81,16 @@ def tile_attend_gcolb_kernel(tc, qT, wT, us, ts, G, wt, offs, docoffs, slotoffs,
         q_rows = qT.rearrange("(p j) r -> p j r", j=PACK)
         q_raw = keep.tile([P, PACK, R], F32, name="q_raw")
         nc.sync.dma_start(q_raw[:, :, 0:P], q_rows[:, :, 0:P])
-        nc.sync.dma_start(uw_rows[0:4, :], us.rearrange("(j p) o -> j (p o)", p=P))
-        nc.sync.dma_start(uw_rows[4:8, :], wt.rearrange("(j p) o -> j (p o)", p=P))
         nc.sync.dma_start(q_raw[:, :, P:R], q_rows[:, :, P:R])
-        slot = keep.tile([P, C // 16], U16, name="slot")
-        nc.sync.dma_start(slot[:], slotoffs)
         g_in = keep.tile([P, R // P, X], F32, name="g_in")
         nc.sync.dma_start(g_in[:], G.rearrange("(j p) x -> p j x", p=P))
-        doc = keep.tile([P, C // 16], U16, name="doc")
-        nc.sync.dma_start(doc[:], docoffs)
 
         w_codes = keep.tile([P, C], U32, name="w_codes", align_bytes=64)
         w_scales = keep.tile([P, C], U8, name="w_scales", align_bytes=64)
         w_grouped = [keep.tile([P, HALF * PACK], BF16, name="w_grouped%d" % h, align_bytes=64) for h in halves]
 
-        def gather_w(u, h):
-            words = w_grouped[h][:].bitcast(U32).rearrange("p (c u) -> p c u", u=2)
-            nc.vector.tensor_copy(words[:, :, u], w_win[u][:].indirect(half_list(idx, h)))
-
-        for h in halves:
-            gather_w(0, h)
+        w_pairs = keep.tile([P, 2 * C], U32, name="w_pairs", tag="w_pairs", align_bytes=64)
+        nc.vector.tensor_copy(w_pairs[:, 0:C], w_win[0][:].indirect(idx[:]))
 
         ts_row = keep.tile([P, C], F32, name="ts_row")
         nc.vector.tensor_copy(ts_row[:], ts_win[:].indirect(idx[:]))
@@ -110,7 +101,7 @@ def tile_attend_gcolb_kernel(tc, qT, wT, us, ts, G, wt, offs, docoffs, slotoffs,
             for b in range(PACK):
                 k = PACK * h + b
                 nc.tensor.transpose(bank[:, b, :], ts_row[:, k * P : (k + 1) * P], ident[:])
-            nc.scalar.copy(ts_col[:, PACK * h : PACK * (h + 1)], bank[:, :, 0])
+            nc.vector.tensor_copy(ts_col[:, PACK * h : PACK * (h + 1)], bank[:, :, 0])
         for h in halves:
             bank = bank_tile(6 + h, [P, PACK, P], "ts_spread")
             for b in range(PACK):
@@ -127,29 +118,35 @@ def tile_attend_gcolb_kernel(tc, qT, wT, us, ts, G, wt, offs, docoffs, slotoffs,
 
         qa_codes = keep.tile([P, R], U32, name="qa_codes", align_bytes=64)
         qa_scales = keep.tile([P, R], U8, name="qa_scales", align_bytes=64)
-        qa = keep.tile([P, R * PACK], BF16, name="qa", align_bytes=64)
 
-        def group_qa(j):
+        def group_qa(j, grouped):
             nc.scalar.activation(
-                qa[:, j * P * PACK : (j + 1) * P * PACK].rearrange("p (r i t) -> p r t i", i=4, t=PACK),
+                grouped.rearrange("p (r i t) -> p r t i", i=4, t=PACK),
                 q_raw[:, :, j * P : (j + 1) * P].rearrange("p t (r i) -> p r t i", i=4),
                 ACT.Copy,
             )
 
-        def quantize_qa(j):
+        def quantize_qa(j, grouped):
             cols = slice(j * P, (j + 1) * P)
-            nc.vector.quantize_mx(qa_codes[:, cols].bitcast(E4M3), qa_scales[:, cols], qa[:, j * P * PACK : (j + 1) * P * PACK])
+            nc.vector.quantize_mx(qa_codes[:, cols].bitcast(E4M3), qa_scales[:, cols], grouped)
 
-        group_qa(0)
+        qa_first = keep.tile([P, P * PACK], BF16, name="qa_first", align_bytes=64)
+        group_qa(0, qa_first[:])
+        for h in halves:
+            nc.vector.tensor_copy(w_pairs[:, C + h * HALF : C + (h + 1) * HALF], w_win[1][:].indirect(half_list(idx, h)))
+        quantize_qa(0, qa_first[:])
         for h in halves:
             cols = slice(h * HALF, (h + 1) * HALF)
-            gather_w(1, h)
-            if h == 0:
-                quantize_qa(0)
+            nc.scalar.copy(
+                w_grouped[h][:].bitcast(U32).rearrange("p (c u) -> p c u", u=2),
+                w_pairs[:].rearrange("p (u c) -> p c u", u=2)[:, cols, :],
+            )
             nc.vector.quantize_mx(w_codes[:, cols].bitcast(E4M3), w_scales[:, cols], w_grouped[h][:])
+        qa_rest = keep.tile([P, (R - P) * PACK], BF16, name="qa_rest", tag="w_pairs", align_bytes=64)
         for j in r_tiles[1:]:
-            group_qa(j)
-            quantize_qa(j)
+            grouped = qa_rest[:, (j - 1) * P * PACK : j * P * PACK]
+            group_qa(j, grouped)
+            quantize_qa(j, grouped)
 
         e = []
         for j in r_tiles:
@@ -209,7 +206,7 @@ def tile_attend_gcolb_kernel(tc, qT, wT, us, ts, G, wt, offs, docoffs, slotoffs,
             nc.vector.tensor_tensor(h_j[:, 0:X], inv[:], g_in[:, j, :], MULT)
             h_win.append(h_j)
             ew_j = stage.tile([P, C], F32, name="ew", tag="stage%d" % j)
-            nc.scalar.activation(ew_j[:], e[j][:], ACT.Copy, scale=wtus[:, j : j + 1])
+            nc.scalar.activation(ew_j[:, 0:HALF], e[j][:, 0:HALF], ACT.Copy, scale=wtus[:, j : j + 1])
             ew.append(ew_j)
 
         qb = keep.tile([P, D * PACK], BF16, name="qb", align_bytes=64)
@@ -224,18 +221,34 @@ def tile_attend_gcolb_kernel(tc, qT, wT, us, ts, G, wt, offs, docoffs, slotoffs,
         qb_scales = keep.tile([P, D], U8, name="qb_scales", align_bytes=64)
         nc.vector.quantize_mx(qb_codes[:].bitcast(E4M3), qb_scales[:], qb[:])
 
+        for j in r_tiles:
+            nc.scalar.activation(ew[j][:, HALF:C], e[j][:, HALF:C], ACT.Copy, scale=wtus[:, j : j + 1])
+
         m_first = [ring.tile([P, HALF], F32, name="m_first", tag="m_first", bufs=4) for j in r_tiles]
         m = [[tile[:] for tile in m_first], [ew[3][:, 0:HALF], ew[0][:, HALF:C], ew[1][:, HALF:C]]]
 
-        def gather_h(h, j):
-            cols = slice(h * HALF, (h + 1) * HALF)
-            nc.vector.tensor_tensor(m[h][j], h_win[j][:].indirect(half_list(doc, h)), ew[j][:, cols], MULT)
+        def gather_h(h, j, pieces=1):
+            width = HALF // pieces
+            for n in range(pieces):
+                first = h * HALF + n * width
+                nc.vector.tensor_tensor(
+                    m[h][j][:, n * width : (n + 1) * width],
+                    h_win[j][:].indirect(doc[:, first // 16 : (first + width) // 16]),
+                    ew[j][:, first : first + width],
+                    MULT,
+                )
 
-        for j in r_tiles:
+        for j in r_tiles[:-1]:
             gather_h(0, j)
+        gather_h(0, 3, pieces=2)
         for j in r_tiles[:-1]:
             gather_h(1, j)
 
+        out_win = []
+        for j in range(PACK):
+            win = keep.tile([P, T], F32, name="out_win%d" % j)
+            nc.vector.memset(win[:].bitcast(I32), 0)
+            out_win.append(win)
         out_rows = out.rearrange("(p j) t -> p j t", j=PACK)
 
         def quantize_g(h, turn_banks):

@@ -16,6 +16,7 @@ E4M3 = mybir.dt.float8_e4m3fn_x4
 E5M2 = mybir.dt.float8_e5m2_x4
 ACT = mybir.ActivationFunctionType
 MULT = mybir.AluOpType.mult
+ADD = mybir.AluOpType.add
 
 P = 128
 PACK = 4
@@ -183,24 +184,31 @@ def tile_attend_gcolb_kernel(tc, qT, wT, us, ts, G, wt, offs, docoffs, slotoffs,
             es = ring.tile([P, C], F32, name="es", tag="es", bufs=3)
             for h in halves:
                 nc.vector.tensor_copy(es[:, h * HALF : (h + 1) * HALF], e[j][:].indirect(half_list(slot, h)))
-            s_turned = bank_tile(4 + j % 2, [P, PACK, P], "s_turned")
-            for b in range(X // P):
-                for u in range(2):
-                    nc.tensor.matmul(
-                        s_turned[:, b, :],
-                        es[:, 2 * P * b + u : 2 * P * (b + 1) : 2],
-                        ident[:],
-                        start=(u == 0),
-                        stop=(u == 1),
-                        is_transpose=True,
-                    )
             root = stage.tile([P, X], F32, name="root", tag="stage%d" % j)
-            nc.scalar.activation(root[:], s_turned[:].rearrange("p b r -> p (b r)"), ACT.Abs_reciprocal_sqrt)
-            inv_turned = ring.tile([P, X], F32, name="inv_turned", tag="inv_turned")
-            nc.scalar.activation(inv_turned[:], root[:], ACT.Square)
-            inv = bank_tile(6 + j % 2, [P, X], "inv")
-            for b in range(X // P):
-                nc.tensor.transpose(inv[:, b * P : (b + 1) * P], inv_turned[:, b * P : (b + 1) * P], ident[:])
+            squared = ring.tile([P, X], F32, name="squared", tag="squared")
+            if j == r_tiles[-1]:
+                s = keep.tile([P, X], F32, name="s")
+                nc.vector.tensor_tensor(s[:], es[:, 0:C:2], es[:, 1:C:2], ADD)
+                nc.scalar.activation(root[:], s[:], ACT.Abs_reciprocal_sqrt)
+                nc.scalar.activation(squared[:], root[:], ACT.Square)
+                inv = squared
+            else:
+                s_turned = bank_tile(4 + j % 2, [P, PACK, P], "s_turned")
+                for b in range(X // P):
+                    for u in range(2):
+                        nc.tensor.matmul(
+                            s_turned[:, b, :],
+                            es[:, 2 * P * b + u : 2 * P * (b + 1) : 2],
+                            ident[:],
+                            start=(u == 0),
+                            stop=(u == 1),
+                            is_transpose=True,
+                        )
+                nc.scalar.activation(root[:], s_turned[:].rearrange("p b r -> p (b r)"), ACT.Abs_reciprocal_sqrt)
+                nc.scalar.activation(squared[:], root[:], ACT.Square)
+                inv = bank_tile(6 + j % 2, [P, X], "inv")
+                for b in range(X // P):
+                    nc.tensor.transpose(inv[:, b * P : (b + 1) * P], squared[:, b * P : (b + 1) * P], ident[:])
             h_j = keep.tile([P, H_COLS], F32, name="h%d" % j)
             nc.gpsimd.memset(h_j[:, X:H_COLS], 0.0)
             nc.vector.tensor_tensor(h_j[:, 0:X], inv[:], g_in[:, j, :], MULT)

@@ -16,275 +16,276 @@ E4M3 = mybir.dt.float8_e4m3fn_x4
 E5M2 = mybir.dt.float8_e5m2_x4
 ACT = mybir.ActivationFunctionType
 MULT = mybir.AluOpType.mult
-ADD = mybir.AluOpType.add
 
 P = 128
 PACK = 4
 HALF = 512
 LIST_COLS = HALF // 16
-W_CHUNK = 512
 H_COLS = X + P
+C_TILES = C // P
 
 
 def tile_attend_gcolb_kernel(tc, qT, wT, us, ts, G, wt, offs, docoffs, slotoffs, out):
     nc = tc.nc
     halves = range(C // HALF)
-    r_tiles = range(R // P)
+    r_tiles = range(PACK)
 
     def half_list(tile, h):
         return tile[:, h * LIST_COLS : (h + 1) * LIST_COLS]
 
+    def half(h):
+        return slice(h * HALF, (h + 1) * HALF)
+
     with ExitStack() as ctx:
         keep = ctx.enter_context(tc.tile_pool(name="keep", bufs=1))
-        stage = ctx.enter_context(tc.tile_pool(name="stage", bufs=1))
-        ring = ctx.enter_context(tc.tile_pool(name="ring", bufs=2))
         psum = ctx.enter_context(tc.psum_pool(name="psum", bufs=1))
+
+        def sb(shape, dtype, name, tag=None):
+            return keep.tile(shape, dtype, name=name, tag=tag or name, align_bytes=64)
 
         def bank_tile(n, shape, name):
             return psum.tile(shape, F32, name=name, tag="bank%d" % n)
 
-        idx = keep.tile([P, C // 16], U16, name="idx")
+        idx = sb([P, C // 16], U16, "idx")
         nc.sync.dma_start(idx[:], offs)
 
-        ts_win = keep.tile([P, T], F32, name="ts_win")
-        nc.vector.memset(ts_win[:].bitcast(I32), 0)
-        nc.sync.dma_start(ts_win[0:1, :], ts[0:1, :])
+        ts_win = sb([P, T], F32, "ts_win")
+        nc.sync.dma_start(ts_win[P - 1 : P, :], ts[0:1, :])
+        nc.vector.memset(ts_win[0 : P - 1, :].bitcast(I32), 0)
 
-        uw_rows = keep.tile([P, P], F32, name="uw_rows")
-        nc.gpsimd.memset(uw_rows[:], 0.0)
-        nc.sync.dma_start(uw_rows[0:4, :], us.rearrange("(j p) o -> j (p o)", p=P))
-        nc.sync.dma_start(uw_rows[4:8, :], wt.rearrange("(j p) o -> j (p o)", p=P))
-        slot = keep.tile([P, C // 16], U16, name="slot")
-        nc.sync.dma_start(slot[:], slotoffs)
-        doc = keep.tile([P, C // 16], U16, name="doc")
-        nc.sync.dma_start(doc[:], docoffs)
-
-        ident = keep.tile([P, P], F32, name="ident")
+        ident = sb([P, P], F32, "ident")
         make_identity(nc, ident[:])
 
         w_rows = wT.rearrange("(p j) t -> p j t", j=PACK)
-        w_win = []
-        n_chunks = T // W_CHUNK
-        for u in range(2):
-            win = keep.tile([P, T], U32, name="w_win%d" % u)
-            win_pairs = win[:].bitcast(BF16).rearrange("p (t e) -> p t e", e=2)
-            for n in range(n_chunks):
-                cols = slice(n * W_CHUNK, (n + 1) * W_CHUNK)
-                raw = stage.tile([P, 2, W_CHUNK], F32, name="w_raw", tag="stage%d" % (u * n_chunks + n))
-                nc.sync.dma_start(raw[:], w_rows[:, 2 * u : 2 * u + 2, cols])
-                src = raw[:].rearrange("p e t -> p t e")
-                if u == 1 and n == n_chunks - 1:
-                    nc.vector.tensor_copy(win_pairs[:, cols, :], src)
-                else:
-                    nc.scalar.activation(win_pairs[:, cols, :], src, ACT.Copy)
-            w_win.append(win)
+        w_win = [sb([P, T], U32, "w_win%d" % u) for u in range(2)]
 
+        def load_w(u, first, width, tag):
+            raw = sb([P, 2, width], F32, "w_raw_" + tag, tag)
+            nc.sync.dma_start(raw[:], w_rows[:, 2 * u : 2 * u + 2, first : first + width])
+            return raw
+
+        def cast_w(u, raw, first, lo, hi, on_vector):
+            dst = w_win[u][:].bitcast(BF16).rearrange("p (t e) -> p t e", e=2)[:, first + lo : first + hi, :]
+            src = raw[:, :, lo:hi].rearrange("p e t -> p t e")
+            if on_vector:
+                nc.vector.tensor_copy(dst, src)
+            else:
+                nc.scalar.activation(dst, src, ACT.Copy)
+
+        w0a = load_w(0, 0, 1024, "m0")
+        w0b = load_w(0, 1024, 1024, "m1")
+        us_col = sb([P, PACK], F32, "us_col")
+        nc.sync.dma_start(us_col[:], us.rearrange("(p j) o -> p (j o)", j=PACK))
+        wt_col = sb([P, PACK], F32, "wt_col")
+        nc.sync.dma_start(wt_col[:], wt.rearrange("(p j) o -> p (j o)", j=PACK))
+        w1 = [load_w(1, n * HALF, HALF, tag) for n, tag in enumerate(["factor1", "x0", "factor2", "x1"])]
         q_rows = qT.rearrange("(p j) r -> p j r", j=PACK)
-        q_raw = keep.tile([P, PACK, R], F32, name="q_raw")
-        nc.sync.dma_start(q_raw[:, :, 0:P], q_rows[:, :, 0:P])
-        nc.sync.dma_start(q_raw[:, :, P:R], q_rows[:, :, P:R])
-        g_in = keep.tile([P, R // P, X], F32, name="g_in")
-        nc.sync.dma_start(g_in[:], G.rearrange("(j p) x -> p j x", p=P))
+        q_raw = [sb([P, PACK, R // 2], F32, "q_raw%d" % n) for n in range(2)]
+        for n in range(2):
+            nc.sync.dma_start(q_raw[n][:], q_rows[:, :, n * R // 2 : (n + 1) * R // 2])
+        slot = sb([P, C // 16], U16, "slot")
+        nc.sync.dma_start(slot[:], slotoffs)
+        doc = sb([P, C // 16], U16, "doc")
+        nc.sync.dma_start(doc[:], docoffs)
+        g_in = sb([P, PACK, X], F32, "g_in")
+        nc.sync.dma_start(g_in[:], G.rearrange("(p j) x -> p j x", j=PACK))
 
-        w_codes = keep.tile([P, C], U32, name="w_codes", align_bytes=64)
-        w_scales = keep.tile([P, C], U8, name="w_scales", align_bytes=64)
-        w_grouped = [keep.tile([P, HALF * PACK], BF16, name="w_grouped%d" % h, align_bytes=64) for h in halves]
+        cast_w(0, w0a, 0, 0, 1024, False)
+        cast_w(0, w0b, 1024, 0, 512, False)
+        cast_w(0, w0b, 1024, 512, 1024, True)
+        for n, raw in enumerate(w1):
+            cast_w(1, raw, n * HALF, 0, HALF, n % 2 == 1)
 
-        w_pairs = keep.tile([P, 2 * C], U32, name="w_pairs", tag="w_pairs", align_bytes=64)
-        nc.vector.tensor_copy(w_pairs[:, 0:C], w_win[0][:].indirect(idx[:]))
-
-        ts_row = keep.tile([P, C], F32, name="ts_row")
-        nc.vector.tensor_copy(ts_row[:], ts_win[:].indirect(idx[:]))
-        ts_col = keep.tile([P, C // P], F32, name="ts_col")
-        ts_all = stage.tile([P, C], F32, name="ts_all", tag="stage6")
+        ts_row = sb([P, C], F32, "ts_row")
+        ts_col = sb([P, C_TILES], F32, "ts_col")
+        ts_all = sb([P, C], F32, "ts_all")
         for h in halves:
+            nc.vector.tensor_copy(ts_row[:, half(h)], ts_win[:].indirect(half_list(idx, h)))
             bank = bank_tile(4 + h, [P, PACK, P], "ts_turned")
             for b in range(PACK):
                 k = PACK * h + b
                 nc.tensor.transpose(bank[:, b, :], ts_row[:, k * P : (k + 1) * P], ident[:])
-            nc.vector.tensor_copy(ts_col[:, PACK * h : PACK * (h + 1)], bank[:, :, 0])
+            nc.vector.tensor_copy(ts_col[:, PACK * h : PACK * (h + 1)], bank[:, :, P - 1])
         for h in halves:
             bank = bank_tile(6 + h, [P, PACK, P], "ts_spread")
             for b in range(PACK):
                 k = PACK * h + b
                 nc.tensor.transpose(bank[:, b, :], ts_col[:, k : k + 1].to_broadcast([P, P]), ident[:])
-            nc.scalar.copy(ts_all[:, h * HALF : (h + 1) * HALF], bank[:].rearrange("p b c -> p (b c)"))
+            nc.vector.tensor_copy(ts_all[:, half(h)], bank[:].rearrange("p b c -> p (b c)"))
+        wtus = sb([P, PACK], F32, "wtus")
+        nc.vector.tensor_tensor(wtus[:], us_col[:], wt_col[:], MULT)
 
-        uw_bank = bank_tile(0, [P, PACK, P], "uw_bank")
-        nc.tensor.transpose(uw_bank[:, 0, :], uw_rows[:], ident[:])
-        uw = keep.tile([P, 8], F32, name="uw")
-        nc.vector.tensor_copy(uw[:], uw_bank[:, 0, 0:8])
-        wtus = keep.tile([P, 4], F32, name="wtus")
-        nc.vector.tensor_tensor(wtus[:], uw[:, 0:4], uw[:, 4:8], MULT)
+        w_codes = sb([P, C], U32, "w_codes")
+        w_scales = sb([P, C], U8, "w_scales")
+        w_pairs = sb([P, 2 * C], U32, "w_pairs", "win0")
+        nc.vector.tensor_copy(w_pairs[:, 0:C], w_win[0][:].indirect(idx[:]))
 
-        qa_codes = keep.tile([P, R], U32, name="qa_codes", align_bytes=64)
-        qa_scales = keep.tile([P, R], U8, name="qa_scales", align_bytes=64)
+        qa_grouped = sb([P, R * PACK], BF16, "qa_grouped")
+        qa_dealt = qa_grouped[:].rearrange("p (j s t) -> p s j t", j=PACK, t=PACK)
+        qa_codes = sb([P, R], U32, "qa_codes")
+        qa_scales = sb([P, R], U8, "qa_scales")
+        nc.scalar.activation(qa_dealt[:, 0 : P // 2], q_raw[0][:].rearrange("p t (s j) -> p s j t", j=PACK), ACT.Copy)
 
-        def group_qa(j, grouped):
-            nc.scalar.activation(
-                grouped.rearrange("p (r i t) -> p r t i", i=4, t=PACK),
-                q_raw[:, :, j * P : (j + 1) * P].rearrange("p t (r i) -> p r t i", i=4),
-                ACT.Copy,
-            )
-
-        def quantize_qa(j, grouped):
-            cols = slice(j * P, (j + 1) * P)
-            nc.vector.quantize_mx(qa_codes[:, cols].bitcast(E4M3), qa_scales[:, cols], grouped)
-
-        qa_first = keep.tile([P, P * PACK], BF16, name="qa_first", align_bytes=64)
-        group_qa(0, qa_first[:])
         for h in halves:
             nc.vector.tensor_copy(w_pairs[:, C + h * HALF : C + (h + 1) * HALF], w_win[1][:].indirect(half_list(idx, h)))
-        quantize_qa(0, qa_first[:])
         for h in halves:
-            cols = slice(h * HALF, (h + 1) * HALF)
+            if h == 1:
+                nc.vector.tensor_copy(qa_dealt[:, P // 2 : P], q_raw[1][:].rearrange("p t (s j) -> p s j t", j=PACK))
+                nc.vector.quantize_mx(qa_codes[:].bitcast(E4M3), qa_scales[:], qa_grouped[:])
+            w_grouped = sb([P, HALF * PACK], BF16, "w_grouped%d" % h, "win1" if h == 0 else None)
             nc.scalar.copy(
-                w_grouped[h][:].bitcast(U32).rearrange("p (c u) -> p c u", u=2),
-                w_pairs[:].rearrange("p (u c) -> p c u", u=2)[:, cols, :],
+                w_grouped[:].bitcast(U32).rearrange("p (c u) -> p c u", u=2),
+                w_pairs[:].rearrange("p (u c) -> p c u", u=2)[:, half(h), :],
             )
-            nc.vector.quantize_mx(w_codes[:, cols].bitcast(E4M3), w_scales[:, cols], w_grouped[h][:])
-        qa_rest = keep.tile([P, (R - P) * PACK], BF16, name="qa_rest", tag="w_pairs", align_bytes=64)
-        for j in r_tiles[1:]:
-            grouped = qa_rest[:, (j - 1) * P * PACK : j * P * PACK]
-            group_qa(j, grouped)
-            quantize_qa(j, grouped)
+            nc.vector.quantize_mx(w_codes[:, half(h)].bitcast(E4M3), w_scales[:, half(h)], w_grouped[:])
 
-        e = []
-        for j in r_tiles:
+        e = [sb([P, C], F32, "e%d" % j, "win2" if j == 3 else None) for j in r_tiles]
+        for j in range(2):
             rows = slice(j * P, (j + 1) * P)
-            e_j = keep.tile([P, C], F32, name="e%d" % j)
             for h in halves:
-                cols = slice(h * HALF, (h + 1) * HALF)
-                a = bank_tile((2 * j + h) % 4, [P, HALF], "a")
+                a = bank_tile(2 * j + h, [P, HALF], "a")
                 nc.tensor.matmul_mx(
                     a[:],
                     lhsT=qa_codes[:, rows].bitcast(E4M3),
                     lhsT_scale=qa_scales[:, rows],
-                    rhs=w_codes[:, cols].bitcast(E4M3),
-                    rhs_scale=w_scales[:, cols],
+                    rhs=w_codes[:, half(h)].bitcast(E4M3),
+                    rhs_scale=w_scales[:, half(h)],
                     start=True,
                     stop=True,
                 )
-                z = keep.tile([P, HALF], F32, name="z", tag="z%d" % ((2 * j + h) % 4))
-                nc.vector.tensor_tensor(z[:], a[:], ts_all[:, cols], MULT)
-                nc.scalar.activation(e_j[:, cols], z[:], ACT.Exp, scale=uw[:, j : j + 1])
-            e.append(e_j)
+                z = sb([P, HALF], F32, "z", "ts_win" if 2 * j + h == 3 else "z%d" % (2 * j + h))
+                nc.vector.tensor_tensor(z[:], a[:], ts_all[:, half(h)], MULT)
+                nc.scalar.activation(e[j][:, half(h)], z[:], ACT.Exp, scale=us_col[:, j : j + 1])
 
-        q_pairs = keep.tile([P, PACK * R], BF16, name="q_pairs", tag="z3")
-        nc.scalar.activation(
-            q_pairs[:].rearrange("p (u s e) -> p s u e", u=2, e=2),
-            q_raw[:].rearrange("p j (s u e) -> p (j s) u e", u=2, e=2),
-            ACT.Copy,
-        )
-        q_words = q_pairs[:].bitcast(F32).rearrange("p (u j s) -> p u j s", u=2, j=PACK)
-
-        h_win = []
-        ew = []
-        for j in r_tiles:
-            es = ring.tile([P, C], F32, name="es", tag="es", bufs=3)
+        y = sb([P, C_TILES * 2 * P], F32, "y", "ts_win")
+        for pair in range(C_TILES // 2):
+            a_turned = bank_tile(4 + pair, [P, 2, 2 * P], "a_turned")
+            for b in range(2):
+                k = 2 * pair + b
+                nc.tensor.matmul_mx(
+                    a_turned[:, b, :],
+                    lhsT=w_codes[:, k * P : (k + 1) * P].bitcast(E4M3),
+                    lhsT_scale=w_scales[:, k * P : (k + 1) * P],
+                    rhs=qa_codes[:, 2 * P : 4 * P].bitcast(E4M3),
+                    rhs_scale=qa_scales[:, 2 * P : 4 * P],
+                    start=True,
+                    stop=True,
+                )
+            for b in range(2):
+                k = 2 * pair + b
+                nc.scalar.activation(y[:, 2 * k * P : 2 * (k + 1) * P], a_turned[:, b, :], ACT.Copy, scale=ts_col[:, k : k + 1])
+        for j in range(2, 4):
             for h in halves:
-                nc.vector.tensor_copy(es[:, h * HALF : (h + 1) * HALF], e[j][:].indirect(half_list(slot, h)))
-            root = stage.tile([P, X], F32, name="root", tag="stage%d" % j)
-            squared = ring.tile([P, X], F32, name="squared", tag="squared")
-            if j == r_tiles[-1]:
-                s = keep.tile([P, X], F32, name="s")
-                nc.vector.tensor_tensor(s[:], es[:, 0:C:2], es[:, 1:C:2], ADD)
-                nc.scalar.activation(root[:], s[:], ACT.Abs_reciprocal_sqrt)
-                nc.scalar.activation(squared[:], root[:], ACT.Square)
-                inv = squared
+                bank = bank_tile(2 * (j - 2) + h, [P, HALF], "y_turned")
+                for b in range(PACK):
+                    first = (2 * (PACK * h + b) + j - 2) * P
+                    nc.tensor.transpose(bank[:, b * P : (b + 1) * P], y[:, first : first + P], ident[:])
+                nc.scalar.activation(e[j][:, half(h)], bank[:], ACT.Exp, scale=us_col[:, j : j + 1])
+
+        x = []
+        for j in r_tiles:
+            if j < 3:
+                factor = sb([P, C], F32, "factor%d" % j, "m1" if j == 0 else None)
+                for h in halves:
+                    nc.scalar.activation(factor[:, half(h)], ts_all[:, half(h)], ACT.Copy, scale=wtus[:, j : j + 1])
+                x_j = sb([P, C], F32, "x%d" % j)
+                nc.gpsimd.tensor_tensor(x_j[:], e[j][:], factor[:], MULT)
+                x.append([x_j[:, half(h)] for h in halves])
             else:
-                s_turned = bank_tile(4 + j % 2, [P, PACK, P], "s_turned")
-                for b in range(X // P):
-                    for u in range(2):
-                        nc.tensor.matmul(
-                            s_turned[:, b, :],
-                            es[:, 2 * P * b + u : 2 * P * (b + 1) : 2],
-                            ident[:],
-                            start=(u == 0),
-                            stop=(u == 1),
-                            is_transpose=True,
-                        )
-                nc.scalar.activation(root[:], s_turned[:].rearrange("p b r -> p (b r)"), ACT.Abs_reciprocal_sqrt)
-                nc.scalar.activation(squared[:], root[:], ACT.Square)
-                inv = bank_tile(6 + j % 2, [P, X], "inv")
-                for b in range(X // P):
-                    nc.tensor.transpose(inv[:, b * P : (b + 1) * P], squared[:, b * P : (b + 1) * P], ident[:])
-            h_j = keep.tile([P, H_COLS], F32, name="h%d" % j)
+                parts = []
+                for h in halves:
+                    factor = sb([P, HALF], F32, "factor3", "win%d" % h)
+                    nc.scalar.activation(factor[:], ts_all[:, half(h)], ACT.Copy, scale=wtus[:, j : j + 1])
+                    part = sb([P, HALF], F32, "x3", "m1" if h == 0 else "x3b")
+                    nc.gpsimd.tensor_tensor(part[:], e[j][:, half(h)], factor[:], MULT)
+                    parts.append(part[:])
+                x.append(parts)
+
+        sum_banks = [2, 3, 1, 4]
+        inv_banks = [4, 5, 6, 7]
+        es_tags = ["w_win0", "w_win1", "es2", "win3"]
+        es = []
+        for j in r_tiles:
+            es_j = sb([P, C], F32, "es%d" % j, es_tags[j])
+            for h in halves:
+                nc.vector.tensor_copy(es_j[:, half(h)], e[j][:].indirect(half_list(slot, h)))
+            es.append(es_j)
+        m0 = sb([P, PACK * HALF], F32, "m0")
+        h_win = []
+        for j in r_tiles:
+            s_turned = bank_tile(sum_banks[j], [P, PACK, P], "s_turned")
+            for b in range(X // P):
+                for u in range(2):
+                    nc.tensor.matmul(
+                        s_turned[:, b, :],
+                        es[j][:, 2 * P * b + u : 2 * P * (b + 1) : 2],
+                        ident[:],
+                        start=(u == 0),
+                        stop=(u == 1),
+                        is_transpose=True,
+                    )
+            root = sb([P, X], F32, "root")
+            nc.scalar.activation(root[:], s_turned[:].rearrange("p b r -> p (b r)"), ACT.Abs_reciprocal_sqrt)
+            squared = sb([P, X], F32, "squared", "squared%d" % (j % 2))
+            nc.scalar.activation(squared[:], root[:], ACT.Square)
+            inv = bank_tile(inv_banks[j], [P, X], "inv")
+            for b in range(X // P):
+                nc.tensor.transpose(inv[:, b * P : (b + 1) * P], squared[:, b * P : (b + 1) * P], ident[:])
+            h_j = sb([P, H_COLS], F32, "h%d" % j)
             nc.gpsimd.memset(h_j[:, X:H_COLS], 0.0)
             nc.vector.tensor_tensor(h_j[:, 0:X], inv[:], g_in[:, j, :], MULT)
             h_win.append(h_j)
-            ew_j = stage.tile([P, C], F32, name="ew", tag="stage%d" % j)
-            nc.scalar.activation(ew_j[:, 0:HALF], e[j][:, 0:HALF], ACT.Copy, scale=wtus[:, j : j + 1])
-            ew.append(ew_j)
+            nc.vector.tensor_tensor(m0[:, j * HALF : (j + 1) * HALF], h_j[:].indirect(half_list(doc, 0)), x[j][0], MULT)
 
-        qb = keep.tile([P, D * PACK], BF16, name="qb", align_bytes=64)
+        out_win = []
+        for j in range(PACK):
+            win = sb([P, T], F32, "out_win%d" % j, "win%d" % j)
+            nc.gpsimd.memset(win[:].bitcast(I32), 0)
+            out_win.append(win)
+        out_rows = out.rearrange("(p j) t -> p j t", j=PACK)
+
+        q_pairs = sb([P, PACK * R], BF16, "q_pairs", "root")
+        for n in range(2):
+            for u in range(2):
+                nc.scalar.activation(
+                    q_pairs[:].rearrange("p (u j s e) -> p u j s e", u=2, j=PACK, e=2)[:, u, :, n * P // 2 : (n + 1) * P // 2, :],
+                    q_raw[n][:].rearrange("p j (s u e) -> p u j s e", u=2, e=2)[:, u],
+                    ACT.Copy,
+                )
+        q_words = q_pairs[:].bitcast(F32).rearrange("p (u j s) -> p u j s", u=2, j=PACK)
+        qb = sb([P, D * PACK], BF16, "qb")
         qb_words = qb[:].bitcast(F32).rearrange("s (j p u) -> s j p u", p=P, u=2)
         for pair in range(2):
-            bank = bank_tile(pair, [P, 2, 2, P], "q_turned")
+            bank = bank_tile(2 + pair, [P, 2, 2, P], "q_turned")
             for b in range(2):
                 for u in range(2):
                     nc.tensor.transpose(bank[:, b, u, :], q_words[:, u, 2 * pair + b, :], ident[:])
             nc.scalar.copy(qb_words[:, 2 * pair : 2 * pair + 2], bank[:].rearrange("s b u p -> s b p u"))
-        qb_codes = keep.tile([P, D], U32, name="qb_codes", align_bytes=64)
-        qb_scales = keep.tile([P, D], U8, name="qb_scales", align_bytes=64)
-        nc.vector.quantize_mx(qb_codes[:].bitcast(E4M3), qb_scales[:], qb[:])
 
-        for j in r_tiles:
-            nc.scalar.activation(ew[j][:, HALF:C], e[j][:, HALF:C], ACT.Copy, scale=wtus[:, j : j + 1])
+        m1 = sb([P, PACK * HALF], F32, "m1")
 
-        m_first = [ring.tile([P, HALF], F32, name="m_first", tag="m_first", bufs=4) for j in r_tiles]
-        m = [[tile[:] for tile in m_first], [ew[3][:, 0:HALF], ew[0][:, HALF:C], ew[1][:, HALF:C]]]
+        def gather_second(j):
+            nc.vector.tensor_tensor(m1[:, j * HALF : (j + 1) * HALF], h_win[j][:].indirect(half_list(doc, 1)), x[j][1], MULT)
 
-        def gather_h(h, j, pieces=1):
-            width = HALF // pieces
-            for n in range(pieces):
-                first = h * HALF + n * width
-                nc.vector.tensor_tensor(
-                    m[h][j][:, n * width : (n + 1) * width],
-                    h_win[j][:].indirect(doc[:, first // 16 : (first + width) // 16]),
-                    ew[j][:, first : first + width],
-                    MULT,
-                )
-
-        for j in r_tiles[:-1]:
-            gather_h(0, j)
-        gather_h(0, 3, pieces=2)
-        for j in r_tiles[:-1]:
-            gather_h(1, j)
-
-        out_win = []
-        for j in range(PACK):
-            win = keep.tile([P, T], F32, name="out_win%d" % j)
-            nc.vector.memset(win[:].bitcast(I32), 0)
-            out_win.append(win)
-        out_rows = out.rearrange("(p j) t -> p j t", j=PACK)
-
-        def quantize_g(h, turn_banks):
-            g_grouped = keep.tile([P, HALF * PACK], BF16, name="g_grouped", tag="g_grouped%d" % h, align_bytes=64)
-            g_words = g_grouped[:].bitcast(F32).rearrange("p (b c u) -> p b c u", c=P, u=2)
-            for pair in range(2):
-                words_bank = bank_tile(4 + pair, [P, 2, 2, P], "words_bank")
-                for b in range(2):
-                    block = 2 * pair + b
-                    bank = bank_tile(turn_banks[block], [P, R], "m_turned")
-                    for j in r_tiles:
-                        nc.tensor.transpose(bank[:, j * P : (j + 1) * P], m[h][j][:, block * P : (block + 1) * P], ident[:])
-                    g_turned = ring.tile([P, R], BF16, name="g_turned", tag="g_turned", bufs=4)
-                    k = PACK * h + block
-                    nc.scalar.activation(
-                        g_turned[:].rearrange("c (u s e) -> c s u e", u=2, e=2),
-                        bank[:].rearrange("c (s u e) -> c s u e", u=2, e=2),
-                        ACT.Copy,
-                        scale=ts_col[:, k : k + 1],
-                    )
-                    words = g_turned[:].bitcast(F32)
-                    for u in range(2):
-                        nc.tensor.transpose(words_bank[:, b, u, :], words[:, u * P : (u + 1) * P], ident[:])
-                nc.scalar.copy(g_words[:, 2 * pair : 2 * pair + 2], words_bank[:].rearrange("p b u c -> p b c u"))
-            g_codes = ring.tile([P, HALF], U32, name="g_codes", tag="g_codes", align_bytes=64)
-            g_scales = ring.tile([P, HALF], U8, name="g_scales", tag="g_scales", align_bytes=64)
-            nc.vector.quantize_mx(g_codes[:].bitcast(E5M2), g_scales[:], g_grouped[:])
+        def quantize_g(h, m, grouped):
+            nc.scalar.activation(
+                grouped.rearrange("p (c i t) -> p c t i", i=4, t=PACK),
+                m.rearrange("p (t c i) -> p c t i", t=PACK, i=4),
+                ACT.Copy,
+            )
+            g_codes = sb([P, HALF], U32, "g_codes%d" % h)
+            g_scales = sb([P, HALF], U8, "g_scales%d" % h)
+            nc.vector.quantize_mx(g_codes[:].bitcast(E5M2), g_scales[:], grouped)
             return g_codes, g_scales
+
+        for j in range(2):
+            gather_second(j)
+        qb_codes = sb([P, D], U32, "qb_codes", "x1")
+        qb_scales = sb([P, D], U8, "qb_scales")
+        nc.vector.quantize_mx(qb_codes[:].bitcast(E4M3), qb_scales[:], qb[:])
+        g_first = quantize_g(0, m0[:], m1[:, 2 * HALF : 4 * HALF].bitcast(BF16))
+        for j in range(2, 4):
+            gather_second(j)
 
         def put_dw(h, j, g_mx, n):
             rows = slice(j * P, (j + 1) * P)
@@ -298,19 +299,16 @@ def tile_attend_gcolb_kernel(tc, qT, wT, us, ts, G, wt, offs, docoffs, slotoffs,
                 start=True,
                 stop=True,
             )
-            dw = ring.tile([P, HALF], F32, name="dw", tag="dw", bufs=4)
+            dw = sb([P, HALF], F32, "dw", "m1" if (h, j) == (0, 3) else "z%d" % j)
             nc.scalar.copy(dw[:], dw_bank[:])
             nc.vector.tensor_copy(out_win[j][:].indirect(half_list(idx, h)), dw[:])
             if h == halves[-1]:
                 nc.sync.dma_start(out_rows[:, j, :], out_win[j][:])
 
-        g_first = quantize_g(0, [0, 1, 2, 3])
-        m_last = keep.tile([P, HALF], F32, name="m_last", tag="g_grouped0", align_bytes=64)
-        m[1].append(m_last[:])
-        gather_h(1, 3)
         for j in range(3):
             put_dw(0, j, g_first, j)
-        g_second = quantize_g(1, [0, 1, 2, 0])
-        put_dw(0, 3, g_first, 5)
+        g_grouped = sb([P, HALF * PACK], BF16, "g_grouped")
+        g_second = quantize_g(1, m1[:], g_grouped[:])
+        put_dw(0, 3, g_first, 3)
         for j in range(PACK):
-            put_dw(1, j, g_second, j)
+            put_dw(1, j, g_second, 4 + j)

@@ -16,6 +16,7 @@ E4M3 = mybir.dt.float8_e4m3fn_x4
 E5M2 = mybir.dt.float8_e5m2_x4
 ACT = mybir.ActivationFunctionType
 MULT = mybir.AluOpType.mult
+ADD = mybir.AluOpType.add
 
 P = 128
 PACK = 4
@@ -53,6 +54,11 @@ def tile_attend_gcolb_kernel(tc, qT, wT, us, ts, G, wt, offs, docoffs, slotoffs,
         nc.sync.dma_start(ts_win[P - 1 : P, :], ts[0:1, :])
         nc.vector.memset(ts_win[0 : P - 1, :].bitcast(I32), 0)
 
+        us_col = sb([P, PACK], F32, "us_col")
+        nc.sync.dma_start(us_col[:], us.rearrange("(p j) o -> p (j o)", j=PACK))
+        wt_col = sb([P, PACK], F32, "wt_col")
+        nc.sync.dma_start(wt_col[:], wt.rearrange("(p j) o -> p (j o)", j=PACK))
+
         ident = sb([P, P], F32, "ident")
         make_identity(nc, ident[:])
 
@@ -72,13 +78,8 @@ def tile_attend_gcolb_kernel(tc, qT, wT, us, ts, G, wt, offs, docoffs, slotoffs,
             else:
                 nc.scalar.activation(dst, src, ACT.Copy)
 
-        w0a = load_w(0, 0, 1024, "m0")
-        w0b = load_w(0, 1024, 1024, "m1")
-        us_col = sb([P, PACK], F32, "us_col")
-        nc.sync.dma_start(us_col[:], us.rearrange("(p j) o -> p (j o)", j=PACK))
-        wt_col = sb([P, PACK], F32, "wt_col")
-        nc.sync.dma_start(wt_col[:], wt.rearrange("(p j) o -> p (j o)", j=PACK))
-        w1 = [load_w(1, n * HALF, HALF, tag) for n, tag in enumerate(["factor1", "x0", "factor2", "x1"])]
+        w0 = [load_w(0, n * HALF, HALF, tag) for n, tag in enumerate(["m0", "m1", "factor1", "x2"])]
+        w1 = [load_w(1, n * HALF, HALF, tag) for n, tag in enumerate(["factor2", "x0", "win0", "x1"])]
         q_rows = qT.rearrange("(p j) r -> p j r", j=PACK)
         q_raw = [sb([P, PACK, R // 2], F32, "q_raw%d" % n) for n in range(2)]
         for n in range(2):
@@ -90,9 +91,8 @@ def tile_attend_gcolb_kernel(tc, qT, wT, us, ts, G, wt, offs, docoffs, slotoffs,
         g_in = sb([P, PACK, X], F32, "g_in")
         nc.sync.dma_start(g_in[:], G.rearrange("(p j) x -> p j x", j=PACK))
 
-        cast_w(0, w0a, 0, 0, 1024, False)
-        cast_w(0, w0b, 1024, 0, 512, False)
-        cast_w(0, w0b, 1024, 512, 1024, True)
+        for n, raw in enumerate(w0):
+            cast_w(0, raw, n * HALF, 0, HALF, n == 3)
         for n, raw in enumerate(w1):
             cast_w(1, raw, n * HALF, 0, HALF, n % 2 == 1)
 
@@ -115,41 +115,46 @@ def tile_attend_gcolb_kernel(tc, qT, wT, us, ts, G, wt, offs, docoffs, slotoffs,
         wtus = sb([P, PACK], F32, "wtus")
         nc.vector.tensor_tensor(wtus[:], us_col[:], wt_col[:], MULT)
 
-        w_codes = sb([P, C], U32, "w_codes")
-        w_scales = sb([P, C], U8, "w_scales")
-        w_pairs = sb([P, 2 * C], U32, "w_pairs", "win0")
+        w_codes = [sb([P, HALF], U32, "w_codes%d" % h) for h in halves]
+        w_scales = [sb([P, HALF], U8, "w_scales%d" % h) for h in halves]
+        w_pairs = sb([P, 2 * C], U32, "w_pairs")
         nc.vector.tensor_copy(w_pairs[:, 0:C], w_win[0][:].indirect(idx[:]))
 
         qa_grouped = sb([P, R * PACK], BF16, "qa_grouped")
         qa_dealt = qa_grouped[:].rearrange("p (j s t) -> p s j t", j=PACK, t=PACK)
-        qa_codes = sb([P, R], U32, "qa_codes")
-        qa_scales = sb([P, R], U8, "qa_scales")
         nc.scalar.activation(qa_dealt[:, 0 : P // 2], q_raw[0][:].rearrange("p t (s j) -> p s j t", j=PACK), ACT.Copy)
 
         for h in halves:
             nc.vector.tensor_copy(w_pairs[:, C + h * HALF : C + (h + 1) * HALF], w_win[1][:].indirect(half_list(idx, h)))
+        nc.vector.tensor_copy(qa_dealt[:, P // 2 : P], q_raw[1][:].rearrange("p t (s j) -> p s j t", j=PACK))
+
+        def quantize_qa(first, last):
+            codes = sb([P, (last - first) * P], U32, "qa_codes%d" % first, ["qa_codes0", "w_grouped1", "z0"][first])
+            scales = sb([P, (last - first) * P], U8, "qa_scales%d" % first)
+            nc.vector.quantize_mx(codes[:].bitcast(E4M3), scales[:], qa_grouped[:, first * P * PACK : last * P * PACK])
+            return codes, scales
+
+        qa = quantize_qa(0, 1)
         for h in halves:
-            if h == 1:
-                nc.vector.tensor_copy(qa_dealt[:, P // 2 : P], q_raw[1][:].rearrange("p t (s j) -> p s j t", j=PACK))
-                nc.vector.quantize_mx(qa_codes[:].bitcast(E4M3), qa_scales[:], qa_grouped[:])
-            w_grouped = sb([P, HALF * PACK], BF16, "w_grouped%d" % h, "win1" if h == 0 else None)
+            w_grouped = sb([P, HALF * PACK], BF16, "w_grouped%d" % h)
             nc.scalar.copy(
                 w_grouped[:].bitcast(U32).rearrange("p (c u) -> p c u", u=2),
                 w_pairs[:].rearrange("p (u c) -> p c u", u=2)[:, half(h), :],
             )
-            nc.vector.quantize_mx(w_codes[:, half(h)].bitcast(E4M3), w_scales[:, half(h)], w_grouped[:])
+            nc.vector.quantize_mx(w_codes[h][:].bitcast(E4M3), w_scales[h][:], w_grouped[:])
 
-        e = [sb([P, C], F32, "e%d" % j, "win2" if j == 3 else None) for j in r_tiles]
+        e = [sb([P, C], F32, "e%d" % j, "win%d" % (j - 1) if j >= 2 else None) for j in r_tiles]
         for j in range(2):
-            rows = slice(j * P, (j + 1) * P)
+            if j == 1:
+                qa = quantize_qa(1, 2)
             for h in halves:
                 a = bank_tile(2 * j + h, [P, HALF], "a")
                 nc.tensor.matmul_mx(
                     a[:],
-                    lhsT=qa_codes[:, rows].bitcast(E4M3),
-                    lhsT_scale=qa_scales[:, rows],
-                    rhs=w_codes[:, half(h)].bitcast(E4M3),
-                    rhs_scale=w_scales[:, half(h)],
+                    lhsT=qa[0][:].bitcast(E4M3),
+                    lhsT_scale=qa[1][:],
+                    rhs=w_codes[h][:].bitcast(E4M3),
+                    rhs_scale=w_scales[h][:],
                     start=True,
                     stop=True,
                 )
@@ -157,6 +162,7 @@ def tile_attend_gcolb_kernel(tc, qT, wT, us, ts, G, wt, offs, docoffs, slotoffs,
                 nc.vector.tensor_tensor(z[:], a[:], ts_all[:, half(h)], MULT)
                 nc.scalar.activation(e[j][:, half(h)], z[:], ACT.Exp, scale=us_col[:, j : j + 1])
 
+        qa_late = quantize_qa(2, 4)
         y = sb([P, C_TILES * 2 * P], F32, "y", "ts_win")
         for pair in range(C_TILES // 2):
             a_turned = bank_tile(4 + pair, [P, 2, 2 * P], "a_turned")
@@ -164,10 +170,10 @@ def tile_attend_gcolb_kernel(tc, qT, wT, us, ts, G, wt, offs, docoffs, slotoffs,
                 k = 2 * pair + b
                 nc.tensor.matmul_mx(
                     a_turned[:, b, :],
-                    lhsT=w_codes[:, k * P : (k + 1) * P].bitcast(E4M3),
-                    lhsT_scale=w_scales[:, k * P : (k + 1) * P],
-                    rhs=qa_codes[:, 2 * P : 4 * P].bitcast(E4M3),
-                    rhs_scale=qa_scales[:, 2 * P : 4 * P],
+                    lhsT=w_codes[k // PACK][:, k % PACK * P : (k % PACK + 1) * P].bitcast(E4M3),
+                    lhsT_scale=w_scales[k // PACK][:, k % PACK * P : (k % PACK + 1) * P],
+                    rhs=qa_late[0][:].bitcast(E4M3),
+                    rhs_scale=qa_late[1][:],
                     start=True,
                     stop=True,
                 )
@@ -182,55 +188,68 @@ def tile_attend_gcolb_kernel(tc, qT, wT, us, ts, G, wt, offs, docoffs, slotoffs,
                     nc.tensor.transpose(bank[:, b * P : (b + 1) * P], y[:, first : first + P], ident[:])
                 nc.scalar.activation(e[j][:, half(h)], bank[:], ACT.Exp, scale=us_col[:, j : j + 1])
 
+        m1 = sb([P, PACK * HALF], F32, "m1", "ts_win")
         x = []
         for j in r_tiles:
             if j < 3:
-                factor = sb([P, C], F32, "factor%d" % j, "m1" if j == 0 else None)
-                for h in halves:
-                    nc.scalar.activation(factor[:, half(h)], ts_all[:, half(h)], ACT.Copy, scale=wtus[:, j : j + 1])
+                factor = sb([P, C], F32, "factor%d" % j)
+                if j == 0:
+                    nc.vector.tensor_scalar(factor[:], ts_all[:], wtus[:, j : j + 1], None, MULT)
+                else:
+                    nc.scalar.activation(factor[:], ts_all[:], ACT.Copy, scale=wtus[:, j : j + 1])
                 x_j = sb([P, C], F32, "x%d" % j)
                 nc.gpsimd.tensor_tensor(x_j[:], e[j][:], factor[:], MULT)
                 x.append([x_j[:, half(h)] for h in halves])
             else:
                 parts = []
+                factor = sb([P, C], F32, "factor3", "win0")
+                nc.scalar.activation(factor[:], ts_all[:], ACT.Copy, scale=wtus[:, j : j + 1])
                 for h in halves:
-                    factor = sb([P, HALF], F32, "factor3", "win%d" % h)
-                    nc.scalar.activation(factor[:], ts_all[:, half(h)], ACT.Copy, scale=wtus[:, j : j + 1])
-                    part = sb([P, HALF], F32, "x3", "m1" if h == 0 else "x3b")
-                    nc.gpsimd.tensor_tensor(part[:], e[j][:, half(h)], factor[:], MULT)
-                    parts.append(part[:])
+                    part = m1[:, HALF // 2 : 3 * HALF // 2] if h == 0 else sb([P, HALF], F32, "x3b")[:]
+                    nc.gpsimd.tensor_tensor(part, e[j][:, half(h)], factor[:, half(h)], MULT)
+                    parts.append(part)
                 x.append(parts)
 
-        sum_banks = [2, 3, 1, 4]
-        inv_banks = [4, 5, 6, 7]
+        sum_banks = [7, 0]
+        inv_banks = [4, 5]
         es_tags = ["w_win0", "w_win1", "es2", "win3"]
         es = []
+        sums = [None, None]
         for j in r_tiles:
             es_j = sb([P, C], F32, "es%d" % j, es_tags[j])
             for h in halves:
                 nc.vector.tensor_copy(es_j[:, half(h)], e[j][:].indirect(half_list(slot, h)))
             es.append(es_j)
+            if j >= 2:
+                s_j = sb([P, X], F32, "s%d" % j)
+                nc.vector.tensor_tensor(s_j[:], es_j[:, 0:C:2], es_j[:, 1:C:2], ADD)
+                sums.append(s_j)
         m0 = sb([P, PACK * HALF], F32, "m0")
         h_win = []
         for j in r_tiles:
-            s_turned = bank_tile(sum_banks[j], [P, PACK, P], "s_turned")
-            for b in range(X // P):
-                for u in range(2):
-                    nc.tensor.matmul(
-                        s_turned[:, b, :],
-                        es[j][:, 2 * P * b + u : 2 * P * (b + 1) : 2],
-                        ident[:],
-                        start=(u == 0),
-                        stop=(u == 1),
-                        is_transpose=True,
-                    )
-            root = sb([P, X], F32, "root")
-            nc.scalar.activation(root[:], s_turned[:].rearrange("p b r -> p (b r)"), ACT.Abs_reciprocal_sqrt)
-            squared = sb([P, X], F32, "squared", "squared%d" % (j % 2))
-            nc.scalar.activation(squared[:], root[:], ACT.Square)
-            inv = bank_tile(inv_banks[j], [P, X], "inv")
-            for b in range(X // P):
-                nc.tensor.transpose(inv[:, b * P : (b + 1) * P], squared[:, b * P : (b + 1) * P], ident[:])
+            root = m1[:, 2 * HALF : 3 * HALF]
+            squared = sb([P, X], F32, "squared%d" % j)
+            if j < 2:
+                s_turned = bank_tile(sum_banks[j], [P, PACK, P], "s_turned")
+                for b in range(X // P):
+                    for u in range(2):
+                        nc.tensor.matmul(
+                            s_turned[:, b, :],
+                            es[j][:, 2 * P * b + u : 2 * P * (b + 1) : 2],
+                            ident[:],
+                            start=(u == 0),
+                            stop=(u == 1),
+                            is_transpose=True,
+                        )
+                nc.scalar.activation(root, s_turned[:].rearrange("p b r -> p (b r)"), ACT.Abs_reciprocal_sqrt)
+                nc.scalar.activation(squared[:], root, ACT.Square)
+                inv = bank_tile(inv_banks[j], [P, X], "inv")
+                for b in range(X // P):
+                    nc.tensor.transpose(inv[:, b * P : (b + 1) * P], squared[:, b * P : (b + 1) * P], ident[:])
+            else:
+                nc.scalar.activation(root, sums[j][:], ACT.Abs_reciprocal_sqrt)
+                nc.scalar.activation(squared[:], root, ACT.Square)
+                inv = squared
             h_j = sb([P, H_COLS], F32, "h%d" % j)
             nc.gpsimd.memset(h_j[:, X:H_COLS], 0.0)
             nc.vector.tensor_tensor(h_j[:, 0:X], inv[:], g_in[:, j, :], MULT)
@@ -244,15 +263,15 @@ def tile_attend_gcolb_kernel(tc, qT, wT, us, ts, G, wt, offs, docoffs, slotoffs,
             out_win.append(win)
         out_rows = out.rearrange("(p j) t -> p j t", j=PACK)
 
-        q_pairs = sb([P, PACK * R], BF16, "q_pairs", "root")
+        q_pairs = m1[:, 2 * HALF : 4 * HALF].bitcast(BF16)
         for n in range(2):
             for u in range(2):
                 nc.scalar.activation(
-                    q_pairs[:].rearrange("p (u j s e) -> p u j s e", u=2, j=PACK, e=2)[:, u, :, n * P // 2 : (n + 1) * P // 2, :],
+                    q_pairs.rearrange("p (u j s e) -> p u j s e", u=2, j=PACK, e=2)[:, u, :, n * P // 2 : (n + 1) * P // 2, :],
                     q_raw[n][:].rearrange("p j (s u e) -> p u j s e", u=2, e=2)[:, u],
                     ACT.Copy,
                 )
-        q_words = q_pairs[:].bitcast(F32).rearrange("p (u j s) -> p u j s", u=2, j=PACK)
+        q_words = m1[:, 2 * HALF : 4 * HALF].rearrange("p (u j s) -> p u j s", u=2, j=PACK)
         qb = sb([P, D * PACK], BF16, "qb")
         qb_words = qb[:].bitcast(F32).rearrange("s (j p u) -> s j p u", p=P, u=2)
         for pair in range(2):
@@ -261,8 +280,6 @@ def tile_attend_gcolb_kernel(tc, qT, wT, us, ts, G, wt, offs, docoffs, slotoffs,
                 for u in range(2):
                     nc.tensor.transpose(bank[:, b, u, :], q_words[:, u, 2 * pair + b, :], ident[:])
             nc.scalar.copy(qb_words[:, 2 * pair : 2 * pair + 2], bank[:].rearrange("s b u p -> s b p u"))
-
-        m1 = sb([P, PACK * HALF], F32, "m1")
 
         def gather_second(j):
             nc.vector.tensor_tensor(m1[:, j * HALF : (j + 1) * HALF], h_win[j][:].indirect(half_list(doc, 1)), x[j][1], MULT)
@@ -299,7 +316,7 @@ def tile_attend_gcolb_kernel(tc, qT, wT, us, ts, G, wt, offs, docoffs, slotoffs,
                 start=True,
                 stop=True,
             )
-            dw = sb([P, HALF], F32, "dw", "m1" if (h, j) == (0, 3) else "z%d" % j)
+            dw = sb([P, HALF], F32, "dw", "ts_win" if (h, j) == (0, 3) else "z%d" % j)
             nc.scalar.copy(dw[:], dw_bank[:])
             nc.vector.tensor_copy(out_win[j][:].indirect(half_list(idx, h)), dw[:])
             if h == halves[-1]:
@@ -307,7 +324,7 @@ def tile_attend_gcolb_kernel(tc, qT, wT, us, ts, G, wt, offs, docoffs, slotoffs,
 
         for j in range(3):
             put_dw(0, j, g_first, j)
-        g_grouped = sb([P, HALF * PACK], BF16, "g_grouped")
+        g_grouped = sb([P, HALF * PACK], BF16, "g_grouped", "z0")
         g_second = quantize_g(1, m1[:], g_grouped[:])
         put_dw(0, 3, g_first, 3)
         for j in range(PACK):

@@ -78,8 +78,8 @@ def tile_attend_gcolb_kernel(tc, qT, wT, us, ts, G, wt, offs, docoffs, slotoffs,
             else:
                 nc.scalar.activation(dst, src, ACT.Copy)
 
-        w0 = [load_w(0, n * HALF, HALF, tag) for n, tag in enumerate(["m0", "m1", "factor1", "x2"])]
-        w1 = [load_w(1, n * HALF, HALF, tag) for n, tag in enumerate(["factor2", "x0", "win0", "x1"])]
+        w0 = [load_w(0, n * HALF, HALF, tag) for n, tag in enumerate(["w0a", "m1", "factor1", "x2"])]
+        w1 = [load_w(1, n * HALF, HALF, tag) for n, tag in enumerate(["factor2", "x0", "factor3", "x1"])]
         q_rows = qT.rearrange("(p j) r -> p j r", j=PACK)
         q_raw = [sb([P, PACK, R // 2], F32, "q_raw%d" % n) for n in range(2)]
         for n in range(2):
@@ -88,8 +88,8 @@ def tile_attend_gcolb_kernel(tc, qT, wT, us, ts, G, wt, offs, docoffs, slotoffs,
         nc.sync.dma_start(slot[:], slotoffs)
         doc = sb([P, C // 16], U16, "doc")
         nc.sync.dma_start(doc[:], docoffs)
-        g_in = sb([P, PACK, X], F32, "g_in")
-        nc.sync.dma_start(g_in[:], G.rearrange("(p j) x -> p j x", j=PACK))
+        m0 = sb([P, (PACK + 1) * HALF], F32, "m0")
+        nc.sync.dma_start(m0[:, 0 : PACK * X], G.rearrange("(p j) x -> p (j x)", j=PACK))
 
         for n, raw in enumerate(w0):
             cast_w(0, raw, n * HALF, 0, HALF, n == 3)
@@ -143,7 +143,7 @@ def tile_attend_gcolb_kernel(tc, qT, wT, us, ts, G, wt, offs, docoffs, slotoffs,
             )
             nc.vector.quantize_mx(w_codes[h][:].bitcast(E4M3), w_scales[h][:], w_grouped[:])
 
-        e = [sb([P, C], F32, "e%d" % j, "win%d" % (j - 1) if j >= 2 else None) for j in r_tiles]
+        e = [sb([P, C], F32, "e%d" % j) for j in r_tiles]
         for j in range(2):
             if j == 1:
                 qa = quantize_qa(1, 2)
@@ -188,7 +188,7 @@ def tile_attend_gcolb_kernel(tc, qT, wT, us, ts, G, wt, offs, docoffs, slotoffs,
                     nc.tensor.transpose(bank[:, b * P : (b + 1) * P], y[:, first : first + P], ident[:])
                 nc.scalar.activation(e[j][:, half(h)], bank[:], ACT.Exp, scale=us_col[:, j : j + 1])
 
-        m1 = sb([P, PACK * HALF], F32, "m1", "ts_win")
+        m1 = sb([P, PACK * HALF], F32, "m1")
         x = []
         for j in r_tiles:
             if j < 3:
@@ -202,34 +202,35 @@ def tile_attend_gcolb_kernel(tc, qT, wT, us, ts, G, wt, offs, docoffs, slotoffs,
                 x.append([x_j[:, half(h)] for h in halves])
             else:
                 parts = []
-                factor = sb([P, C], F32, "factor3", "win0")
+                factor = sb([P, C], F32, "factor3")
                 nc.scalar.activation(factor[:], ts_all[:], ACT.Copy, scale=wtus[:, j : j + 1])
                 for h in halves:
-                    part = m1[:, HALF // 2 : 3 * HALF // 2] if h == 0 else sb([P, HALF], F32, "x3b")[:]
+                    part = m1[:, HALF // 2 : 3 * HALF // 2] if h == 0 else sb([P, HALF], F32, "x3b", "win2")[:]
                     nc.gpsimd.tensor_tensor(part, e[j][:, half(h)], factor[:, half(h)], MULT)
                     parts.append(part)
                 x.append(parts)
 
-        sum_banks = [7, 0]
-        inv_banks = [4, 5]
-        es_tags = ["w_win0", "w_win1", "es2", "win3"]
+        sum_banks = [7, 0, 1]
+        inv_banks = [4, 5, 6]
+        es_tags = ["w_win0", "w_win1", "w_pairs", "es3"]
         es = []
-        sums = [None, None]
         for j in r_tiles:
             es_j = sb([P, C], F32, "es%d" % j, es_tags[j])
             for h in halves:
                 nc.vector.tensor_copy(es_j[:, half(h)], e[j][:].indirect(half_list(slot, h)))
             es.append(es_j)
-            if j >= 2:
-                s_j = sb([P, X], F32, "s%d" % j)
-                nc.vector.tensor_tensor(s_j[:], es_j[:, 0:C:2], es_j[:, 1:C:2], ADD)
-                sums.append(s_j)
-        m0 = sb([P, PACK * HALF], F32, "m0")
+        s_last = sb([P, X], F32, "s_last")
+        nc.vector.tensor_tensor(s_last[:], es[3][:, 0:C:2], es[3][:, 1:C:2], ADD)
+        roots = sb([P, 2 * X], F32, "roots", "ts_win")
         h_win = []
+
+        def gather_first(j):
+            nc.vector.tensor_tensor(m0[:, (j + 1) * HALF : (j + 2) * HALF], h_win[j][:].indirect(half_list(doc, 0)), x[j][0], MULT)
+
         for j in r_tiles:
-            root = m1[:, 2 * HALF : 3 * HALF]
-            squared = sb([P, X], F32, "squared%d" % j)
-            if j < 2:
+            root = m1[:, 2 * HALF : 3 * HALF] if j == 3 else roots[:, j % 2 * X : (j % 2 + 1) * X]
+            squared = sb([P, X], F32, "squared%d" % j)[:]
+            if j < 3:
                 s_turned = bank_tile(sum_banks[j], [P, PACK, P], "s_turned")
                 for b in range(X // P):
                     for u in range(2):
@@ -242,25 +243,31 @@ def tile_attend_gcolb_kernel(tc, qT, wT, us, ts, G, wt, offs, docoffs, slotoffs,
                             is_transpose=True,
                         )
                 nc.scalar.activation(root, s_turned[:].rearrange("p b r -> p (b r)"), ACT.Abs_reciprocal_sqrt)
-                nc.scalar.activation(squared[:], root, ACT.Square)
+                nc.scalar.activation(squared, root, ACT.Square)
                 inv = bank_tile(inv_banks[j], [P, X], "inv")
                 for b in range(X // P):
                     nc.tensor.transpose(inv[:, b * P : (b + 1) * P], squared[:, b * P : (b + 1) * P], ident[:])
             else:
-                nc.scalar.activation(root, sums[j][:], ACT.Abs_reciprocal_sqrt)
-                nc.scalar.activation(squared[:], root, ACT.Square)
+                nc.scalar.activation(root, s_last[:], ACT.Abs_reciprocal_sqrt)
+                nc.scalar.activation(squared, root, ACT.Square)
                 inv = squared
-            h_j = sb([P, H_COLS], F32, "h%d" % j)
+            h_j = sb([P, H_COLS], F32, "h%d" % j, "win3" if j == 3 else None)
             nc.gpsimd.memset(h_j[:, X:H_COLS], 0.0)
-            nc.vector.tensor_tensor(h_j[:, 0:X], inv[:], g_in[:, j, :], MULT)
+            nc.vector.tensor_tensor(h_j[:, 0:X], inv[:], m0[:, j * X : (j + 1) * X], MULT)
             h_win.append(h_j)
-            nc.vector.tensor_tensor(m0[:, j * HALF : (j + 1) * HALF], h_j[:].indirect(half_list(doc, 0)), x[j][0], MULT)
+            if j > 0:
+                gather_first(j - 1)
+        gather_first(3)
 
         out_win = []
-        for j in range(PACK):
+
+        def zero_window(j):
             win = sb([P, T], F32, "out_win%d" % j, "win%d" % j)
             nc.gpsimd.memset(win[:].bitcast(I32), 0)
             out_win.append(win)
+
+        for j in range(2):
+            zero_window(j)
         out_rows = out.rearrange("(p j) t -> p j t", j=PACK)
 
         q_pairs = m1[:, 2 * HALF : 4 * HALF].bitcast(BF16)
@@ -300,9 +307,12 @@ def tile_attend_gcolb_kernel(tc, qT, wT, us, ts, G, wt, offs, docoffs, slotoffs,
         qb_codes = sb([P, D], U32, "qb_codes", "x1")
         qb_scales = sb([P, D], U8, "qb_scales")
         nc.vector.quantize_mx(qb_codes[:].bitcast(E4M3), qb_scales[:], qb[:])
-        g_first = quantize_g(0, m0[:], m1[:, 2 * HALF : 4 * HALF].bitcast(BF16))
+        g_first = quantize_g(0, m0[:, HALF : (PACK + 1) * HALF], m1[:, 2 * HALF : 4 * HALF].bitcast(BF16))
         for j in range(2, 4):
             gather_second(j)
+
+        for j in range(2, 4):
+            zero_window(j)
 
         def put_dw(h, j, g_mx, n):
             rows = slice(j * P, (j + 1) * P)
@@ -316,7 +326,7 @@ def tile_attend_gcolb_kernel(tc, qT, wT, us, ts, G, wt, offs, docoffs, slotoffs,
                 start=True,
                 stop=True,
             )
-            dw = sb([P, HALF], F32, "dw", "ts_win" if (h, j) == (0, 3) else "z%d" % j)
+            dw = sb([P, HALF], F32, "dw", "m1" if (h, j) == (0, 3) else "z%d" % j)
             nc.scalar.copy(dw[:], dw_bank[:])
             nc.vector.tensor_copy(out_win[j][:].indirect(half_list(idx, h)), dw[:])
             if h == halves[-1]:

@@ -24,6 +24,8 @@ HALF = 512
 LIST_COLS = HALF // 16
 H_COLS = X + P
 C_TILES = C // P
+E_COLS = C + 3 * P
+SCALAR_COLS = 160
 
 
 def tile_attend_gcolb_kernel(tc, qT, wT, us, ts, G, wt, offs, docoffs, slotoffs, out):
@@ -79,7 +81,7 @@ def tile_attend_gcolb_kernel(tc, qT, wT, us, ts, G, wt, offs, docoffs, slotoffs,
                 nc.scalar.activation(dst, src, ACT.Copy)
 
         w0 = [load_w(0, n * HALF, HALF, tag) for n, tag in enumerate(["w0a", "m1", "factor1", "x2"])]
-        w1 = [load_w(1, n * HALF, HALF, tag) for n, tag in enumerate(["factor2", "x0", "factor3", "x1"])]
+        w1 = [load_w(1, n * HALF, HALF, tag) for n, tag in enumerate(["factor2", "w1b", "factor3", "x1"])]
         q_rows = qT.rearrange("(p j) r -> p j r", j=PACK)
         q_raw = [sb([P, PACK, R // 2], F32, "q_raw%d" % n) for n in range(2)]
         for n in range(2):
@@ -93,8 +95,10 @@ def tile_attend_gcolb_kernel(tc, qT, wT, us, ts, G, wt, offs, docoffs, slotoffs,
 
         for n, raw in enumerate(w0):
             cast_w(0, raw, n * HALF, 0, HALF, n == 3)
-        for n, raw in enumerate(w1):
+        for n, raw in enumerate(w1[:3]):
             cast_w(1, raw, n * HALF, 0, HALF, n % 2 == 1)
+        cast_w(1, w1[3], 3 * HALF, 0, SCALAR_COLS, False)
+        cast_w(1, w1[3], 3 * HALF, SCALAR_COLS, HALF, True)
 
         ts_row = sb([P, C], F32, "ts_row")
         ts_col = sb([P, C_TILES], F32, "ts_col")
@@ -121,15 +125,21 @@ def tile_attend_gcolb_kernel(tc, qT, wT, us, ts, G, wt, offs, docoffs, slotoffs,
         nc.vector.tensor_copy(w_pairs[:, 0:C], w_win[0][:].indirect(idx[:]))
 
         qa_grouped = sb([P, R * PACK], BF16, "qa_grouped")
-        qa_dealt = qa_grouped[:].rearrange("p (j s t) -> p s j t", j=PACK, t=PACK)
-        nc.scalar.activation(qa_dealt[:, 0 : P // 2], q_raw[0][:].rearrange("p t (s j) -> p s j t", j=PACK), ACT.Copy)
+
+        def q_piece(first, n):
+            dealt = qa_grouped[:].rearrange("p (j s t) -> p s j t", j=PACK, t=PACK)
+            source = q_raw[n][:].rearrange("p t (s j) -> p s j t", j=PACK)
+            return dealt[:, n * P // 2 : (n + 1) * P // 2, first : first + 2], source[:, :, first : first + 2]
+
+        nc.scalar.activation(*q_piece(0, 0), ACT.Copy)
+        nc.gpsimd.tensor_scalar(*q_piece(2, 0), 1.0, 0.0, MULT, ADD)
 
         for h in halves:
             nc.vector.tensor_copy(w_pairs[:, C + h * HALF : C + (h + 1) * HALF], w_win[1][:].indirect(half_list(idx, h)))
-        nc.vector.tensor_copy(qa_dealt[:, P // 2 : P], q_raw[1][:].rearrange("p t (s j) -> p s j t", j=PACK))
+        nc.vector.tensor_copy(*q_piece(0, 1))
 
         def quantize_qa(first, last):
-            codes = sb([P, (last - first) * P], U32, "qa_codes%d" % first, ["qa_codes0", "w_grouped1", "z0"][first])
+            codes = sb([P, (last - first) * P], U32, "qa_codes%d" % first, ["qa_codes0", "w_grouped1", "qa_codes2"][first])
             scales = sb([P, (last - first) * P], U8, "qa_scales%d" % first)
             nc.vector.quantize_mx(codes[:].bitcast(E4M3), scales[:], qa_grouped[:, first * P * PACK : last * P * PACK])
             return codes, scales
@@ -143,7 +153,11 @@ def tile_attend_gcolb_kernel(tc, qT, wT, us, ts, G, wt, offs, docoffs, slotoffs,
             )
             nc.vector.quantize_mx(w_codes[h][:].bitcast(E4M3), w_scales[h][:], w_grouped[:])
 
-        e = [sb([P, C], F32, "e%d" % j) for j in r_tiles]
+        nc.scalar.activation(*q_piece(2, 1), ACT.Copy)
+
+        e = [sb([P, E_COLS], F32, "e%d" % j) for j in r_tiles]
+        for j in r_tiles:
+            nc.gpsimd.memset(e[j][:, C:E_COLS], 0.0)
         for j in range(2):
             if j == 1:
                 qa = quantize_qa(1, 2)
@@ -158,7 +172,7 @@ def tile_attend_gcolb_kernel(tc, qT, wT, us, ts, G, wt, offs, docoffs, slotoffs,
                     start=True,
                     stop=True,
                 )
-                z = sb([P, HALF], F32, "z", "ts_win" if 2 * j + h == 3 else "z%d" % (2 * j + h))
+                z = sb([P, HALF], F32, "z", "z%d" % (2 * j + h))
                 nc.vector.tensor_tensor(z[:], a[:], ts_all[:, half(h)], MULT)
                 nc.scalar.activation(e[j][:, half(h)], z[:], ACT.Exp, scale=us_col[:, j : j + 1])
 
@@ -197,8 +211,8 @@ def tile_attend_gcolb_kernel(tc, qT, wT, us, ts, G, wt, offs, docoffs, slotoffs,
                     nc.vector.tensor_scalar(factor[:], ts_all[:], wtus[:, j : j + 1], None, MULT)
                 else:
                     nc.scalar.activation(factor[:], ts_all[:], ACT.Copy, scale=wtus[:, j : j + 1])
-                x_j = sb([P, C], F32, "x%d" % j)
-                nc.gpsimd.tensor_tensor(x_j[:], e[j][:], factor[:], MULT)
+                x_j = sb([P, C], F32, "x%d" % j, "qa_grouped" if j == 0 else None)
+                nc.gpsimd.tensor_tensor(x_j[:], e[j][:, 0:C], factor[:], MULT)
                 x.append([x_j[:, half(h)] for h in halves])
             else:
                 parts = []
@@ -216,8 +230,7 @@ def tile_attend_gcolb_kernel(tc, qT, wT, us, ts, G, wt, offs, docoffs, slotoffs,
         es = []
         for j in r_tiles:
             es_j = sb([P, C], F32, "es%d" % j, es_tags[j])
-            for h in halves:
-                nc.vector.tensor_copy(es_j[:, half(h)], e[j][:].indirect(half_list(slot, h)))
+            nc.vector.tensor_copy(es_j[:], e[j][:].indirect(slot[:]))
             es.append(es_j)
         s_last = sb([P, X], F32, "s_last")
         nc.vector.tensor_tensor(s_last[:], es[3][:, 0:C:2], es[3][:, 1:C:2], ADD)

@@ -80,7 +80,7 @@ def tile_attend_gcolb_kernel(tc, qT, wT, us, ts, G, wt, offs, docoffs, slotoffs,
             else:
                 nc.scalar.activation(dst, src, ACT.Copy)
 
-        w0 = [load_w(0, n * HALF, HALF, tag) for n, tag in enumerate(["w0a", "m1", "factor1", "x2"])]
+        w0 = [load_w(0, n * HALF, HALF, tag) for n, tag in enumerate(["w0a", "m1", "factor1", "win0"])]
         w1 = [load_w(1, n * HALF, HALF, tag) for n, tag in enumerate(["factor2", "w1b", "factor3", "x1"])]
         q_rows = qT.rearrange("(p j) r -> p j r", j=PACK)
         q_raw = [sb([P, PACK, R // 2], F32, "q_raw%d" % n) for n in range(2)]
@@ -124,24 +124,24 @@ def tile_attend_gcolb_kernel(tc, qT, wT, us, ts, G, wt, offs, docoffs, slotoffs,
         w_pairs = sb([P, 2 * C], U32, "w_pairs")
         nc.vector.tensor_copy(w_pairs[:, 0:C], w_win[0][:].indirect(idx[:]))
 
-        qa_grouped = sb([P, R * PACK], BF16, "qa_grouped")
+        qa_grouped = sb([P, R * PACK // 2], BF16, "qa_grouped")
 
-        def q_piece(first, n):
-            dealt = qa_grouped[:].rearrange("p (j s t) -> p s j t", j=PACK, t=PACK)
+        def q_piece(grouped, first, n):
+            dealt = grouped[:].rearrange("p (j s t) -> p s j t", j=2, t=PACK)
             source = q_raw[n][:].rearrange("p t (s j) -> p s j t", j=PACK)
-            return dealt[:, n * P // 2 : (n + 1) * P // 2, first : first + 2], source[:, :, first : first + 2]
+            return dealt[:, n * P // 2 : (n + 1) * P // 2], source[:, :, first : first + 2]
 
-        nc.scalar.activation(*q_piece(0, 0), ACT.Copy)
-        nc.gpsimd.tensor_scalar(*q_piece(2, 0), 1.0, 0.0, MULT, ADD)
+        nc.scalar.activation(*q_piece(qa_grouped, 0, 0), ACT.Copy)
 
         for h in halves:
             nc.vector.tensor_copy(w_pairs[:, C + h * HALF : C + (h + 1) * HALF], w_win[1][:].indirect(half_list(idx, h)))
-        nc.vector.tensor_copy(*q_piece(0, 1))
+        nc.vector.tensor_copy(*q_piece(qa_grouped, 0, 1))
 
         def quantize_qa(first, last):
             codes = sb([P, (last - first) * P], U32, "qa_codes%d" % first, ["qa_codes0", "w_grouped1", "qa_codes2"][first])
             scales = sb([P, (last - first) * P], U8, "qa_scales%d" % first)
-            nc.vector.quantize_mx(codes[:].bitcast(E4M3), scales[:], qa_grouped[:, first * P * PACK : last * P * PACK])
+            source = qa_late_grouped[:] if first == 2 else qa_grouped[:, first * P * PACK : last * P * PACK]
+            nc.vector.quantize_mx(codes[:].bitcast(E4M3), scales[:], source)
             return codes, scales
 
         qa = quantize_qa(0, 1)
@@ -153,7 +153,9 @@ def tile_attend_gcolb_kernel(tc, qT, wT, us, ts, G, wt, offs, docoffs, slotoffs,
             )
             nc.vector.quantize_mx(w_codes[h][:].bitcast(E4M3), w_scales[h][:], w_grouped[:])
 
-        nc.scalar.activation(*q_piece(2, 1), ACT.Copy)
+        qa_late_grouped = sb([P, R * PACK // 2], BF16, "qa_late_grouped", "w_pairs")
+        for n in range(2):
+            nc.scalar.activation(*q_piece(qa_late_grouped, 2, n), ACT.Copy)
 
         e = [sb([P, E_COLS], F32, "e%d" % j) for j in r_tiles]
         for j in r_tiles:
@@ -211,7 +213,7 @@ def tile_attend_gcolb_kernel(tc, qT, wT, us, ts, G, wt, offs, docoffs, slotoffs,
                     nc.vector.tensor_scalar(factor[:], ts_all[:], wtus[:, j : j + 1], None, MULT)
                 else:
                     nc.scalar.activation(factor[:], ts_all[:], ACT.Copy, scale=wtus[:, j : j + 1])
-                x_j = sb([P, C], F32, "x%d" % j, "qa_grouped" if j == 0 else None)
+                x_j = sb([P, C], F32, "x%d" % j, ["w_pairs", "x1", "win1"][j])
                 nc.gpsimd.tensor_tensor(x_j[:], e[j][:, 0:C], factor[:], MULT)
                 x.append([x_j[:, half(h)] for h in halves])
             else:
@@ -226,7 +228,7 @@ def tile_attend_gcolb_kernel(tc, qT, wT, us, ts, G, wt, offs, docoffs, slotoffs,
 
         sum_banks = [7, 0, 1]
         inv_banks = [4, 5, 6]
-        es_tags = ["w_win0", "w_win1", "w_pairs", "es3"]
+        es_tags = ["w_win0", "w_win1", "w1b", "es3"]
         es = []
         for j in r_tiles:
             es_j = sb([P, C], F32, "es%d" % j, es_tags[j])
@@ -279,8 +281,7 @@ def tile_attend_gcolb_kernel(tc, qT, wT, us, ts, G, wt, offs, docoffs, slotoffs,
             nc.gpsimd.memset(win[:].bitcast(I32), 0)
             out_win.append(win)
 
-        for j in range(2):
-            zero_window(j)
+        zero_window(0)
         out_rows = out.rearrange("(p j) t -> p j t", j=PACK)
 
         q_pairs = m1[:, 2 * HALF : 4 * HALF].bitcast(BF16)
@@ -324,7 +325,7 @@ def tile_attend_gcolb_kernel(tc, qT, wT, us, ts, G, wt, offs, docoffs, slotoffs,
         for j in range(2, 4):
             gather_second(j)
 
-        for j in range(2, 4):
+        for j in range(1, 4):
             zero_window(j)
 
         def put_dw(h, j, g_mx, n):

@@ -54,12 +54,7 @@ def tile_attend_gcolb_kernel(tc, qT, wT, us, ts, G, wt, offs, docoffs, slotoffs,
 
         ts_win = sb([P, T], F32, "ts_win")
         nc.sync.dma_start(ts_win[P - 1 : P, :], ts[0:1, :])
-        nc.vector.memset(ts_win[0 : P - 1, :].bitcast(I32), 0)
-
-        us_col = sb([P, PACK], F32, "us_col")
-        nc.sync.dma_start(us_col[:], us.rearrange("(p j) o -> p (j o)", j=PACK))
-        wt_col = sb([P, PACK], F32, "wt_col")
-        nc.sync.dma_start(wt_col[:], wt.rearrange("(p j) o -> p (j o)", j=PACK))
+        nc.gpsimd.memset(ts_win[0 : P - 1, :].bitcast(I32), 0)
 
         ident = sb([P, P], F32, "ident")
         make_identity(nc, ident[:])
@@ -81,11 +76,14 @@ def tile_attend_gcolb_kernel(tc, qT, wT, us, ts, G, wt, offs, docoffs, slotoffs,
                 nc.scalar.activation(dst, src, ACT.Copy)
 
         w0 = [load_w(0, n * HALF, HALF, tag) for n, tag in enumerate(["w0a", "m1", "factor1", "win0"])]
-        w1 = [load_w(1, n * HALF, HALF, tag) for n, tag in enumerate(["factor2", "w1b", "factor3", "x1"])]
+        us_col = sb([P, PACK], F32, "us_col")
+        nc.sync.dma_start(us_col[:], us.rearrange("(p j) o -> p (j o)", j=PACK))
+        wt_col = sb([P, PACK], F32, "wt_col")
+        nc.sync.dma_start(wt_col[:], wt.rearrange("(p j) o -> p (j o)", j=PACK))
+        w1 = [load_w(1, n * HALF, HALF, tag) for n, tag in enumerate(["factor2", "w1b", "x1", "factor3"])]
         q_rows = qT.rearrange("(p j) r -> p j r", j=PACK)
-        q_raw = [sb([P, PACK, R // 2], F32, "q_raw%d" % n) for n in range(2)]
-        for n in range(2):
-            nc.sync.dma_start(q_raw[n][:], q_rows[:, :, n * R // 2 : (n + 1) * R // 2])
+        q_raw = sb([P, PACK, R], F32, "q_raw")
+        nc.sync.dma_start(q_raw[:], q_rows)
         slot = sb([P, C // 16], U16, "slot")
         nc.sync.dma_start(slot[:], slotoffs)
         doc = sb([P, C // 16], U16, "doc")
@@ -94,13 +92,13 @@ def tile_attend_gcolb_kernel(tc, qT, wT, us, ts, G, wt, offs, docoffs, slotoffs,
         nc.sync.dma_start(m0[:, 0 : PACK * X], G.rearrange("(p j) x -> p (j x)", j=PACK))
 
         for n, raw in enumerate(w0):
-            cast_w(0, raw, n * HALF, 0, HALF, n == 3)
+            cast_w(0, raw, n * HALF, 0, HALF, False)
         for n, raw in enumerate(w1[:3]):
-            cast_w(1, raw, n * HALF, 0, HALF, n % 2 == 1)
+            cast_w(1, raw, n * HALF, 0, HALF, False)
         cast_w(1, w1[3], 3 * HALF, 0, SCALAR_COLS, False)
         cast_w(1, w1[3], 3 * HALF, SCALAR_COLS, HALF, True)
 
-        ts_row = sb([P, C], F32, "ts_row")
+        ts_row = sb([P, C], F32, "ts_row", "w_pairs")
         ts_col = sb([P, C_TILES], F32, "ts_col")
         ts_all = sb([P, C], F32, "ts_all")
         for h in halves:
@@ -117,7 +115,7 @@ def tile_attend_gcolb_kernel(tc, qT, wT, us, ts, G, wt, offs, docoffs, slotoffs,
                 nc.tensor.transpose(bank[:, b, :], ts_col[:, k : k + 1].to_broadcast([P, P]), ident[:])
             nc.vector.tensor_copy(ts_all[:, half(h)], bank[:].rearrange("p b c -> p (b c)"))
         wtus = sb([P, PACK], F32, "wtus")
-        nc.vector.tensor_tensor(wtus[:], us_col[:], wt_col[:], MULT)
+        nc.gpsimd.tensor_tensor(wtus[:], us_col[:], wt_col[:], MULT)
 
         w_codes = [sb([P, HALF], U32, "w_codes%d" % h) for h in halves]
         w_scales = [sb([P, HALF], U8, "w_scales%d" % h) for h in halves]
@@ -126,25 +124,21 @@ def tile_attend_gcolb_kernel(tc, qT, wT, us, ts, G, wt, offs, docoffs, slotoffs,
 
         qa_grouped = sb([P, R * PACK // 2], BF16, "qa_grouped")
 
-        def q_piece(grouped, first, n):
+        def q_piece(grouped, first):
             dealt = grouped[:].rearrange("p (j s t) -> p s j t", j=2, t=PACK)
-            source = q_raw[n][:].rearrange("p t (s j) -> p s j t", j=PACK)
-            return dealt[:, n * P // 2 : (n + 1) * P // 2], source[:, :, first : first + 2]
-
-        nc.scalar.activation(*q_piece(qa_grouped, 0, 0), ACT.Copy)
+            source = q_raw[:].rearrange("p t (s j) -> p s j t", j=PACK)
+            return dealt, source[:, :, first : first + 2]
 
         for h in halves:
             nc.vector.tensor_copy(w_pairs[:, C + h * HALF : C + (h + 1) * HALF], w_win[1][:].indirect(half_list(idx, h)))
-        nc.vector.tensor_copy(*q_piece(qa_grouped, 0, 1))
+        nc.vector.tensor_copy(*q_piece(qa_grouped, 0))
 
-        def quantize_qa(first, last):
-            codes = sb([P, (last - first) * P], U32, "qa_codes%d" % first, ["qa_codes0", "w_grouped1", "qa_codes2"][first])
-            scales = sb([P, (last - first) * P], U8, "qa_scales%d" % first)
-            source = qa_late_grouped[:] if first == 2 else qa_grouped[:, first * P * PACK : last * P * PACK]
-            nc.vector.quantize_mx(codes[:].bitcast(E4M3), scales[:], source)
+        def quantize_qa(first, source):
+            codes = sb([P, 2 * P], U32, "qa_codes%d" % first)
+            scales = sb([P, 2 * P], U8, "qa_scales%d" % first)
+            nc.vector.quantize_mx(codes[:].bitcast(E4M3), scales[:], source[:])
             return codes, scales
 
-        qa = quantize_qa(0, 1)
         for h in halves:
             w_grouped = sb([P, HALF * PACK], BF16, "w_grouped%d" % h)
             nc.scalar.copy(
@@ -152,35 +146,35 @@ def tile_attend_gcolb_kernel(tc, qT, wT, us, ts, G, wt, offs, docoffs, slotoffs,
                 w_pairs[:].rearrange("p (u c) -> p c u", u=2)[:, half(h), :],
             )
             nc.vector.quantize_mx(w_codes[h][:].bitcast(E4M3), w_scales[h][:], w_grouped[:])
+            if h == 0:
+                qa = quantize_qa(0, qa_grouped)
 
         qa_late_grouped = sb([P, R * PACK // 2], BF16, "qa_late_grouped", "w_pairs")
-        for n in range(2):
-            nc.scalar.activation(*q_piece(qa_late_grouped, 2, n), ACT.Copy)
+        nc.scalar.activation(*[side.rearrange("p s j t -> p s t j") for side in q_piece(qa_late_grouped, 2)], ACT.Copy)
+        qa_late = quantize_qa(2, qa_late_grouped)
 
         e = [sb([P, E_COLS], F32, "e%d" % j) for j in r_tiles]
         for j in r_tiles:
             nc.gpsimd.memset(e[j][:, C:E_COLS], 0.0)
-        for j in range(2):
-            if j == 1:
-                qa = quantize_qa(1, 2)
+        y = sb([P, C_TILES * 2 * P], F32, "y", "ts_win")
+
+        def direct(j):
             for h in halves:
                 a = bank_tile(2 * j + h, [P, HALF], "a")
                 nc.tensor.matmul_mx(
                     a[:],
-                    lhsT=qa[0][:].bitcast(E4M3),
-                    lhsT_scale=qa[1][:],
+                    lhsT=qa[0][:, j * P : (j + 1) * P].bitcast(E4M3),
+                    lhsT_scale=qa[1][:, j * P : (j + 1) * P],
                     rhs=w_codes[h][:].bitcast(E4M3),
                     rhs_scale=w_scales[h][:],
                     start=True,
                     stop=True,
                 )
-                z = sb([P, HALF], F32, "z", "z%d" % (2 * j + h))
+                z = sb([P, HALF], F32, "z", ["z0", "z1", "z0", "z3"][2 * j + h])
                 nc.vector.tensor_tensor(z[:], a[:], ts_all[:, half(h)], MULT)
                 nc.scalar.activation(e[j][:, half(h)], z[:], ACT.Exp, scale=us_col[:, j : j + 1])
 
-        qa_late = quantize_qa(2, 4)
-        y = sb([P, C_TILES * 2 * P], F32, "y", "ts_win")
-        for pair in range(C_TILES // 2):
+        def turned(pair):
             a_turned = bank_tile(4 + pair, [P, 2, 2 * P], "a_turned")
             for b in range(2):
                 k = 2 * pair + b
@@ -196,6 +190,12 @@ def tile_attend_gcolb_kernel(tc, qT, wT, us, ts, G, wt, offs, docoffs, slotoffs,
             for b in range(2):
                 k = 2 * pair + b
                 nc.scalar.activation(y[:, 2 * k * P : 2 * (k + 1) * P], a_turned[:, b, :], ACT.Copy, scale=ts_col[:, k : k + 1])
+
+        direct(0)
+        turned(0)
+        direct(1)
+        for pair in range(1, C_TILES // 2):
+            turned(pair)
         for j in range(2, 4):
             for h in halves:
                 bank = bank_tile(2 * (j - 2) + h, [P, HALF], "y_turned")
@@ -209,17 +209,14 @@ def tile_attend_gcolb_kernel(tc, qT, wT, us, ts, G, wt, offs, docoffs, slotoffs,
         for j in r_tiles:
             if j < 3:
                 factor = sb([P, C], F32, "factor%d" % j)
-                if j == 0:
-                    nc.vector.tensor_scalar(factor[:], ts_all[:], wtus[:, j : j + 1], None, MULT)
-                else:
-                    nc.scalar.activation(factor[:], ts_all[:], ACT.Copy, scale=wtus[:, j : j + 1])
+                nc.gpsimd.tensor_scalar(factor[:], ts_all[:], wtus[:, j : j + 1], 0.0, MULT, ADD)
                 x_j = sb([P, C], F32, "x%d" % j, ["w_pairs", "x1", "win1"][j])
                 nc.gpsimd.tensor_tensor(x_j[:], e[j][:, 0:C], factor[:], MULT)
                 x.append([x_j[:, half(h)] for h in halves])
             else:
                 parts = []
                 factor = sb([P, C], F32, "factor3")
-                nc.scalar.activation(factor[:], ts_all[:], ACT.Copy, scale=wtus[:, j : j + 1])
+                nc.gpsimd.tensor_scalar(factor[:], ts_all[:], wtus[:, j : j + 1], 0.0, MULT, ADD)
                 for h in halves:
                     part = m1[:, HALF // 2 : 3 * HALF // 2] if h == 0 else sb([P, HALF], F32, "x3b", "win2")[:]
                     nc.gpsimd.tensor_tensor(part, e[j][:, half(h)], factor[:, half(h)], MULT)
@@ -285,13 +282,12 @@ def tile_attend_gcolb_kernel(tc, qT, wT, us, ts, G, wt, offs, docoffs, slotoffs,
         out_rows = out.rearrange("(p j) t -> p j t", j=PACK)
 
         q_pairs = m1[:, 2 * HALF : 4 * HALF].bitcast(BF16)
-        for n in range(2):
-            for u in range(2):
-                nc.scalar.activation(
-                    q_pairs.rearrange("p (u j s e) -> p u j s e", u=2, j=PACK, e=2)[:, u, :, n * P // 2 : (n + 1) * P // 2, :],
-                    q_raw[n][:].rearrange("p j (s u e) -> p u j s e", u=2, e=2)[:, u],
-                    ACT.Copy,
-                )
+        for u in range(2):
+            nc.scalar.activation(
+                q_pairs.rearrange("p (u j s e) -> p u j s e", u=2, j=PACK, e=2)[:, u],
+                q_raw[:].rearrange("p j (s u e) -> p u j s e", u=2, e=2)[:, u],
+                ACT.Copy,
+            )
         q_words = m1[:, 2 * HALF : 4 * HALF].rearrange("p (u j s) -> p u j s", u=2, j=PACK)
         qb = sb([P, D * PACK], BF16, "qb")
         qb_words = qb[:].bitcast(F32).rearrange("s (j p u) -> s j p u", p=P, u=2)

@@ -56,8 +56,19 @@ def tile_attend_gcolb_kernel(tc, qT, wT, us, ts, G, wt, offs, docoffs, slotoffs,
         nc.sync.dma_start(ts_win[P - 1 : P, :], ts[0:1, :])
         nc.gpsimd.memset(ts_win[0 : P - 1, :].bitcast(I32), 0)
 
+        us_col = sb([P, PACK], F32, "us_col")
+        nc.sync.dma_start(us_col[:], us.rearrange("(p j) o -> p (j o)", j=PACK))
+        wt_col = sb([P, PACK], F32, "wt_col")
+        nc.sync.dma_start(wt_col[:], wt.rearrange("(p j) o -> p (j o)", j=PACK))
+
         ident = sb([P, P], F32, "ident")
         make_identity(nc, ident[:])
+        e = [sb([P, E_COLS], F32, "e%d" % j) for j in r_tiles]
+        for j in r_tiles:
+            nc.gpsimd.memset(e[j][:, C:E_COLS], 0.0)
+        h_early = [sb([P, H_COLS], F32, "h%d" % j) for j in range(3)]
+        for j in range(3):
+            nc.gpsimd.memset(h_early[j][:, X:H_COLS], 0.0)
 
         w_rows = wT.rearrange("(p j) t -> p j t", j=PACK)
         w_win = [sb([P, T], U32, "w_win%d" % u) for u in range(2)]
@@ -75,12 +86,8 @@ def tile_attend_gcolb_kernel(tc, qT, wT, us, ts, G, wt, offs, docoffs, slotoffs,
             else:
                 nc.scalar.activation(dst, src, ACT.Copy)
 
-        w0 = [load_w(0, n * HALF, HALF, tag) for n, tag in enumerate(["w0a", "m1", "factor1", "win0"])]
-        us_col = sb([P, PACK], F32, "us_col")
-        nc.sync.dma_start(us_col[:], us.rearrange("(p j) o -> p (j o)", j=PACK))
-        wt_col = sb([P, PACK], F32, "wt_col")
-        nc.sync.dma_start(wt_col[:], wt.rearrange("(p j) o -> p (j o)", j=PACK))
-        w1 = [load_w(1, n * HALF, HALF, tag) for n, tag in enumerate(["factor2", "w1b", "x1", "factor3"])]
+        w0 = [load_w(0, n * HALF, HALF, tag) for n, tag in enumerate(["factor1", "factor2", "m1", "win0"])]
+        w1 = [load_w(1, n * HALF, HALF, tag) for n, tag in enumerate(["es3", "w1b", "x1", "factor3"])]
         q_rows = qT.rearrange("(p j) r -> p j r", j=PACK)
         q_raw = sb([P, PACK, R], F32, "q_raw")
         nc.sync.dma_start(q_raw[:], q_rows)
@@ -95,8 +102,7 @@ def tile_attend_gcolb_kernel(tc, qT, wT, us, ts, G, wt, offs, docoffs, slotoffs,
             cast_w(0, raw, n * HALF, 0, HALF, False)
         for n, raw in enumerate(w1[:3]):
             cast_w(1, raw, n * HALF, 0, HALF, False)
-        cast_w(1, w1[3], 3 * HALF, 0, SCALAR_COLS, False)
-        cast_w(1, w1[3], 3 * HALF, SCALAR_COLS, HALF, True)
+        cast_w(1, w1[3], 3 * HALF, 0, HALF, True)
 
         ts_row = sb([P, C], F32, "ts_row", "w_pairs")
         ts_col = sb([P, C_TILES], F32, "ts_col")
@@ -115,7 +121,11 @@ def tile_attend_gcolb_kernel(tc, qT, wT, us, ts, G, wt, offs, docoffs, slotoffs,
                 nc.tensor.transpose(bank[:, b, :], ts_col[:, k : k + 1].to_broadcast([P, P]), ident[:])
             nc.vector.tensor_copy(ts_all[:, half(h)], bank[:].rearrange("p b c -> p (b c)"))
         wtus = sb([P, PACK], F32, "wtus")
-        nc.gpsimd.tensor_tensor(wtus[:], us_col[:], wt_col[:], MULT)
+        nc.vector.tensor_tensor(wtus[:, 1:PACK], us_col[:, 1:PACK], wt_col[:, 1:PACK], MULT)
+        wtus_first = sb([P, 1], F32, "wtus_first", "w_pairs")
+        nc.vector.tensor_tensor(wtus_first[:], us_col[:, 0:1], wt_col[:, 0:1], MULT)
+        factor_first = sb([P, C], F32, "factor0")
+        nc.vector.tensor_scalar(factor_first[:], ts_all[:], wtus_first[:], None, MULT)
 
         w_codes = [sb([P, HALF], U32, "w_codes%d" % h) for h in halves]
         w_scales = [sb([P, HALF], U8, "w_scales%d" % h) for h in halves]
@@ -131,7 +141,7 @@ def tile_attend_gcolb_kernel(tc, qT, wT, us, ts, G, wt, offs, docoffs, slotoffs,
 
         for h in halves:
             nc.vector.tensor_copy(w_pairs[:, C + h * HALF : C + (h + 1) * HALF], w_win[1][:].indirect(half_list(idx, h)))
-        nc.vector.tensor_copy(*q_piece(qa_grouped, 0))
+        nc.vector.tensor_copy(*[side.rearrange("p s j t -> p s t j") for side in q_piece(qa_grouped, 0)])
 
         def quantize_qa(first, source):
             codes = sb([P, 2 * P], U32, "qa_codes%d" % first)
@@ -153,9 +163,6 @@ def tile_attend_gcolb_kernel(tc, qT, wT, us, ts, G, wt, offs, docoffs, slotoffs,
         nc.scalar.activation(*[side.rearrange("p s j t -> p s t j") for side in q_piece(qa_late_grouped, 2)], ACT.Copy)
         qa_late = quantize_qa(2, qa_late_grouped)
 
-        e = [sb([P, E_COLS], F32, "e%d" % j) for j in r_tiles]
-        for j in r_tiles:
-            nc.gpsimd.memset(e[j][:, C:E_COLS], 0.0)
         y = sb([P, C_TILES * 2 * P], F32, "y", "ts_win")
 
         def direct(j):
@@ -208,8 +215,11 @@ def tile_attend_gcolb_kernel(tc, qT, wT, us, ts, G, wt, offs, docoffs, slotoffs,
         x = []
         for j in r_tiles:
             if j < 3:
-                factor = sb([P, C], F32, "factor%d" % j)
-                nc.gpsimd.tensor_scalar(factor[:], ts_all[:], wtus[:, j : j + 1], 0.0, MULT, ADD)
+                if j == 0:
+                    factor = factor_first
+                else:
+                    factor = sb([P, C], F32, "factor%d" % j)
+                    nc.gpsimd.tensor_scalar(factor[:], ts_all[:], wtus[:, j : j + 1], 0.0, MULT, ADD)
                 x_j = sb([P, C], F32, "x%d" % j, ["w_pairs", "x1", "win1"][j])
                 nc.gpsimd.tensor_tensor(x_j[:], e[j][:, 0:C], factor[:], MULT)
                 x.append([x_j[:, half(h)] for h in halves])
@@ -263,8 +273,11 @@ def tile_attend_gcolb_kernel(tc, qT, wT, us, ts, G, wt, offs, docoffs, slotoffs,
                 nc.scalar.activation(root, s_last[:], ACT.Abs_reciprocal_sqrt)
                 nc.scalar.activation(squared, root, ACT.Square)
                 inv = squared
-            h_j = sb([P, H_COLS], F32, "h%d" % j, "win3" if j == 3 else None)
-            nc.gpsimd.memset(h_j[:, X:H_COLS], 0.0)
+            if j < 3:
+                h_j = h_early[j]
+            else:
+                h_j = sb([P, H_COLS], F32, "h3", "win3")
+                nc.gpsimd.memset(h_j[:, X:H_COLS], 0.0)
             nc.vector.tensor_tensor(h_j[:, 0:X], inv[:], m0[:, j * X : (j + 1) * X], MULT)
             h_win.append(h_j)
             if j > 0:

@@ -87,10 +87,11 @@ def tile_attend_gcolb_kernel(tc, qT, wT, us, ts, G, wt, offs, docoffs, slotoffs,
                 nc.scalar.activation(dst, src, ACT.Copy)
 
         w0 = [load_w(0, n * HALF, HALF, tag) for n, tag in enumerate(["factor1", "factor2", "m1", "win0"])]
-        w1 = [load_w(1, n * HALF, HALF, tag) for n, tag in enumerate(["es3", "w1b", "x1", "factor3"])]
+        w1 = [load_w(1, n * HALF, HALF, tag) for n, tag in enumerate(["es3", "w1b", "x1", "w1d"])]
         q_rows = qT.rearrange("(p j) r -> p j r", j=PACK)
-        q_raw = sb([P, PACK, R], F32, "q_raw")
-        nc.sync.dma_start(q_raw[:], q_rows)
+        q_raw = [sb([P, PACK, R // 2], F32, "q_raw%d" % n) for n in range(2)]
+        for n in range(2):
+            nc.sync.dma_start(q_raw[n][:], q_rows[:, :, n * R // 2 : (n + 1) * R // 2])
         slot = sb([P, C // 16], U16, "slot")
         nc.sync.dma_start(slot[:], slotoffs)
         doc = sb([P, C // 16], U16, "doc")
@@ -102,7 +103,8 @@ def tile_attend_gcolb_kernel(tc, qT, wT, us, ts, G, wt, offs, docoffs, slotoffs,
             cast_w(0, raw, n * HALF, 0, HALF, False)
         for n, raw in enumerate(w1[:3]):
             cast_w(1, raw, n * HALF, 0, HALF, False)
-        cast_w(1, w1[3], 3 * HALF, 0, HALF, True)
+        cast_w(1, w1[3], 3 * HALF, SCALAR_COLS, HALF, True)
+        cast_w(1, w1[3], 3 * HALF, 0, SCALAR_COLS, False)
 
         ts_row = sb([P, C], F32, "ts_row", "w_pairs")
         ts_col = sb([P, C_TILES], F32, "ts_col")
@@ -127,21 +129,31 @@ def tile_attend_gcolb_kernel(tc, qT, wT, us, ts, G, wt, offs, docoffs, slotoffs,
         factor_first = sb([P, C], F32, "factor0")
         nc.vector.tensor_scalar(factor_first[:], ts_all[:], wtus_first[:], None, MULT)
 
-        w_codes = [sb([P, HALF], U32, "w_codes%d" % h) for h in halves]
+        w_codes = []
         w_scales = [sb([P, HALF], U8, "w_scales%d" % h) for h in halves]
         w_pairs = sb([P, 2 * C], U32, "w_pairs")
         nc.vector.tensor_copy(w_pairs[:, 0:C], w_win[0][:].indirect(idx[:]))
 
         qa_grouped = sb([P, R * PACK // 2], BF16, "qa_grouped")
 
-        def q_piece(grouped, first):
-            dealt = grouped[:].rearrange("p (j s t) -> p s j t", j=2, t=PACK)
-            source = q_raw[:].rearrange("p t (s j) -> p s j t", j=PACK)
-            return dealt, source[:, :, first : first + 2]
+        def q_piece(grouped, first, n):
+            dealt = grouped[:].rearrange("p (j s t) -> p s t j", j=2, t=PACK)
+            source = q_raw[n][:].rearrange("p t (s j) -> p s t j", j=PACK)
+            return dealt[:, n * P // 2 : (n + 1) * P // 2], source[:, :, :, first : first + 2]
 
         for h in halves:
             nc.vector.tensor_copy(w_pairs[:, C + h * HALF : C + (h + 1) * HALF], w_win[1][:].indirect(half_list(idx, h)))
-        nc.vector.tensor_copy(*[side.rearrange("p s j t -> p s t j") for side in q_piece(qa_grouped, 0)])
+        nc.scalar.activation(*q_piece(qa_grouped, 0, 0), ACT.Copy)
+        late_first = sb([P, R], BF16, "qa_late_grouped0")
+        nc.gpsimd.tensor_scalar(
+            late_first[:].rearrange("p (j s t) -> p s j t", j=2, t=PACK),
+            q_raw[0][:].rearrange("p t (s j) -> p s j t", j=PACK)[:, :, 2:4],
+            1.0,
+            0.0,
+            MULT,
+            ADD,
+        )
+        nc.gpsimd.tensor_scalar(*[side.rearrange("p s t j -> p s j t") for side in q_piece(qa_grouped, 0, 1)], 1.0, 0.0, MULT, ADD)
 
         def quantize_qa(first, source):
             codes = sb([P, 2 * P], U32, "qa_codes%d" % first)
@@ -155,13 +167,21 @@ def tile_attend_gcolb_kernel(tc, qT, wT, us, ts, G, wt, offs, docoffs, slotoffs,
                 w_grouped[:].bitcast(U32).rearrange("p (c u) -> p c u", u=2),
                 w_pairs[:].rearrange("p (u c) -> p c u", u=2)[:, half(h), :],
             )
+            w_codes.append(sb([P, HALF], U32, "w_codes%d" % h, ["w_codes0", "qa_grouped"][h]))
             nc.vector.quantize_mx(w_codes[h][:].bitcast(E4M3), w_scales[h][:], w_grouped[:])
             if h == 0:
                 qa = quantize_qa(0, qa_grouped)
 
-        qa_late_grouped = sb([P, R * PACK // 2], BF16, "qa_late_grouped", "w_pairs")
-        nc.scalar.activation(*[side.rearrange("p s j t -> p s t j") for side in q_piece(qa_late_grouped, 2)], ACT.Copy)
-        qa_late = quantize_qa(2, qa_late_grouped)
+        qa_late = (sb([P, 2 * P], U32, "qa_late_codes"), sb([P, 2 * P], U8, "qa_late_scales"))
+        for n in range(2):
+            if n == 0:
+                late = late_first
+            else:
+                late = sb([P, R], BF16, "qa_late_grouped1", "w_pairs")
+                dealt = late[:].rearrange("p (j s t) -> p s t j", j=2, t=PACK)
+                source = q_raw[n][:].rearrange("p t (s j) -> p s t j", j=PACK)[:, :, :, 2:4]
+                nc.scalar.activation(dealt, source, ACT.Copy)
+            nc.vector.quantize_mx(qa_late[0][:, n * P : (n + 1) * P].bitcast(E4M3), qa_late[1][:, n * P : (n + 1) * P], late[:])
 
         y = sb([P, C_TILES * 2 * P], F32, "y", "ts_win")
 
@@ -196,7 +216,12 @@ def tile_attend_gcolb_kernel(tc, qT, wT, us, ts, G, wt, offs, docoffs, slotoffs,
                 )
             for b in range(2):
                 k = 2 * pair + b
-                nc.scalar.activation(y[:, 2 * k * P : 2 * (k + 1) * P], a_turned[:, b, :], ACT.Copy, scale=ts_col[:, k : k + 1])
+                nc.scalar.activation(
+                    y[:, 2 * k * P : 2 * (k + 1) * P].rearrange("p (j n s) -> p n j s", j=2, n=2),
+                    a_turned[:, b, :].rearrange("p (n j s) -> p n j s", j=2, n=2),
+                    ACT.Copy,
+                    scale=ts_col[:, k : k + 1],
+                )
 
         direct(0)
         turned(0)
@@ -225,7 +250,7 @@ def tile_attend_gcolb_kernel(tc, qT, wT, us, ts, G, wt, offs, docoffs, slotoffs,
                 x.append([x_j[:, half(h)] for h in halves])
             else:
                 parts = []
-                factor = sb([P, C], F32, "factor3")
+                factor = sb([P, C], F32, "factor3", "w_grouped1")
                 nc.gpsimd.tensor_scalar(factor[:], ts_all[:], wtus[:, j : j + 1], 0.0, MULT, ADD)
                 for h in halves:
                     part = m1[:, HALF // 2 : 3 * HALF // 2] if h == 0 else sb([P, HALF], F32, "x3b", "win2")[:]
@@ -295,12 +320,13 @@ def tile_attend_gcolb_kernel(tc, qT, wT, us, ts, G, wt, offs, docoffs, slotoffs,
         out_rows = out.rearrange("(p j) t -> p j t", j=PACK)
 
         q_pairs = m1[:, 2 * HALF : 4 * HALF].bitcast(BF16)
-        for u in range(2):
-            nc.scalar.activation(
-                q_pairs.rearrange("p (u j s e) -> p u j s e", u=2, j=PACK, e=2)[:, u],
-                q_raw[:].rearrange("p j (s u e) -> p u j s e", u=2, e=2)[:, u],
-                ACT.Copy,
-            )
+        for n in range(2):
+            for u in range(2):
+                nc.scalar.activation(
+                    q_pairs.rearrange("p (u j s e) -> p u j s e", u=2, j=PACK, e=2)[:, u, :, n * P // 2 : (n + 1) * P // 2, :],
+                    q_raw[n][:].rearrange("p j (s u e) -> p u j s e", u=2, e=2)[:, u],
+                    ACT.Copy,
+                )
         q_words = m1[:, 2 * HALF : 4 * HALF].rearrange("p (u j s) -> p u j s", u=2, j=PACK)
         qb = sb([P, D * PACK], BF16, "qb")
         qb_words = qb[:].bitcast(F32).rearrange("s (j p u) -> s j p u", p=P, u=2)

@@ -66,7 +66,7 @@ def tile_attend_gcolb_kernel(tc, qT, wT, us, ts, G, wt, offs, docoffs, slotoffs,
         e = [sb([P, E_COLS], F32, "e%d" % j) for j in r_tiles]
         for j in r_tiles:
             nc.gpsimd.memset(e[j][:, C:E_COLS], 0.0)
-        h_early = [sb([P, H_COLS], F32, "h%d" % j) for j in range(3)]
+        h_early = [sb([P, H_COLS], F32, "h%d" % j, ["h0", "h1", "win2"][j]) for j in range(3)]
         for j in range(3):
             nc.gpsimd.memset(h_early[j][:, X:H_COLS], 0.0)
 
@@ -86,7 +86,7 @@ def tile_attend_gcolb_kernel(tc, qT, wT, us, ts, G, wt, offs, docoffs, slotoffs,
             else:
                 nc.scalar.activation(dst, src, ACT.Copy)
 
-        w0 = [load_w(0, n * HALF, HALF, tag) for n, tag in enumerate(["factor1", "factor2", "m1", "win0"])]
+        w0 = [load_w(0, n * HALF, HALF, tag) for n, tag in enumerate(["factor1", "factor2", "m1", "squared0"])]
         w1 = [load_w(1, n * HALF, HALF, tag) for n, tag in enumerate(["es3", "w1b", "x1", "w1d"])]
         q_rows = qT.rearrange("(p j) r -> p j r", j=PACK)
         q_raw = [sb([P, PACK, R // 2], F32, "q_raw%d" % n) for n in range(2)]
@@ -183,6 +183,9 @@ def tile_attend_gcolb_kernel(tc, qT, wT, us, ts, G, wt, offs, docoffs, slotoffs,
                 nc.scalar.activation(dealt, source, ACT.Copy)
             nc.vector.quantize_mx(qa_late[0][:, n * P : (n + 1) * P].bitcast(E4M3), qa_late[1][:, n * P : (n + 1) * P], late[:])
 
+        factor_last = sb([P, C], F32, "factor3", "w_pairs")
+        nc.gpsimd.tensor_scalar(factor_last[:], ts_all[:], wtus[:, 3:4], 0.0, MULT, ADD)
+
         y = sb([P, C_TILES * 2 * P], F32, "y", "ts_win")
 
         def direct(j):
@@ -245,17 +248,14 @@ def tile_attend_gcolb_kernel(tc, qT, wT, us, ts, G, wt, offs, docoffs, slotoffs,
                 else:
                     factor = sb([P, C], F32, "factor%d" % j)
                     nc.gpsimd.tensor_scalar(factor[:], ts_all[:], wtus[:, j : j + 1], 0.0, MULT, ADD)
-                x_j = sb([P, C], F32, "x%d" % j, ["w_pairs", "x1", "win1"][j])
+                x_j = sb([P, C], F32, "x%d" % j, ["w_grouped1", "x1", "win1"][j])
                 nc.gpsimd.tensor_tensor(x_j[:], e[j][:, 0:C], factor[:], MULT)
                 x.append([x_j[:, half(h)] for h in halves])
             else:
                 parts = []
-                factor = sb([P, C], F32, "factor3", "w_grouped1")
-                nc.gpsimd.tensor_scalar(factor[:], ts_all[:], wtus[:, j : j + 1], 0.0, MULT, ADD)
-                for h in halves:
-                    part = m1[:, HALF // 2 : 3 * HALF // 2] if h == 0 else sb([P, HALF], F32, "x3b", "win2")[:]
-                    nc.gpsimd.tensor_tensor(part, e[j][:, half(h)], factor[:, half(h)], MULT)
-                    parts.append(part)
+                factor = factor_last
+                parts.append(m1[:, HALF // 2 : 3 * HALF // 2])
+                nc.gpsimd.tensor_tensor(parts[0], e[j][:, half(0)], factor[:, half(0)], MULT)
                 x.append(parts)
 
         sum_banks = [7, 0, 1]
@@ -268,6 +268,9 @@ def tile_attend_gcolb_kernel(tc, qT, wT, us, ts, G, wt, offs, docoffs, slotoffs,
             es.append(es_j)
         s_last = sb([P, X], F32, "s_last")
         nc.vector.tensor_tensor(s_last[:], es[3][:, 0:C:2], es[3][:, 1:C:2], ADD)
+        x_last = sb([P, HALF], F32, "x_last", "es3")
+        nc.gpsimd.tensor_tensor(x_last[:], e[3][:, half(1)], factor_last[:, half(1)], MULT)
+        x[3].append(x_last[:])
         roots = sb([P, 2 * X], F32, "roots", "ts_win")
         h_win = []
 

@@ -96,8 +96,9 @@ def tile_attend_gcolb_kernel(tc, qT, wT, us, ts, G, wt, offs, docoffs, slotoffs,
         nc.sync.dma_start(slot[:], slotoffs)
         doc = sb([P, C // 16], U16, "doc")
         nc.sync.dma_start(doc[:], docoffs)
-        m0 = sb([P, (PACK + 1) * HALF], F32, "m0")
-        nc.sync.dma_start(m0[:, 0 : PACK * X], G.rearrange("(p j) x -> p (j x)", j=PACK))
+        g_all = sb([P, PACK * X], F32, "g_all")
+        nc.sync.dma_start(g_all[:], G.rearrange("(p j) x -> p (j x)", j=PACK))
+        g_in = [g_all[:, j * X : (j + 1) * X] for j in range(PACK)]
 
         for n, raw in enumerate(w0):
             cast_w(0, raw, n * HALF, 0, HALF, False)
@@ -172,7 +173,7 @@ def tile_attend_gcolb_kernel(tc, qT, wT, us, ts, G, wt, offs, docoffs, slotoffs,
             if h == 0:
                 qa = quantize_qa(0, qa_grouped)
 
-        qa_late = (sb([P, 2 * P], U32, "qa_late_codes"), sb([P, 2 * P], U8, "qa_late_scales"))
+        qa_late = (sb([P, 2 * P], U32, "qa_late_codes", "w_grouped0"), sb([P, 2 * P], U8, "qa_late_scales"))
         for n in range(2):
             if n == 0:
                 late = late_first
@@ -239,7 +240,7 @@ def tile_attend_gcolb_kernel(tc, qT, wT, us, ts, G, wt, offs, docoffs, slotoffs,
                     nc.tensor.transpose(bank[:, b * P : (b + 1) * P], y[:, first : first + P], ident[:])
                 nc.scalar.activation(e[j][:, half(h)], bank[:], ACT.Exp, scale=us_col[:, j : j + 1])
 
-        m1 = sb([P, PACK * HALF], F32, "m1")
+        m = sb([P, 6 * HALF], F32, "m")
         x = []
         for j in r_tiles:
             if j < 3:
@@ -248,13 +249,18 @@ def tile_attend_gcolb_kernel(tc, qT, wT, us, ts, G, wt, offs, docoffs, slotoffs,
                 else:
                     factor = sb([P, C], F32, "factor%d" % j)
                     nc.gpsimd.tensor_scalar(factor[:], ts_all[:], wtus[:, j : j + 1], 0.0, MULT, ADD)
-                x_j = sb([P, C], F32, "x%d" % j, ["w_grouped1", "x1", "win1"][j])
-                nc.gpsimd.tensor_tensor(x_j[:], e[j][:, 0:C], factor[:], MULT)
-                x.append([x_j[:, half(h)] for h in halves])
+                if j < 2:
+                    x_j = sb([P, C], F32, "x%d" % j, ["w_grouped1", "x1"][j])
+                    nc.gpsimd.tensor_tensor(x_j[:], e[j][:, 0:C], factor[:], MULT)
+                    x.append([x_j[:, half(h)] for h in halves])
+                else:
+                    x_j = sb([P, C], F32, "x2", "win1")
+                    nc.gpsimd.tensor_tensor(x_j[:], e[j][:, 0:C], factor[:], MULT)
+                    x.append([x_j[:, half(h)] for h in halves])
             else:
                 parts = []
                 factor = factor_last
-                parts.append(m1[:, HALF // 2 : 3 * HALF // 2])
+                parts.append(m[:, HALF // 2 : 3 * HALF // 2])
                 nc.gpsimd.tensor_tensor(parts[0], e[j][:, half(0)], factor[:, half(0)], MULT)
                 x.append(parts)
 
@@ -271,15 +277,19 @@ def tile_attend_gcolb_kernel(tc, qT, wT, us, ts, G, wt, offs, docoffs, slotoffs,
         x_last = sb([P, HALF], F32, "x_last", "es3")
         nc.gpsimd.tensor_tensor(x_last[:], e[3][:, half(1)], factor_last[:, half(1)], MULT)
         x[3].append(x_last[:])
+        turns = sb([P, 2 * HALF], F32, "turns", "m1")
         roots = sb([P, 2 * X], F32, "roots", "ts_win")
         h_win = []
 
         def gather_first(j):
-            nc.vector.tensor_tensor(m0[:, (j + 1) * HALF : (j + 2) * HALF], h_win[j][:].indirect(half_list(doc, 0)), x[j][0], MULT)
+            nc.vector.tensor_tensor(m[:, (j + 2) * HALF : (j + 3) * HALF], h_win[j][:].indirect(half_list(doc, 0)), x[j][0], MULT)
 
         for j in r_tiles:
-            root = m1[:, 2 * HALF : 3 * HALF] if j == 3 else roots[:, j % 2 * X : (j % 2 + 1) * X]
-            squared = sb([P, X], F32, "squared%d" % j)[:]
+            root = turns[:, 0:HALF] if j == 3 else roots[:, j % 2 * X : (j % 2 + 1) * X]
+            if j in (1, 2):
+                squared = m[:, (3 * j - 1) * HALF : 3 * j * HALF]
+            else:
+                squared = sb([P, X], F32, "squared%d" % j)[:]
             if j < 3:
                 s_turned = bank_tile(sum_banks[j], [P, PACK, P], "s_turned")
                 for b in range(X // P):
@@ -306,11 +316,16 @@ def tile_attend_gcolb_kernel(tc, qT, wT, us, ts, G, wt, offs, docoffs, slotoffs,
             else:
                 h_j = sb([P, H_COLS], F32, "h3", "win3")
                 nc.gpsimd.memset(h_j[:, X:H_COLS], 0.0)
-            nc.vector.tensor_tensor(h_j[:, 0:X], inv[:], m0[:, j * X : (j + 1) * X], MULT)
+            nc.vector.tensor_tensor(h_j[:, 0:X], inv[:], g_in[j], MULT)
             h_win.append(h_j)
-            if j > 0:
-                gather_first(j - 1)
+            if j == 1:
+                gather_first(0)
+                gather_first(1)
         gather_first(3)
+        for part in range(2):
+            cols = slice(part * HALF // 2, (part + 1) * HALF // 2)
+            offsets = doc[:, part * LIST_COLS // 2 : (part + 1) * LIST_COLS // 2]
+            nc.vector.tensor_tensor(m[:, 4 * HALF : 5 * HALF][:, cols], h_win[2][:].indirect(offsets), x[2][0][:, cols], MULT)
 
         out_win = []
 
@@ -322,7 +337,7 @@ def tile_attend_gcolb_kernel(tc, qT, wT, us, ts, G, wt, offs, docoffs, slotoffs,
         zero_window(0)
         out_rows = out.rearrange("(p j) t -> p j t", j=PACK)
 
-        q_pairs = m1[:, 2 * HALF : 4 * HALF].bitcast(BF16)
+        q_pairs = turns[:].bitcast(BF16)
         for n in range(2):
             for u in range(2):
                 nc.scalar.activation(
@@ -330,7 +345,7 @@ def tile_attend_gcolb_kernel(tc, qT, wT, us, ts, G, wt, offs, docoffs, slotoffs,
                     q_raw[n][:].rearrange("p j (s u e) -> p u j s e", u=2, e=2)[:, u],
                     ACT.Copy,
                 )
-        q_words = m1[:, 2 * HALF : 4 * HALF].rearrange("p (u j s) -> p u j s", u=2, j=PACK)
+        q_words = turns[:].rearrange("p (u j s) -> p u j s", u=2, j=PACK)
         qb = sb([P, D * PACK], BF16, "qb")
         qb_words = qb[:].bitcast(F32).rearrange("s (j p u) -> s j p u", p=P, u=2)
         for pair in range(2):
@@ -341,14 +356,17 @@ def tile_attend_gcolb_kernel(tc, qT, wT, us, ts, G, wt, offs, docoffs, slotoffs,
             nc.scalar.copy(qb_words[:, 2 * pair : 2 * pair + 2], bank[:].rearrange("s b u p -> s b p u"))
 
         def gather_second(j):
-            nc.vector.tensor_tensor(m1[:, j * HALF : (j + 1) * HALF], h_win[j][:].indirect(half_list(doc, 1)), x[j][1], MULT)
+            nc.vector.tensor_tensor(m[:, j * HALF : (j + 1) * HALF], h_win[j][:].indirect(half_list(doc, 1)), x[j][1], MULT)
 
-        def quantize_g(h, m, grouped):
-            nc.scalar.activation(
-                grouped.rearrange("p (c i t) -> p c t i", i=4, t=PACK),
-                m.rearrange("p (t c i) -> p c t i", t=PACK, i=4),
-                ACT.Copy,
-            )
+        def quantize_g(h, planes, grouped):
+            pieces = 2 - h
+            for part in range(pieces):
+                cols = slice(part * P // pieces, (part + 1) * P // pieces)
+                nc.scalar.activation(
+                    grouped.rearrange("p (c i t) -> p c t i", i=4, t=PACK)[:, cols],
+                    planes.rearrange("p (t c i) -> p c t i", t=PACK, i=4)[:, cols],
+                    ACT.Copy,
+                )
             g_codes = sb([P, HALF], U32, "g_codes%d" % h)
             g_scales = sb([P, HALF], U8, "g_scales%d" % h)
             nc.vector.quantize_mx(g_codes[:].bitcast(E5M2), g_scales[:], grouped)
@@ -359,7 +377,7 @@ def tile_attend_gcolb_kernel(tc, qT, wT, us, ts, G, wt, offs, docoffs, slotoffs,
         qb_codes = sb([P, D], U32, "qb_codes", "x1")
         qb_scales = sb([P, D], U8, "qb_scales")
         nc.vector.quantize_mx(qb_codes[:].bitcast(E4M3), qb_scales[:], qb[:])
-        g_first = quantize_g(0, m0[:, HALF : (PACK + 1) * HALF], m1[:, 2 * HALF : 4 * HALF].bitcast(BF16))
+        g_first = quantize_g(0, m[:, 2 * HALF : 6 * HALF], turns[:].bitcast(BF16))
         for j in range(2, 4):
             gather_second(j)
 
@@ -378,7 +396,7 @@ def tile_attend_gcolb_kernel(tc, qT, wT, us, ts, G, wt, offs, docoffs, slotoffs,
                 start=True,
                 stop=True,
             )
-            dw = sb([P, HALF], F32, "dw", "m1" if (h, j) == (0, 3) else "z%d" % j)
+            dw = sb([P, HALF], F32, "dw", "m" if (h, j) == (0, 3) else "z%d" % j)
             nc.scalar.copy(dw[:], dw_bank[:])
             nc.vector.tensor_copy(out_win[j][:].indirect(half_list(idx, h)), dw[:])
             if h == halves[-1]:
@@ -387,7 +405,7 @@ def tile_attend_gcolb_kernel(tc, qT, wT, us, ts, G, wt, offs, docoffs, slotoffs,
         for j in range(3):
             put_dw(0, j, g_first, j)
         g_grouped = sb([P, HALF * PACK], BF16, "g_grouped", "z0")
-        g_second = quantize_g(1, m1[:], g_grouped[:])
+        g_second = quantize_g(1, m[:, 0 : 4 * HALF], g_grouped[:])
         put_dw(0, 3, g_first, 3)
         for j in range(PACK):
             put_dw(1, j, g_second, 4 + j)

@@ -142,8 +142,9 @@ def tile_attend_gcolb_kernel(tc, qT, wT, us, ts, G, wt, offs, docoffs, slotoffs,
             source = q_raw[n][:].rearrange("p t (s j) -> p s t j", j=PACK)
             return dealt[:, n * P // 2 : (n + 1) * P // 2], source[:, :, :, first : first + 2]
 
-        for h in halves:
-            nc.vector.tensor_copy(w_pairs[:, C + h * HALF : C + (h + 1) * HALF], w_win[1][:].indirect(half_list(idx, h)))
+        for n in range(4):
+            offsets = idx[:, n * LIST_COLS // 2 : (n + 1) * LIST_COLS // 2]
+            nc.vector.tensor_copy(w_pairs[:, C + n * HALF // 2 : C + (n + 1) * HALF // 2], w_win[1][:].indirect(offsets))
         nc.scalar.activation(*q_piece(qa_grouped, 0, 0), ACT.Copy)
         late_first = sb([P, R], BF16, "qa_late_grouped0")
         nc.gpsimd.tensor_scalar(
@@ -154,7 +155,7 @@ def tile_attend_gcolb_kernel(tc, qT, wT, us, ts, G, wt, offs, docoffs, slotoffs,
             MULT,
             ADD,
         )
-        nc.gpsimd.tensor_scalar(*[side.rearrange("p s t j -> p s j t") for side in q_piece(qa_grouped, 0, 1)], 1.0, 0.0, MULT, ADD)
+        nc.vector.tensor_copy(*q_piece(qa_grouped, 0, 1))
 
         def quantize_qa(first, source):
             codes = sb([P, 2 * P], U32, "qa_codes%d" % first)
@@ -164,10 +165,11 @@ def tile_attend_gcolb_kernel(tc, qT, wT, us, ts, G, wt, offs, docoffs, slotoffs,
 
         for h in halves:
             w_grouped = sb([P, HALF * PACK], BF16, "w_grouped%d" % h)
-            nc.scalar.copy(
-                w_grouped[:].bitcast(U32).rearrange("p (c u) -> p c u", u=2),
-                w_pairs[:].rearrange("p (u c) -> p c u", u=2)[:, half(h), :],
-            )
+            for n in range(2):
+                nc.scalar.copy(
+                    w_grouped[:].bitcast(U32).rearrange("p (c u) -> p c u", u=2)[:, n * HALF // 2 : (n + 1) * HALF // 2],
+                    w_pairs[:].rearrange("p (u c) -> p c u", u=2)[:, half(h), :][:, n * HALF // 2 : (n + 1) * HALF // 2],
+                )
             w_codes.append(sb([P, HALF], U32, "w_codes%d" % h, ["w_codes0", "qa_grouped"][h]))
             nc.vector.quantize_mx(w_codes[h][:].bitcast(E4M3), w_scales[h][:], w_grouped[:])
             if h == 0:
@@ -187,7 +189,7 @@ def tile_attend_gcolb_kernel(tc, qT, wT, us, ts, G, wt, offs, docoffs, slotoffs,
         factor_last = sb([P, C], F32, "factor3", "w_pairs")
         nc.gpsimd.tensor_scalar(factor_last[:], ts_all[:], wtus[:, 3:4], 0.0, MULT, ADD)
 
-        y = sb([P, C_TILES * 2 * P], F32, "y", "ts_win")
+        shared = sb([P, 3 * HALF // 2], F32, "shared")
 
         def direct(j):
             for h in halves:
@@ -201,9 +203,9 @@ def tile_attend_gcolb_kernel(tc, qT, wT, us, ts, G, wt, offs, docoffs, slotoffs,
                     start=True,
                     stop=True,
                 )
-                z = sb([P, HALF], F32, "z", ["z0", "z1", "z0", "z3"][2 * j + h])
-                nc.vector.tensor_tensor(z[:], a[:], ts_all[:, half(h)], MULT)
-                nc.scalar.activation(e[j][:, half(h)], z[:], ACT.Exp, scale=us_col[:, j : j + 1])
+                z = shared[:, 0:HALF] if (j, h) == (1, 1) else sb([P, HALF], F32, "z", ["z0", "ts_win", "z2"][2 * j + h])[:]
+                nc.vector.tensor_tensor(z, a[:], ts_all[:, half(h)], MULT)
+                nc.scalar.activation(e[j][:, half(h)], z, ACT.Exp, scale=us_col[:, j : j + 1])
 
         def turned(pair):
             a_turned = bank_tile(4 + pair, [P, 2, 2 * P], "a_turned")
@@ -228,9 +230,9 @@ def tile_attend_gcolb_kernel(tc, qT, wT, us, ts, G, wt, offs, docoffs, slotoffs,
                 )
 
         direct(0)
-        turned(0)
         direct(1)
-        for pair in range(1, C_TILES // 2):
+        y = sb([P, C_TILES * 2 * P], F32, "y", "ts_win")
+        for pair in range(C_TILES // 2):
             turned(pair)
         for j in range(2, 4):
             for h in halves:
@@ -262,21 +264,27 @@ def tile_attend_gcolb_kernel(tc, qT, wT, us, ts, G, wt, offs, docoffs, slotoffs,
                 factor = factor_last
                 parts.append(m[:, HALF // 2 : 3 * HALF // 2])
                 nc.gpsimd.tensor_tensor(parts[0], e[j][:, half(0)], factor[:, half(0)], MULT)
+                third = slice(HALF, 3 * HALF // 2)
+                nc.gpsimd.tensor_tensor(shared[:, 0 : HALF // 2], e[j][:, third], factor[:, third], MULT)
                 x.append(parts)
 
         sum_banks = [7, 0, 1]
         inv_banks = [4, 5, 6]
         es_tags = ["w_win0", "w_win1", "w1b", "es3"]
         es = []
-        for j in r_tiles:
+        for j in range(3):
             es_j = sb([P, C], F32, "es%d" % j, es_tags[j])
             nc.vector.tensor_copy(es_j[:], e[j][:].indirect(slot[:]))
             es.append(es_j)
+        es_last = [sb([P, HALF], F32, "es3")[:], shared[:, HALF // 2 : 3 * HALF // 2]]
+        for h in halves:
+            nc.vector.tensor_copy(es_last[h], e[3][:].indirect(half_list(slot, h)))
         s_last = sb([P, X], F32, "s_last")
-        nc.vector.tensor_tensor(s_last[:], es[3][:, 0:C:2], es[3][:, 1:C:2], ADD)
-        x_last = sb([P, HALF], F32, "x_last", "es3")
-        nc.gpsimd.tensor_tensor(x_last[:], e[3][:, half(1)], factor_last[:, half(1)], MULT)
-        x[3].append(x_last[:])
+        for h in halves:
+            nc.vector.tensor_tensor(s_last[:, h * X // 2 : (h + 1) * X // 2], es_last[h][:, 0:HALF:2], es_last[h][:, 1:HALF:2], ADD)
+        fourth = slice(3 * HALF // 2, C)
+        nc.gpsimd.tensor_tensor(shared[:, HALF // 2 : HALF], e[3][:, fourth], factor_last[:, fourth], MULT)
+        x[3].append(shared[:, 0:HALF])
         turns = sb([P, 2 * HALF], F32, "turns", "m1")
         roots = sb([P, 2 * X], F32, "roots", "ts_win")
         h_win = []
@@ -374,7 +382,7 @@ def tile_attend_gcolb_kernel(tc, qT, wT, us, ts, G, wt, offs, docoffs, slotoffs,
 
         for j in range(2):
             gather_second(j)
-        qb_codes = sb([P, D], U32, "qb_codes", "x1")
+        qb_codes = sb([P, D], U32, "qb_codes", "w_grouped1")
         qb_scales = sb([P, D], U8, "qb_scales")
         nc.vector.quantize_mx(qb_codes[:].bitcast(E4M3), qb_scales[:], qb[:])
         g_first = quantize_g(0, m[:, 2 * HALF : 6 * HALF], turns[:].bitcast(BF16))

@@ -21,23 +21,24 @@ ADD = mybir.AluOpType.add
 P = 128
 PACK = 4
 HALF = 512
-LIST_COLS = HALF // 16
-H_COLS = X + P
+CHUNK = 256
 C_TILES = C // P
-E_COLS = C + 3 * P
-SCALAR_COLS = 160
 
 
 def tile_attend_gcolb_kernel(tc, qT, wT, us, ts, G, wt, offs, docoffs, slotoffs, out):
     nc = tc.nc
     halves = range(C // HALF)
+    chunks = range(C // CHUNK)
     r_tiles = range(PACK)
 
-    def half_list(tile, h):
-        return tile[:, h * LIST_COLS : (h + 1) * LIST_COLS]
+    def entries(tile, first, count):
+        return tile[:, first // 16 : (first + count) // 16]
 
     def half(h):
         return slice(h * HALF, (h + 1) * HALF)
+
+    def chunk(k):
+        return slice(k * CHUNK, (k + 1) * CHUNK)
 
     with ExitStack() as ctx:
         keep = ctx.enter_context(tc.tile_pool(name="keep", bufs=1))
@@ -51,309 +52,63 @@ def tile_attend_gcolb_kernel(tc, qT, wT, us, ts, G, wt, offs, docoffs, slotoffs,
 
         idx = sb([P, C // 16], U16, "idx")
         nc.sync.dma_start(idx[:], offs)
-
         ts_win = sb([P, T], F32, "ts_win")
         nc.sync.dma_start(ts_win[P - 1 : P, :], ts[0:1, :])
-        nc.gpsimd.memset(ts_win[0 : P - 1, :].bitcast(I32), 0)
-
-        us_col = sb([P, PACK], F32, "us_col")
-        nc.sync.dma_start(us_col[:], us.rearrange("(p j) o -> p (j o)", j=PACK))
-        wt_col = sb([P, PACK], F32, "wt_col")
-        nc.sync.dma_start(wt_col[:], wt.rearrange("(p j) o -> p (j o)", j=PACK))
-
-        ident = sb([P, P], F32, "ident")
-        make_identity(nc, ident[:])
-        e = [sb([P, E_COLS], F32, "e%d" % j) for j in r_tiles]
-        for j in r_tiles:
-            nc.gpsimd.memset(e[j][:, C:E_COLS], 0.0)
-        h_early = [sb([P, H_COLS], F32, "h%d" % j, ["h0", "h1", "win2"][j]) for j in range(3)]
-        for j in range(3):
-            nc.gpsimd.memset(h_early[j][:, X:H_COLS], 0.0)
-
+        q_raw = sb([P, PACK, R], F32, "q_raw")
+        nc.sync.dma_start(q_raw[:], qT.rearrange("(p j) r -> p j r", j=PACK))
         w_rows = wT.rearrange("(p j) t -> p j t", j=PACK)
-        w_win = [sb([P, T], U32, "w_win%d" % u) for u in range(2)]
-
-        def load_w(u, first, width, tag):
-            raw = sb([P, 2, width], F32, "w_raw_" + tag, tag)
-            nc.sync.dma_start(raw[:], w_rows[:, 2 * u : 2 * u + 2, first : first + width])
-            return raw
-
-        def cast_w(u, raw, first, lo, hi, on_vector):
-            dst = w_win[u][:].bitcast(BF16).rearrange("p (t e) -> p t e", e=2)[:, first + lo : first + hi, :]
-            src = raw[:, :, lo:hi].rearrange("p e t -> p t e")
-            if on_vector:
-                nc.vector.tensor_copy(dst, src)
-            else:
-                nc.scalar.activation(dst, src, ACT.Copy)
-
-        w0 = [load_w(0, n * HALF, HALF, tag) for n, tag in enumerate(["factor1", "factor2", "m1", "squared0"])]
-        w1 = [load_w(1, n * HALF, HALF, tag) for n, tag in enumerate(["es3", "w1b", "x1", "w1d"])]
-        q_rows = qT.rearrange("(p j) r -> p j r", j=PACK)
-        q_raw = [sb([P, PACK, R // 2], F32, "q_raw%d" % n) for n in range(2)]
-        for n in range(2):
-            nc.sync.dma_start(q_raw[n][:], q_rows[:, :, n * R // 2 : (n + 1) * R // 2])
+        w_win = [sb([P, T], F32, "w_win%d" % t) for t in range(PACK)]
+        us_col = sb([P, PACK], F32, "us_col")
+        wt_col = sb([P, PACK], F32, "wt_col")
+        for t in range(PACK):
+            nc.sync.dma_start(w_win[t][:], w_rows[:, t, :])
+            if t == 0:
+                nc.sync.dma_start(us_col[:], us.rearrange("(p j) o -> p (j o)", j=PACK))
+                nc.sync.dma_start(wt_col[:], wt.rearrange("(p j) o -> p (j o)", j=PACK))
         slot = sb([P, C // 16], U16, "slot")
         nc.sync.dma_start(slot[:], slotoffs)
         doc = sb([P, C // 16], U16, "doc")
         nc.sync.dma_start(doc[:], docoffs)
-        g_all = sb([P, PACK * X], F32, "g_all")
-        nc.sync.dma_start(g_all[:], G.rearrange("(p j) x -> p (j x)", j=PACK))
-        g_in = [g_all[:, j * X : (j + 1) * X] for j in range(PACK)]
+        g_in = sb([P, PACK * X], F32, "g_in")
+        nc.sync.dma_start(g_in[:], G.rearrange("(p j) x -> p (j x)", j=PACK))
 
-        for n, raw in enumerate(w0):
-            cast_w(0, raw, n * HALF, 0, HALF, False)
-        for n, raw in enumerate(w1[:3]):
-            cast_w(1, raw, n * HALF, 0, HALF, False)
-        cast_w(1, w1[3], 3 * HALF, SCALAR_COLS, HALF, True)
-        cast_w(1, w1[3], 3 * HALF, 0, SCALAR_COLS, False)
+        nc.gpsimd.memset(ts_win[0 : P - 1, :].bitcast(I32), 0)
+        ident = sb([P, P], F32, "ident")
+        make_identity(nc, ident[:])
 
-        ts_row = sb([P, C], F32, "ts_row", "w_pairs")
-        ts_col = sb([P, C_TILES], F32, "ts_col")
-        ts_all = sb([P, C], F32, "ts_all")
+        ts_row = [sb([P, HALF], F32, "ts_row%d" % h) for h in halves]
+        nc.vector.tensor_copy(ts_row[0][:], ts_win[:].indirect(entries(idx, 0, HALF)))
+        nc.scalar.activation(ts_row[1][:], ts_win[:].indirect(entries(idx, HALF, HALF)), ACT.Copy)
+        ts_col = [sb([P, PACK], F32, "ts_col%d" % h) for h in halves]
+        ts_all = [sb([P, HALF], F32, "ts_all%d" % h) for h in halves]
         for h in halves:
-            nc.vector.tensor_copy(ts_row[:, half(h)], ts_win[:].indirect(half_list(idx, h)))
             bank = bank_tile(4 + h, [P, PACK, P], "ts_turned")
             for b in range(PACK):
-                k = PACK * h + b
-                nc.tensor.transpose(bank[:, b, :], ts_row[:, k * P : (k + 1) * P], ident[:])
-            nc.vector.tensor_copy(ts_col[:, PACK * h : PACK * (h + 1)], bank[:, :, P - 1])
+                nc.tensor.transpose(bank[:, b, :], ts_row[h][:, b * P : (b + 1) * P], ident[:])
+            nc.vector.tensor_copy(ts_col[h][:], bank[:, :, P - 1])
         for h in halves:
             bank = bank_tile(6 + h, [P, PACK, P], "ts_spread")
             for b in range(PACK):
-                k = PACK * h + b
-                nc.tensor.transpose(bank[:, b, :], ts_col[:, k : k + 1].to_broadcast([P, P]), ident[:])
-            nc.vector.tensor_copy(ts_all[:, half(h)], bank[:].rearrange("p b c -> p (b c)"))
-        wtus = sb([P, PACK], F32, "wtus")
-        nc.vector.tensor_tensor(wtus[:, 1:PACK], us_col[:, 1:PACK], wt_col[:, 1:PACK], MULT)
-        wtus_first = sb([P, 1], F32, "wtus_first", "w_pairs")
-        nc.vector.tensor_tensor(wtus_first[:], us_col[:, 0:1], wt_col[:, 0:1], MULT)
-        factor_first = sb([P, C], F32, "factor0")
-        nc.vector.tensor_scalar(factor_first[:], ts_all[:], wtus_first[:], None, MULT)
+                nc.tensor.transpose(bank[:, b, :], ts_col[h][:, b : b + 1].to_broadcast([P, P]), ident[:])
+            nc.vector.tensor_copy(ts_all[h][:], bank[:].rearrange("p b c -> p (b c)"))
 
-        w_codes = []
-        w_scales = [sb([P, HALF], U8, "w_scales%d" % h) for h in halves]
-        w_pairs = sb([P, 2 * C], U32, "w_pairs")
-        nc.vector.tensor_copy(w_pairs[:, 0:C], w_win[0][:].indirect(idx[:]))
-
-        qa_grouped = sb([P, R * PACK // 2], BF16, "qa_grouped")
-
-        def q_piece(grouped, first, n):
-            dealt = grouped[:].rearrange("p (j s t) -> p s t j", j=2, t=PACK)
-            source = q_raw[n][:].rearrange("p t (s j) -> p s t j", j=PACK)
-            return dealt[:, n * P // 2 : (n + 1) * P // 2], source[:, :, :, first : first + 2]
-
-        for n in range(4):
-            offsets = idx[:, n * LIST_COLS // 2 : (n + 1) * LIST_COLS // 2]
-            nc.vector.tensor_copy(w_pairs[:, C + n * HALF // 2 : C + (n + 1) * HALF // 2], w_win[1][:].indirect(offsets))
-        nc.scalar.activation(*q_piece(qa_grouped, 0, 0), ACT.Copy)
-        late_first = sb([P, R], BF16, "qa_late_grouped0")
-        nc.gpsimd.tensor_scalar(
-            late_first[:].rearrange("p (j s t) -> p s j t", j=2, t=PACK),
-            q_raw[0][:].rearrange("p t (s j) -> p s j t", j=PACK)[:, :, 2:4],
-            1.0,
-            0.0,
-            MULT,
-            ADD,
+        qa = sb([P, R * PACK], BF16, "qa")
+        nc.vector.tensor_copy(
+            qa[:].rearrange("p (j s t) -> p s t j", j=PACK, t=PACK),
+            q_raw[:].rearrange("p t (s j) -> p s t j", j=PACK),
         )
-        nc.vector.tensor_copy(*q_piece(qa_grouped, 0, 1))
+        qa_codes = sb([P, R], U32, "qa_codes")
+        qa_scales = sb([P, R], U8, "qa_scales")
+        nc.vector.quantize_mx(qa_codes[:].bitcast(E4M3), qa_scales[:], qa[:])
 
-        def quantize_qa(first, source):
-            codes = sb([P, 2 * P], U32, "qa_codes%d" % first)
-            scales = sb([P, 2 * P], U8, "qa_scales%d" % first)
-            nc.vector.quantize_mx(codes[:].bitcast(E4M3), scales[:], source[:])
-            return codes, scales
-
-        for h in halves:
-            w_grouped = sb([P, HALF * PACK], BF16, "w_grouped%d" % h)
-            for n in range(2):
-                nc.scalar.copy(
-                    w_grouped[:].bitcast(U32).rearrange("p (c u) -> p c u", u=2)[:, n * HALF // 2 : (n + 1) * HALF // 2],
-                    w_pairs[:].rearrange("p (u c) -> p c u", u=2)[:, half(h), :][:, n * HALF // 2 : (n + 1) * HALF // 2],
-                )
-            w_codes.append(sb([P, HALF], U32, "w_codes%d" % h, ["w_codes0", "qa_grouped"][h]))
-            nc.vector.quantize_mx(w_codes[h][:].bitcast(E4M3), w_scales[h][:], w_grouped[:])
-            if h == 0:
-                qa = quantize_qa(0, qa_grouped)
-
-        qa_late = (sb([P, 2 * P], U32, "qa_late_codes", "w_grouped0"), sb([P, 2 * P], U8, "qa_late_scales"))
-        for n in range(2):
-            if n == 0:
-                late = late_first
-            else:
-                late = sb([P, R], BF16, "qa_late_grouped1", "w_pairs")
-                dealt = late[:].rearrange("p (j s t) -> p s t j", j=2, t=PACK)
-                source = q_raw[n][:].rearrange("p t (s j) -> p s t j", j=PACK)[:, :, :, 2:4]
-                nc.scalar.activation(dealt, source, ACT.Copy)
-            nc.vector.quantize_mx(qa_late[0][:, n * P : (n + 1) * P].bitcast(E4M3), qa_late[1][:, n * P : (n + 1) * P], late[:])
-
-        factor_last = sb([P, C], F32, "factor3", "w_pairs")
-        nc.gpsimd.tensor_scalar(factor_last[:], ts_all[:], wtus[:, 3:4], 0.0, MULT, ADD)
-
-        shared = sb([P, 3 * HALF // 2], F32, "shared")
-
-        def direct(j):
-            for h in halves:
-                a = bank_tile(2 * j + h, [P, HALF], "a")
-                nc.tensor.matmul_mx(
-                    a[:],
-                    lhsT=qa[0][:, j * P : (j + 1) * P].bitcast(E4M3),
-                    lhsT_scale=qa[1][:, j * P : (j + 1) * P],
-                    rhs=w_codes[h][:].bitcast(E4M3),
-                    rhs_scale=w_scales[h][:],
-                    start=True,
-                    stop=True,
-                )
-                z = shared[:, 0:HALF] if (j, h) == (1, 1) else sb([P, HALF], F32, "z", ["z0", "ts_win", "z2"][2 * j + h])[:]
-                nc.vector.tensor_tensor(z, a[:], ts_all[:, half(h)], MULT)
-                nc.scalar.activation(e[j][:, half(h)], z, ACT.Exp, scale=us_col[:, j : j + 1])
-
-        def turned(pair):
-            a_turned = bank_tile(4 + pair, [P, 2, 2 * P], "a_turned")
-            for b in range(2):
-                k = 2 * pair + b
-                nc.tensor.matmul_mx(
-                    a_turned[:, b, :],
-                    lhsT=w_codes[k // PACK][:, k % PACK * P : (k % PACK + 1) * P].bitcast(E4M3),
-                    lhsT_scale=w_scales[k // PACK][:, k % PACK * P : (k % PACK + 1) * P],
-                    rhs=qa_late[0][:].bitcast(E4M3),
-                    rhs_scale=qa_late[1][:],
-                    start=True,
-                    stop=True,
-                )
-            for b in range(2):
-                k = 2 * pair + b
-                nc.scalar.activation(
-                    y[:, 2 * k * P : 2 * (k + 1) * P].rearrange("p (j n s) -> p n j s", j=2, n=2),
-                    a_turned[:, b, :].rearrange("p (n j s) -> p n j s", j=2, n=2),
-                    ACT.Copy,
-                    scale=ts_col[:, k : k + 1],
-                )
-
-        direct(0)
-        direct(1)
-        y = sb([P, C_TILES * 2 * P], F32, "y", "ts_win")
-        for pair in range(C_TILES // 2):
-            turned(pair)
-        for j in range(2, 4):
-            for h in halves:
-                bank = bank_tile(2 * (j - 2) + h, [P, HALF], "y_turned")
-                for b in range(PACK):
-                    first = (2 * (PACK * h + b) + j - 2) * P
-                    nc.tensor.transpose(bank[:, b * P : (b + 1) * P], y[:, first : first + P], ident[:])
-                nc.scalar.activation(e[j][:, half(h)], bank[:], ACT.Exp, scale=us_col[:, j : j + 1])
-
-        m = sb([P, 6 * HALF], F32, "m")
-        x = []
-        for j in r_tiles:
-            if j < 3:
-                if j == 0:
-                    factor = factor_first
-                else:
-                    factor = sb([P, C], F32, "factor%d" % j)
-                    nc.gpsimd.tensor_scalar(factor[:], ts_all[:], wtus[:, j : j + 1], 0.0, MULT, ADD)
-                if j < 2:
-                    x_j = sb([P, C], F32, "x%d" % j, ["w_grouped1", "x1"][j])
-                    nc.gpsimd.tensor_tensor(x_j[:], e[j][:, 0:C], factor[:], MULT)
-                    x.append([x_j[:, half(h)] for h in halves])
-                else:
-                    x_j = sb([P, C], F32, "x2", "win1")
-                    nc.gpsimd.tensor_tensor(x_j[:], e[j][:, 0:C], factor[:], MULT)
-                    x.append([x_j[:, half(h)] for h in halves])
-            else:
-                parts = []
-                factor = factor_last
-                parts.append(m[:, HALF // 2 : 3 * HALF // 2])
-                nc.gpsimd.tensor_tensor(parts[0], e[j][:, half(0)], factor[:, half(0)], MULT)
-                third = slice(HALF, 3 * HALF // 2)
-                nc.gpsimd.tensor_tensor(shared[:, 0 : HALF // 2], e[j][:, third], factor[:, third], MULT)
-                x.append(parts)
-
-        sum_banks = [7, 0, 1]
-        inv_banks = [4, 5, 6]
-        es_tags = ["w_win0", "w_win1", "w1b", "es3"]
-        es = []
-        for j in range(3):
-            es_j = sb([P, C], F32, "es%d" % j, es_tags[j])
-            nc.vector.tensor_copy(es_j[:], e[j][:].indirect(slot[:]))
-            es.append(es_j)
-        es_last = [sb([P, HALF], F32, "es3")[:], shared[:, HALF // 2 : 3 * HALF // 2]]
-        for h in halves:
-            nc.vector.tensor_copy(es_last[h], e[3][:].indirect(half_list(slot, h)))
-        s_last = sb([P, X], F32, "s_last")
-        for h in halves:
-            nc.vector.tensor_tensor(s_last[:, h * X // 2 : (h + 1) * X // 2], es_last[h][:, 0:HALF:2], es_last[h][:, 1:HALF:2], ADD)
-        fourth = slice(3 * HALF // 2, C)
-        nc.gpsimd.tensor_tensor(shared[:, HALF // 2 : HALF], e[3][:, fourth], factor_last[:, fourth], MULT)
-        x[3].append(shared[:, 0:HALF])
-        turns = sb([P, 2 * HALF], F32, "turns", "m1")
-        roots = sb([P, 2 * X], F32, "roots", "ts_win")
-        h_win = []
-
-        def gather_first(j):
-            nc.vector.tensor_tensor(m[:, (j + 2) * HALF : (j + 3) * HALF], h_win[j][:].indirect(half_list(doc, 0)), x[j][0], MULT)
-
-        for j in r_tiles:
-            root = turns[:, 0:HALF] if j == 3 else roots[:, j % 2 * X : (j % 2 + 1) * X]
-            if j in (1, 2):
-                squared = m[:, (3 * j - 1) * HALF : 3 * j * HALF]
-            else:
-                squared = sb([P, X], F32, "squared%d" % j)[:]
-            if j < 3:
-                s_turned = bank_tile(sum_banks[j], [P, PACK, P], "s_turned")
-                for b in range(X // P):
-                    for u in range(2):
-                        nc.tensor.matmul(
-                            s_turned[:, b, :],
-                            es[j][:, 2 * P * b + u : 2 * P * (b + 1) : 2],
-                            ident[:],
-                            start=(u == 0),
-                            stop=(u == 1),
-                            is_transpose=True,
-                        )
-                nc.scalar.activation(root, s_turned[:].rearrange("p b r -> p (b r)"), ACT.Abs_reciprocal_sqrt)
-                nc.scalar.activation(squared, root, ACT.Square)
-                inv = bank_tile(inv_banks[j], [P, X], "inv")
-                for b in range(X // P):
-                    nc.tensor.transpose(inv[:, b * P : (b + 1) * P], squared[:, b * P : (b + 1) * P], ident[:])
-            else:
-                nc.scalar.activation(root, s_last[:], ACT.Abs_reciprocal_sqrt)
-                nc.scalar.activation(squared, root, ACT.Square)
-                inv = squared
-            if j < 3:
-                h_j = h_early[j]
-            else:
-                h_j = sb([P, H_COLS], F32, "h3", "win3")
-                nc.gpsimd.memset(h_j[:, X:H_COLS], 0.0)
-            nc.vector.tensor_tensor(h_j[:, 0:X], inv[:], g_in[j], MULT)
-            h_win.append(h_j)
-            if j == 1:
-                gather_first(0)
-                gather_first(1)
-        gather_first(3)
-        for part in range(2):
-            cols = slice(part * HALF // 2, (part + 1) * HALF // 2)
-            offsets = doc[:, part * LIST_COLS // 2 : (part + 1) * LIST_COLS // 2]
-            nc.vector.tensor_tensor(m[:, 4 * HALF : 5 * HALF][:, cols], h_win[2][:].indirect(offsets), x[2][0][:, cols], MULT)
-
-        out_win = []
-
-        def zero_window(j):
-            win = sb([P, T], F32, "out_win%d" % j, "win%d" % j)
-            nc.gpsimd.memset(win[:].bitcast(I32), 0)
-            out_win.append(win)
-
-        zero_window(0)
-        out_rows = out.rearrange("(p j) t -> p j t", j=PACK)
-
-        q_pairs = turns[:].bitcast(BF16)
-        for n in range(2):
-            for u in range(2):
-                nc.scalar.activation(
-                    q_pairs.rearrange("p (u j s e) -> p u j s e", u=2, j=PACK, e=2)[:, u, :, n * P // 2 : (n + 1) * P // 2, :],
-                    q_raw[n][:].rearrange("p j (s u e) -> p u j s e", u=2, e=2)[:, u],
-                    ACT.Copy,
-                )
-        q_words = turns[:].rearrange("p (u j s) -> p u j s", u=2, j=PACK)
+        q_pairs = sb([P, 2 * HALF], F32, "q_pairs")
+        for u in range(2):
+            nc.scalar.activation(
+                q_pairs[:].bitcast(BF16).rearrange("p (u j s e) -> p u j s e", u=2, j=PACK, e=2)[:, u],
+                q_raw[:].rearrange("p j (s u e) -> p u j s e", u=2, e=2)[:, u],
+                ACT.Copy,
+            )
+        q_words = q_pairs[:].rearrange("p (u j s) -> p u j s", u=2, j=PACK)
         qb = sb([P, D * PACK], BF16, "qb")
         qb_words = qb[:].bitcast(F32).rearrange("s (j p u) -> s j p u", p=P, u=2)
         for pair in range(2):
@@ -362,58 +117,179 @@ def tile_attend_gcolb_kernel(tc, qT, wT, us, ts, G, wt, offs, docoffs, slotoffs,
                 for u in range(2):
                     nc.tensor.transpose(bank[:, b, u, :], q_words[:, u, 2 * pair + b, :], ident[:])
             nc.scalar.copy(qb_words[:, 2 * pair : 2 * pair + 2], bank[:].rearrange("s b u p -> s b p u"))
-
-        def gather_second(j):
-            nc.vector.tensor_tensor(m[:, j * HALF : (j + 1) * HALF], h_win[j][:].indirect(half_list(doc, 1)), x[j][1], MULT)
-
-        def quantize_g(h, planes, grouped):
-            pieces = 2 - h
-            for part in range(pieces):
-                cols = slice(part * P // pieces, (part + 1) * P // pieces)
-                nc.scalar.activation(
-                    grouped.rearrange("p (c i t) -> p c t i", i=4, t=PACK)[:, cols],
-                    planes.rearrange("p (t c i) -> p c t i", t=PACK, i=4)[:, cols],
-                    ACT.Copy,
-                )
-            g_codes = sb([P, HALF], U32, "g_codes%d" % h)
-            g_scales = sb([P, HALF], U8, "g_scales%d" % h)
-            nc.vector.quantize_mx(g_codes[:].bitcast(E5M2), g_scales[:], grouped)
-            return g_codes, g_scales
-
-        for j in range(2):
-            gather_second(j)
-        qb_codes = sb([P, D], U32, "qb_codes", "w_grouped1")
+        qb_codes = sb([P, D], U32, "qb_codes")
         qb_scales = sb([P, D], U8, "qb_scales")
         nc.vector.quantize_mx(qb_codes[:].bitcast(E4M3), qb_scales[:], qb[:])
-        g_first = quantize_g(0, m[:, 2 * HALF : 6 * HALF], turns[:].bitcast(BF16))
-        for j in range(2, 4):
-            gather_second(j)
 
-        for j in range(1, 4):
-            zero_window(j)
+        wtus = sb([P, PACK], F32, "wtus")
+        nc.vector.tensor_tensor(wtus[:], us_col[:], wt_col[:], MULT)
+        factor = [sb([P, C], F32, "factor%d" % j) for j in r_tiles]
+        for j in r_tiles:
+            for h in halves:
+                nc.gpsimd.tensor_scalar(factor[j][:, half(h)], ts_all[h][:], wtus[:, j : j + 1], 0.0, MULT, ADD)
 
-        def put_dw(h, j, g_mx, n):
-            rows = slice(j * P, (j + 1) * P)
-            dw_bank = bank_tile(n, [P, HALF], "dw_bank")
+        w_grouped = [sb([P, HALF * PACK], BF16, "w_grouped%d" % h) for h in halves]
+        w_planes = [sb([P, 2, HALF], BF16, "w_planes%d" % u) for u in range(2)]
+        for t in range(PACK):
+            nc.vector.tensor_copy(
+                w_grouped[0][:].rearrange("p (c t) -> p c t", t=PACK)[:, :, t],
+                w_win[t][:].indirect(entries(idx, 0, HALF)),
+            )
+            nc.scalar.activation(w_planes[t // 2][:, t % 2, :], w_win[t][:].indirect(entries(idx, HALF, HALF)), ACT.Copy)
+            if t % 2 == 1:
+                nc.scalar.copy(
+                    w_grouped[1][:].rearrange("p (c t) -> p c t", t=PACK)[:, :, t - 1 : t + 1],
+                    w_planes[t // 2][:].rearrange("p t c -> p c t"),
+                )
+        w_codes = [sb([P, HALF], U32, "w_codes%d" % h) for h in halves]
+        w_scales = [sb([P, HALF], U8, "w_scales%d" % h) for h in halves]
+        for h in halves:
+            nc.vector.quantize_mx(w_codes[h][:].bitcast(E4M3), w_scales[h][:], w_grouped[h][:])
+
+        e = [sb([P, C], F32, "e%d" % j) for j in r_tiles]
+        score_order = [(0, 0), (1, 0), (0, 1), (1, 1), (2, 0), (2, 1), (3, 0), (3, 1)]
+        for n, (j, h) in enumerate(score_order):
+            a = bank_tile(n, [P, HALF], "a")
             nc.tensor.matmul_mx(
-                dw_bank[:],
-                lhsT=qb_codes[:, rows].bitcast(E4M3),
-                lhsT_scale=qb_scales[:, rows],
-                rhs=g_mx[0][:].bitcast(E5M2),
-                rhs_scale=g_mx[1][:],
+                a[:],
+                lhsT=qa_codes[:, j * P : (j + 1) * P].bitcast(E4M3),
+                lhsT_scale=qa_scales[:, j * P : (j + 1) * P],
+                rhs=w_codes[h][:].bitcast(E4M3),
+                rhs_scale=w_scales[h][:],
                 start=True,
                 stop=True,
             )
-            dw = sb([P, HALF], F32, "dw", "m" if (h, j) == (0, 3) else "z%d" % j)
-            nc.scalar.copy(dw[:], dw_bank[:])
-            nc.vector.tensor_copy(out_win[j][:].indirect(half_list(idx, h)), dw[:])
+            z = sb([P, HALF], F32, "z", "z%d" % n)
+            nc.vector.tensor_tensor(z[:], a[:], ts_all[h][:], MULT)
+            nc.scalar.activation(e[j][:, half(h)], z[:], ACT.Exp, scale=us_col[:, j : j + 1])
+
+        x = sb([P, PACK, C], F32, "x", "w_win0")
+        for j in r_tiles:
+            nc.gpsimd.tensor_tensor(x[:, j, :], e[j][:], factor[j][:], MULT)
+
+        out_win = {}
+
+        def zero_window(j, tag):
+            out_win[j] = sb([P, T], F32, "out_win%d" % j, tag)
+            nc.gpsimd.memset(out_win[j][:].bitcast(I32), 0)
+
+        zero_window(0, "factor2")
+        zero_window(2, "factor3")
+
+        es = {}
+
+        def gather_e(j, on_vector):
+            for h in halves:
+                es[j, h] = sb([P, HALF], F32, "es%d_%d" % (j, h), "ts_all0" if (j, h) == (0, 0) else None)
+                window = e[j][:].indirect(entries(slot, h * HALF, HALF))
+                if on_vector:
+                    nc.vector.tensor_copy(es[j, h][:], window)
+                else:
+                    nc.scalar.activation(es[j, h][:], window, ACT.Copy)
+
+        roots = sb([P, PACK * X], F32, "roots", "q_raw")
+        squares = sb([P, PACK * X], F32, "squares", "ts_win")
+        h_win = {}
+
+        def form_h(j, sum_bank, inv_bank):
+            cols = slice(j * X, (j + 1) * X)
+            s_turned = bank_tile(sum_bank, [P, PACK, P], "s_turned")
+            for b in range(X // P):
+                for u in range(2):
+                    first = 2 * P * (b % 2)
+                    nc.tensor.matmul(
+                        s_turned[:, b, :],
+                        es[j, b // 2][:, first + u : first + 2 * P : 2],
+                        ident[:],
+                        start=(u == 0),
+                        stop=(u == 1),
+                        is_transpose=True,
+                    )
+            nc.scalar.activation(roots[:, cols], s_turned[:].rearrange("p b r -> p (b r)"), ACT.Abs_reciprocal_sqrt)
+            nc.scalar.activation(squares[:, cols], roots[:, cols], ACT.Square)
+            inv = bank_tile(inv_bank, [P, X], "inv")
+            for b in range(X // P):
+                nc.tensor.transpose(inv[:, b * P : (b + 1) * P], squares[:, cols][:, b * P : (b + 1) * P], ident[:])
+            h_win[j] = sb([P, X], F32, "h%d" % j)
+            nc.vector.tensor_tensor(h_win[j][:], inv[:], g_in[:, cols], MULT)
+
+        gather_e(0, True)
+        gather_e(2, False)
+        gather_e(1, True)
+        gather_e(3, True)
+        form_h(0, 0, 3)
+        form_h(2, 1, 4)
+        form_h(1, 2, 5)
+        form_h(3, 2, 6)
+
+        planes = [sb([P, PACK, CHUNK], F32, "planes%d" % k) for k in chunks]
+
+        def gather_h(k, j):
+            window = h_win[j][:].indirect(entries(doc, k * CHUNK, CHUNK))
+            if k % 2 == 0:
+                nc.vector.tensor_tensor(planes[k][:, j, :], window, x[:, j, chunk(k)], MULT)
+            else:
+                nc.scalar.activation(planes[k][:, j, :], window, ACT.Copy)
+
+        g_codes = [sb([P, HALF], U32, "g_codes%d" % h) for h in halves]
+        g_scales = [sb([P, HALF], U8, "g_scales%d" % h) for h in halves]
+
+        def quantize_g(k):
+            grouped = sb([P, CHUNK * PACK], BF16, "g_grouped%d" % k)
+            woven = grouped[:].rearrange("p (c i t) -> p c t i", i=4, t=PACK)
+            source = planes[k][:].rearrange("p t (c i) -> p c t i", i=4)
+            if k % 2 == 0:
+                nc.scalar.activation(woven, source, ACT.Copy)
+            else:
+                nc.vector.tensor_tensor(woven, source, x[:, :, chunk(k)].rearrange("p t (c i) -> p c t i", i=4), MULT)
+            nc.vector.quantize_mx(g_codes[k // 2][:, chunk(k % 2)].bitcast(E5M2), g_scales[k // 2][:, chunk(k % 2)], grouped[:])
+
+        for pair in range(2):
+            for j in (0, 2, 1, 3):
+                gather_h(2 * pair, j)
+                gather_h(2 * pair + 1, j)
+        for k in chunks:
+            quantize_g(k)
+
+        dw = {}
+
+        def form_dw(j, h):
+            bank = bank_tile((PACK * h + j + 7) % 8, [P, HALF], "dw_bank")
+            rows = slice(j * P, (j + 1) * P)
+            nc.tensor.matmul_mx(
+                bank[:],
+                lhsT=qb_codes[:, rows].bitcast(E4M3),
+                lhsT_scale=qb_scales[:, rows],
+                rhs=g_codes[h][:].bitcast(E5M2),
+                rhs_scale=g_scales[h][:],
+                start=True,
+                stop=True,
+            )
+            dw[j, h] = sb([P, HALF], F32, "dw", "z%d" % (PACK * h + j))
+            if j < 2:
+                nc.vector.tensor_copy(dw[j, h][:], bank[:])
+            else:
+                nc.scalar.copy(dw[j, h][:], bank[:])
+
+        out_rows = out.rearrange("(p j) t -> p j t", j=PACK)
+
+        def put_dw(j, h):
+            if j < 2:
+                nc.vector.tensor_copy(out_win[j][:].indirect(entries(idx, h * HALF, HALF)), dw[j, h][:])
+            else:
+                for part in range(2):
+                    window = out_win[j][:].indirect(entries(idx, h * HALF + part * CHUNK, CHUNK))
+                    nc.scalar.activation(window, dw[j, h][:, chunk(part)], ACT.Copy)
             if h == halves[-1]:
                 nc.sync.dma_start(out_rows[:, j, :], out_win[j][:])
 
-        for j in range(3):
-            put_dw(0, j, g_first, j)
-        g_grouped = sb([P, HALF * PACK], BF16, "g_grouped", "z0")
-        g_second = quantize_g(1, m[:, 0 : 4 * HALF], g_grouped[:])
-        put_dw(0, 3, g_first, 3)
-        for j in range(PACK):
-            put_dw(1, j, g_second, 4 + j)
+        for h in halves:
+            for j in (0, 2, 1, 3):
+                form_dw(j, h)
+        for j in (0, 2):
+            for h in halves:
+                put_dw(j, h)
+        for j in (1, 3):
+            zero_window(j, "z%d" % (j - 1))
+            for h in halves:
+                put_dw(j, h)

@@ -77,8 +77,8 @@ def tile_attend_gcolb_kernel(tc, qT, wT, us, ts, G, wt, offs, docoffs, slotoffs,
         make_identity(nc, ident[:])
 
         ts_row = [sb([P, HALF], F32, "ts_row%d" % h) for h in halves]
-        nc.vector.tensor_copy(ts_row[0][:], ts_win[:].indirect(entries(idx, 0, HALF)))
-        nc.scalar.activation(ts_row[1][:], ts_win[:].indirect(entries(idx, HALF, HALF)), ACT.Copy)
+        for h in halves:
+            nc.vector.tensor_copy(ts_row[h][:], ts_win[:].indirect(entries(idx, h * HALF, HALF)))
         ts_col = [sb([P, PACK], F32, "ts_col%d" % h) for h in halves]
         ts_all = [sb([P, HALF], F32, "ts_all%d" % h) for h in halves]
         for h in halves:
@@ -147,7 +147,7 @@ def tile_attend_gcolb_kernel(tc, qT, wT, us, ts, G, wt, offs, docoffs, slotoffs,
             nc.vector.quantize_mx(w_codes[h][:].bitcast(E4M3), w_scales[h][:], w_grouped[h][:])
 
         e = [sb([P, C], F32, "e%d" % j) for j in r_tiles]
-        score_order = [(0, 0), (1, 0), (0, 1), (1, 1), (2, 0), (2, 1), (3, 0), (3, 1)]
+        score_order = [(j, h) for h in halves for j in r_tiles]
         for n, (j, h) in enumerate(score_order):
             a = bank_tile(n, [P, HALF], "a")
             nc.tensor.matmul_mx(
@@ -164,8 +164,8 @@ def tile_attend_gcolb_kernel(tc, qT, wT, us, ts, G, wt, offs, docoffs, slotoffs,
             nc.scalar.activation(e[j][:, half(h)], z[:], ACT.Exp, scale=us_col[:, j : j + 1])
 
         x = sb([P, PACK, C], F32, "x", "w_win0")
-        for j in r_tiles:
-            nc.gpsimd.tensor_tensor(x[:, j, :], e[j][:], factor[j][:], MULT)
+        for j, h in score_order:
+            nc.gpsimd.tensor_tensor(x[:, j, half(h)], e[j][:, half(h)], factor[j][:, half(h)], MULT)
 
         out_win = {}
 
@@ -173,14 +173,14 @@ def tile_attend_gcolb_kernel(tc, qT, wT, us, ts, G, wt, offs, docoffs, slotoffs,
             out_win[j] = sb([P, T], F32, "out_win%d" % j, tag)
             nc.gpsimd.memset(out_win[j][:].bitcast(I32), 0)
 
-        zero_window(0, "factor2")
-        zero_window(2, "factor3")
+        for j, tag in zip((0, 2, 1, 3), ("factor3", "factor2", "factor1", "factor0")):
+            zero_window(j, tag)
 
         es = {}
 
         def gather_e(j, on_vector):
             for h in halves:
-                es[j, h] = sb([P, HALF], F32, "es%d_%d" % (j, h), "ts_all0" if (j, h) == (0, 0) else None)
+                es[j, h] = sb([P, HALF], F32, "es%d_%d" % (j, h), "z5" if (j, h) == (0, 0) else None)
                 window = e[j][:].indirect(entries(slot, h * HALF, HALF))
                 if on_vector:
                     nc.vector.tensor_copy(es[j, h][:], window)
@@ -222,7 +222,7 @@ def tile_attend_gcolb_kernel(tc, qT, wT, us, ts, G, wt, offs, docoffs, slotoffs,
         form_h(1, 2, 5)
         form_h(3, 2, 6)
 
-        planes = [sb([P, PACK, CHUNK], F32, "planes%d" % k) for k in chunks]
+        planes = [sb([P, PACK, CHUNK], F32, "planes%d" % k, "es3_%d" % (k // 2) if k % 2 else None) for k in chunks]
 
         def gather_h(k, j):
             window = h_win[j][:].indirect(entries(doc, k * CHUNK, CHUNK))
@@ -253,8 +253,11 @@ def tile_attend_gcolb_kernel(tc, qT, wT, us, ts, G, wt, offs, docoffs, slotoffs,
 
         dw = {}
 
+        dw_banks = {}
+
         def form_dw(j, h):
             bank = bank_tile((PACK * h + j + 7) % 8, [P, HALF], "dw_bank")
+            dw_banks[j, h] = bank
             rows = slice(j * P, (j + 1) * P)
             nc.tensor.matmul_mx(
                 bank[:],
@@ -265,7 +268,10 @@ def tile_attend_gcolb_kernel(tc, qT, wT, us, ts, G, wt, offs, docoffs, slotoffs,
                 start=True,
                 stop=True,
             )
-            dw[j, h] = sb([P, HALF], F32, "dw", "z%d" % (PACK * h + j))
+
+        def take_dw(j, h):
+            bank = dw_banks[j, h]
+            dw[j, h] = sb([P, HALF], F32, "dw", "z%d" % (j - j % 2 if h == 0 else PACK + j))
             if j < 2:
                 nc.vector.tensor_copy(dw[j, h][:], bank[:])
             else:
@@ -286,10 +292,8 @@ def tile_attend_gcolb_kernel(tc, qT, wT, us, ts, G, wt, offs, docoffs, slotoffs,
         for h in halves:
             for j in (0, 2, 1, 3):
                 form_dw(j, h)
-        for j in (0, 2):
+        for j in (0, 2, 1, 3):
             for h in halves:
-                put_dw(j, h)
-        for j in (1, 3):
-            zero_window(j, "z%d" % (j - 1))
+                take_dw(j, h)
             for h in halves:
                 put_dw(j, h)

@@ -128,23 +128,35 @@ def tile_attend_gcolb_kernel(tc, qT, wT, us, ts, G, wt, offs, docoffs, slotoffs,
             for h in halves:
                 nc.gpsimd.tensor_scalar(factor[j][:, half(h)], ts_all[h][:], wtus[:, j : j + 1], 0.0, MULT, ADD)
 
-        w_grouped = [sb([P, HALF * PACK], BF16, "w_grouped%d" % h) for h in halves]
+        w_grouped = [sb([P, CHUNK * PACK], BF16, "w_grouped%d" % k) for k in chunks]
         w_planes = [sb([P, 2, HALF], BF16, "w_planes%d" % u) for u in range(2)]
-        for t in range(PACK):
-            nc.vector.tensor_copy(
-                w_grouped[0][:].rearrange("p (c t) -> p c t", t=PACK)[:, :, t],
-                w_win[t][:].indirect(entries(idx, 0, HALF)),
+
+        def place(u, k):
+            nc.scalar.copy(
+                w_grouped[k][:].rearrange("p (c t) -> p c t", t=PACK)[:, :, 2 * u : 2 * u + 2],
+                w_planes[u][:, :, chunk(k - 2)].rearrange("p t c -> p c t"),
             )
-            nc.scalar.activation(w_planes[t // 2][:, t % 2, :], w_win[t][:].indirect(entries(idx, HALF, HALF)), ACT.Copy)
-            if t % 2 == 1:
-                nc.scalar.copy(
-                    w_grouped[1][:].rearrange("p (c t) -> p c t", t=PACK)[:, :, t - 1 : t + 1],
-                    w_planes[t // 2][:].rearrange("p t c -> p c t"),
+
+        for t in range(PACK):
+            for k in range(2):
+                nc.vector.tensor_copy(
+                    w_grouped[k][:].rearrange("p (c t) -> p c t", t=PACK)[:, :, t],
+                    w_win[t][:].indirect(entries(idx, k * CHUNK, CHUNK)),
                 )
+            width = CHUNK if t == PACK - 1 else HALF
+            for first in range(0, HALF, width):
+                nc.scalar.activation(
+                    w_planes[t // 2][:, t % 2, first : first + width],
+                    w_win[t][:].indirect(entries(idx, HALF + first, width)),
+                    ACT.Copy,
+                )
+            if t % 2 == 1:
+                for k in range(2, 4):
+                    place(t // 2, k)
         w_codes = [sb([P, HALF], U32, "w_codes%d" % h) for h in halves]
         w_scales = [sb([P, HALF], U8, "w_scales%d" % h) for h in halves]
-        for h in halves:
-            nc.vector.quantize_mx(w_codes[h][:].bitcast(E4M3), w_scales[h][:], w_grouped[h][:])
+        for k in chunks:
+            nc.vector.quantize_mx(w_codes[k // 2][:, chunk(k % 2)].bitcast(E4M3), w_scales[k // 2][:, chunk(k % 2)], w_grouped[k][:])
 
         e = [sb([P, C], F32, "e%d" % j) for j in r_tiles]
         score_order = [(j, h) for h in halves for j in r_tiles]
@@ -173,91 +185,139 @@ def tile_attend_gcolb_kernel(tc, qT, wT, us, ts, G, wt, offs, docoffs, slotoffs,
             out_win[j] = sb([P, T], F32, "out_win%d" % j, tag)
             nc.gpsimd.memset(out_win[j][:].bitcast(I32), 0)
 
-        for j, tag in zip((0, 2, 1, 3), ("factor3", "factor2", "factor1", "factor0")):
-            zero_window(j, tag)
+        zero_window(0, "factor3")
+        zero_window(2, "factor2")
 
         es = {}
 
-        def gather_e(j, on_vector):
-            for h in halves:
-                es[j, h] = sb([P, HALF], F32, "es%d_%d" % (j, h), "z5" if (j, h) == (0, 0) else None)
-                window = e[j][:].indirect(entries(slot, h * HALF, HALF))
-                if on_vector:
-                    nc.vector.tensor_copy(es[j, h][:], window)
-                else:
-                    nc.scalar.activation(es[j, h][:], window, ACT.Copy)
+        def gather_e(j, h, tag=None):
+            es[j, h] = sb([P, HALF], F32, "es%d_%d" % (j, h), tag)
+            window = e[j][:].indirect(entries(slot, h * HALF, HALF))
+            if j == 2:
+                nc.scalar.activation(es[j, h][:], window, ACT.Copy)
+            else:
+                nc.vector.tensor_copy(es[j, h][:].rearrange("p (u x) -> p x u", u=2), window)
 
-        roots = sb([P, PACK * X], F32, "roots", "q_raw")
-        squares = sb([P, PACK * X], F32, "squares", "ts_win")
-        h_win = {}
+        s_turned = {}
 
-        def form_h(j, sum_bank, inv_bank):
-            cols = slice(j * X, (j + 1) * X)
-            s_turned = bank_tile(sum_bank, [P, PACK, P], "s_turned")
-            for b in range(X // P):
+        def add_pairs(j, h, n):
+            if (j, h) not in s_turned:
+                bank = bank_tile(n, [P, X], "s_turned")
+                for part in range(h, 1 if j == 2 else 2):
+                    s_turned[j, part] = bank
+                s_turned[j, h] = bank
+            for b in range(2):
                 for u in range(2):
-                    first = 2 * P * (b % 2)
+                    if j == 2:
+                        members = slice(2 * P * b + u, 2 * P * (b + 1), 2)
+                    else:
+                        members = slice((2 * u + b) * P, (2 * u + b + 1) * P)
                     nc.tensor.matmul(
-                        s_turned[:, b, :],
-                        es[j, b // 2][:, first + u : first + 2 * P : 2],
+                        s_turned[j, h][:, (2 * h + b) * P : (2 * h + b + 1) * P],
+                        es[j, h][:, members],
                         ident[:],
                         start=(u == 0),
                         stop=(u == 1),
                         is_transpose=True,
                     )
-            nc.scalar.activation(roots[:, cols], s_turned[:].rearrange("p b r -> p (b r)"), ACT.Abs_reciprocal_sqrt)
-            nc.scalar.activation(squares[:, cols], roots[:, cols], ACT.Square)
-            inv = bank_tile(inv_bank, [P, X], "inv")
+
+        roots = [sb([P, X], F32, "roots%d" % j, "w_grouped%d" % j) for j in r_tiles]
+        squares = [sb([P, X], F32, "squares%d" % j, ["q_raw", "ts_win", "qa", "qb"][j]) for j in r_tiles]
+        whole = slice(0, X)
+
+        def root(j, h=0, cols=whole):
+            nc.scalar.activation(roots[j][:, cols], s_turned[j, h][:, cols], ACT.Abs_reciprocal_sqrt)
+
+        def square(j, cols=whole):
+            nc.scalar.activation(squares[j][:, cols], roots[j][:, cols], ACT.Square)
+
+        h_win = {}
+
+        def form_h(j, n):
+            inv = bank_tile(n, [P, X], "inv")
             for b in range(X // P):
-                nc.tensor.transpose(inv[:, b * P : (b + 1) * P], squares[:, cols][:, b * P : (b + 1) * P], ident[:])
+                nc.tensor.transpose(inv[:, b * P : (b + 1) * P], squares[j][:, b * P : (b + 1) * P], ident[:])
             h_win[j] = sb([P, X], F32, "h%d" % j)
-            nc.vector.tensor_tensor(h_win[j][:], inv[:], g_in[:, cols], MULT)
+            nc.vector.tensor_tensor(h_win[j][:], inv[:], g_in[:, j * X : (j + 1) * X], MULT)
 
-        gather_e(0, True)
-        gather_e(2, False)
-        gather_e(1, True)
-        gather_e(3, True)
-        form_h(0, 0, 3)
-        form_h(2, 1, 4)
-        form_h(1, 2, 5)
-        form_h(3, 2, 6)
-
-        planes = [sb([P, PACK, CHUNK], F32, "planes%d" % k, "es3_%d" % (k // 2) if k % 2 else None) for k in chunks]
+        planes = [sb([P, PACK, CHUNK], F32, "planes%d" % k) for k in chunks]
 
         def gather_h(k, j):
             window = h_win[j][:].indirect(entries(doc, k * CHUNK, CHUNK))
             if k % 2 == 0:
                 nc.vector.tensor_tensor(planes[k][:, j, :], window, x[:, j, chunk(k)], MULT)
+            elif (k, j) == (1, 0):
+                nc.vector.tensor_copy(planes[k][:, j, :], window)
             else:
                 nc.scalar.activation(planes[k][:, j, :], window, ACT.Copy)
 
         g_codes = [sb([P, HALF], U32, "g_codes%d" % h) for h in halves]
         g_scales = [sb([P, HALF], U8, "g_scales%d" % h) for h in halves]
+        grouped = [sb([P, CHUNK * PACK], BF16, "g_grouped%d" % k) for k in chunks]
 
-        def quantize_g(k):
-            grouped = sb([P, CHUNK * PACK], BF16, "g_grouped%d" % k)
-            woven = grouped[:].rearrange("p (c i t) -> p c t i", i=4, t=PACK)
+        def weave(k):
+            woven = grouped[k][:].rearrange("p (c i t) -> p c t i", i=4, t=PACK)
             source = planes[k][:].rearrange("p t (c i) -> p c t i", i=4)
             if k % 2 == 0:
                 nc.scalar.activation(woven, source, ACT.Copy)
             else:
                 nc.vector.tensor_tensor(woven, source, x[:, :, chunk(k)].rearrange("p t (c i) -> p c t i", i=4), MULT)
-            nc.vector.quantize_mx(g_codes[k // 2][:, chunk(k % 2)].bitcast(E5M2), g_scales[k // 2][:, chunk(k % 2)], grouped[:])
 
-        for pair in range(2):
-            for j in (0, 2, 1, 3):
-                gather_h(2 * pair, j)
-                gather_h(2 * pair + 1, j)
-        for k in chunks:
-            quantize_g(k)
+        def quantize_g(k):
+            nc.vector.quantize_mx(g_codes[k // 2][:, chunk(k % 2)].bitcast(E5M2), g_scales[k // 2][:, chunk(k % 2)], grouped[k][:])
+
+        for h in halves:
+            gather_e(0, h, "z5" if h == 0 else None)
+        gather_e(2, 0)
+        add_pairs(2, 0, 1)
+        for h in halves:
+            add_pairs(0, h, 0)
+        for j in (1, 3):
+            for h in halves:
+                gather_e(j, h)
+        for h in halves:
+            add_pairs(1, h, 2)
+        root(0)
+        root(2, 0, chunk(0))
+        square(0)
+        form_h(0, 3)
+        root(1)
+        gather_e(2, 1, "w_grouped0")
+        for h in halves:
+            add_pairs(3, h, 2)
+        add_pairs(2, 1, 7)
+        square(2, chunk(0))
+        square(1)
+        root(3)
+        root(2, 1, chunk(1))
+        square(3)
+        square(2, chunk(1))
+        for k in (0, 2, 1):
+            gather_h(k, 0)
+        form_h(1, 4)
+        gather_h(0, 1)
+        form_h(3, 5)
+        gather_h(2, 1)
+        form_h(2, 6)
+        for k, j in ((3, 0), (1, 1), (3, 1), (1, 3), (0, 3), (1, 2), (0, 2), (3, 3), (2, 3)):
+            gather_h(k, j)
+        weave(0)
+        weave(1)
+        gather_h(3, 2)
+        gather_h(2, 2)
+        weave(2)
+        quantize_g(0)
+        quantize_g(1)
+        weave(3)
+        quantize_g(2)
+        quantize_g(3)
+        zero_window(1, "g_grouped3")
+        zero_window(3, "g_grouped2")
 
         dw = {}
 
-        dw_banks = {}
-
-        def form_dw(j, h):
+        def form_dw(j, h, on_vector):
             bank = bank_tile((PACK * h + j + 7) % 8, [P, HALF], "dw_bank")
-            dw_banks[j, h] = bank
             rows = slice(j * P, (j + 1) * P)
             nc.tensor.matmul_mx(
                 bank[:],
@@ -268,11 +328,8 @@ def tile_attend_gcolb_kernel(tc, qT, wT, us, ts, G, wt, offs, docoffs, slotoffs,
                 start=True,
                 stop=True,
             )
-
-        def take_dw(j, h):
-            bank = dw_banks[j, h]
-            dw[j, h] = sb([P, HALF], F32, "dw", "z%d" % (j - j % 2 if h == 0 else PACK + j))
-            if j < 2:
+            dw[j, h] = sb([P, HALF], F32, "dw", "z%d" % (PACK * h + j))
+            if on_vector:
                 nc.vector.tensor_copy(dw[j, h][:], bank[:])
             else:
                 nc.scalar.copy(dw[j, h][:], bank[:])
@@ -289,11 +346,18 @@ def tile_attend_gcolb_kernel(tc, qT, wT, us, ts, G, wt, offs, docoffs, slotoffs,
             if h == halves[-1]:
                 nc.sync.dma_start(out_rows[:, j, :], out_win[j][:])
 
-        for h in halves:
-            for j in (0, 2, 1, 3):
-                form_dw(j, h)
-        for j in (0, 2, 1, 3):
-            for h in halves:
-                take_dw(j, h)
+        form_dw(2, 0, False)
+        form_dw(0, 0, False)
+        put_dw(0, 0)
+        put_dw(2, 0)
+        form_dw(0, 1, True)
+        form_dw(2, 1, False)
+        form_dw(1, 1, True)
+        form_dw(3, 1, False)
+        put_dw(0, 1)
+        put_dw(2, 1)
+        form_dw(1, 0, False)
+        form_dw(3, 0, False)
+        for j in (1, 3):
             for h in halves:
                 put_dw(j, h)

@@ -72,9 +72,17 @@ def tile_attend_gcolb_kernel(tc, qT, wT, us, ts, G, wt, offs, docoffs, slotoffs,
         g_in = sb([P, PACK * X], F32, "g_in")
         nc.sync.dma_start(g_in[:], G.rearrange("(p j) x -> p (j x)", j=PACK))
 
-        nc.gpsimd.memset(ts_win[0 : P - 1, :].bitcast(I32), 0)
         ident = sb([P, P], F32, "ident")
         make_identity(nc, ident[:])
+        nc.gpsimd.memset(ts_win[0 : P - 1, :].bitcast(I32), 0)
+
+        out_win = {}
+
+        def zero_window(j, tag):
+            out_win[j] = sb([P, T], F32, "out_win%d" % j, tag)
+            nc.gpsimd.memset(out_win[j][:].bitcast(I32), 0)
+
+        zero_window(0, "out_win0")
 
         ts_row = [sb([P, HALF], F32, "ts_row%d" % h) for h in halves]
         for h in halves:
@@ -93,9 +101,13 @@ def tile_attend_gcolb_kernel(tc, qT, wT, us, ts, G, wt, offs, docoffs, slotoffs,
             nc.vector.tensor_copy(ts_all[h][:], bank[:].rearrange("p b c -> p (b c)"))
 
         qa = sb([P, R * PACK], BF16, "qa")
-        nc.vector.tensor_copy(
-            qa[:].rearrange("p (j s t) -> p s t j", j=PACK, t=PACK),
-            q_raw[:].rearrange("p t (s j) -> p s t j", j=PACK),
+        nc.gpsimd.tensor_scalar(
+            qa[:].rearrange("p (j s t) -> p s j t", j=PACK, t=PACK),
+            q_raw[:].rearrange("p t (s j) -> p s j t", j=PACK),
+            1.0,
+            0.0,
+            MULT,
+            ADD,
         )
         qa_codes = sb([P, R], U32, "qa_codes")
         qa_scales = sb([P, R], U8, "qa_scales")
@@ -123,10 +135,16 @@ def tile_attend_gcolb_kernel(tc, qT, wT, us, ts, G, wt, offs, docoffs, slotoffs,
 
         wtus = sb([P, PACK], F32, "wtus")
         nc.vector.tensor_tensor(wtus[:], us_col[:], wt_col[:], MULT)
-        factor = [sb([P, C], F32, "factor%d" % j) for j in r_tiles]
-        for j in r_tiles:
-            for h in halves:
-                nc.gpsimd.tensor_scalar(factor[j][:, half(h)], ts_all[h][:], wtus[:, j : j + 1], 0.0, MULT, ADD)
+        factor = {}
+
+        def form_factors(h, tag):
+            factor[h] = sb([P, PACK, HALF], F32, "factor%d" % h, tag)
+            for j in r_tiles:
+                nc.gpsimd.tensor_scalar(factor[h][:, j, :], ts_all[h][:], wtus[:, j : j + 1], 0.0, MULT, ADD)
+
+        form_factors(0, "factor0")
+        zero_window(2, "qb")
+        form_factors(1, "factor1")
 
         w_grouped = [sb([P, CHUNK * PACK], BF16, "w_grouped%d" % k) for k in chunks]
         w_planes = [sb([P, 2, HALF], BF16, "w_planes%d" % u) for u in range(2)]
@@ -177,23 +195,14 @@ def tile_attend_gcolb_kernel(tc, qT, wT, us, ts, G, wt, offs, docoffs, slotoffs,
 
         x = sb([P, PACK, C], F32, "x", "w_win0")
         for j, h in score_order:
-            nc.gpsimd.tensor_tensor(x[:, j, half(h)], e[j][:, half(h)], factor[j][:, half(h)], MULT)
-
-        out_win = {}
-
-        def zero_window(j, tag):
-            out_win[j] = sb([P, T], F32, "out_win%d" % j, tag)
-            nc.gpsimd.memset(out_win[j][:].bitcast(I32), 0)
-
-        zero_window(0, "factor3")
-        zero_window(2, "factor2")
+            nc.gpsimd.tensor_tensor(x[:, j, half(h)], e[j][:, half(h)], factor[h][:, j, :], MULT)
 
         es = {}
 
         def gather_e(j, h, tag=None):
             es[j, h] = sb([P, HALF], F32, "es%d_%d" % (j, h), tag)
             window = e[j][:].indirect(entries(slot, h * HALF, HALF))
-            if j == 2:
+            if (j, h) == (2, 0):
                 nc.scalar.activation(es[j, h][:], window, ACT.Copy)
             else:
                 nc.vector.tensor_copy(es[j, h][:].rearrange("p (u x) -> p x u", u=2), window)
@@ -203,12 +212,12 @@ def tile_attend_gcolb_kernel(tc, qT, wT, us, ts, G, wt, offs, docoffs, slotoffs,
         def add_pairs(j, h, n):
             if (j, h) not in s_turned:
                 bank = bank_tile(n, [P, X], "s_turned")
-                for part in range(h, 1 if j == 2 else 2):
+                for part in range(h, 1 if j >= 2 else 2):
                     s_turned[j, part] = bank
                 s_turned[j, h] = bank
             for b in range(2):
                 for u in range(2):
-                    if j == 2:
+                    if (j, h) == (2, 0):
                         members = slice(2 * P * b + u, 2 * P * (b + 1), 2)
                     else:
                         members = slice((2 * u + b) * P, (2 * u + b + 1) * P)
@@ -221,32 +230,38 @@ def tile_attend_gcolb_kernel(tc, qT, wT, us, ts, G, wt, offs, docoffs, slotoffs,
                         is_transpose=True,
                     )
 
-        roots = [sb([P, X], F32, "roots%d" % j, "w_grouped%d" % j) for j in r_tiles]
-        squares = [sb([P, X], F32, "squares%d" % j, ["q_raw", "ts_win", "qa", "qb"][j]) for j in r_tiles]
+        roots = [sb([P, X], F32, "roots%d" % j, ["ts_row0", "ts_row1", "w_planes0", "w_planes1"][j]) for j in r_tiles]
+        squares = [sb([P, X], F32, "squares%d" % j, ["q_raw", "ts_win", "qa", "q_pairs"][j]) for j in r_tiles]
         whole = slice(0, X)
 
         def root(j, h=0, cols=whole):
             nc.scalar.activation(roots[j][:, cols], s_turned[j, h][:, cols], ACT.Abs_reciprocal_sqrt)
 
-        def square(j, cols=whole):
-            nc.scalar.activation(squares[j][:, cols], roots[j][:, cols], ACT.Square)
+        def turn(source, n, blocks=range(X // P)):
+            bank = bank_tile(n, [P, X], "turned_back")
+            for b in blocks:
+                nc.tensor.transpose(bank[:, b * P : (b + 1) * P], source[:, b * P : (b + 1) * P], ident[:])
+            return bank
 
         h_win = {}
 
         def form_h(j, n):
-            inv = bank_tile(n, [P, X], "inv")
-            for b in range(X // P):
-                nc.tensor.transpose(inv[:, b * P : (b + 1) * P], squares[j][:, b * P : (b + 1) * P], ident[:])
             h_win[j] = sb([P, X], F32, "h%d" % j)
-            nc.vector.tensor_tensor(h_win[j][:], inv[:], g_in[:, j * X : (j + 1) * X], MULT)
+            nc.scalar.activation(squares[j][:], turn(roots[j], n)[:], ACT.Square)
+            nc.gpsimd.tensor_tensor(h_win[j][:], squares[j][:], g_in[:, j * X : (j + 1) * X], MULT)
+
+        def square_last(h):
+            nc.scalar.activation(squares[3][:, chunk(h)], roots[3][:, chunk(h)], ACT.Square)
+
+        def form_h_last(h, n):
+            inv = turn(squares[3], n, range(2 * h, 2 * h + 2))
+            nc.vector.tensor_tensor(h_win[3][:, chunk(h)], inv[:, chunk(h)], g_in[:, 3 * X : 4 * X][:, chunk(h)], MULT)
 
         planes = [sb([P, PACK, CHUNK], F32, "planes%d" % k) for k in chunks]
 
         def gather_h(k, j):
             window = h_win[j][:].indirect(entries(doc, k * CHUNK, CHUNK))
-            if k % 2 == 0:
-                nc.vector.tensor_tensor(planes[k][:, j, :], window, x[:, j, chunk(k)], MULT)
-            elif (k, j) == (1, 0):
+            if j == 0 or (k, j) == (0, 3):
                 nc.vector.tensor_copy(planes[k][:, j, :], window)
             else:
                 nc.scalar.activation(planes[k][:, j, :], window, ACT.Copy)
@@ -258,10 +273,7 @@ def tile_attend_gcolb_kernel(tc, qT, wT, us, ts, G, wt, offs, docoffs, slotoffs,
         def weave(k):
             woven = grouped[k][:].rearrange("p (c i t) -> p c t i", i=4, t=PACK)
             source = planes[k][:].rearrange("p t (c i) -> p c t i", i=4)
-            if k % 2 == 0:
-                nc.scalar.activation(woven, source, ACT.Copy)
-            else:
-                nc.vector.tensor_tensor(woven, source, x[:, :, chunk(k)].rearrange("p t (c i) -> p c t i", i=4), MULT)
+            nc.vector.tensor_tensor(woven, source, x[:, :, chunk(k)].rearrange("p t (c i) -> p c t i", i=4), MULT)
 
         def quantize_g(k):
             nc.vector.quantize_mx(g_codes[k // 2][:, chunk(k % 2)].bitcast(E5M2), g_scales[k // 2][:, chunk(k % 2)], grouped[k][:])
@@ -272,45 +284,40 @@ def tile_attend_gcolb_kernel(tc, qT, wT, us, ts, G, wt, offs, docoffs, slotoffs,
         add_pairs(2, 0, 1)
         for h in halves:
             add_pairs(0, h, 0)
-        for j in (1, 3):
-            for h in halves:
-                gather_e(j, h)
+        for j, h in ((1, 0), (1, 1), (2, 1), (3, 0), (3, 1)):
+            gather_e(j, h)
         for h in halves:
             add_pairs(1, h, 2)
         root(0)
         root(2, 0, chunk(0))
-        square(0)
         form_h(0, 3)
+        add_pairs(2, 1, 0)
         root(1)
-        gather_e(2, 1, "w_grouped0")
-        for h in halves:
-            add_pairs(3, h, 2)
-        add_pairs(2, 1, 7)
-        square(2, chunk(0))
-        square(1)
-        root(3)
         root(2, 1, chunk(1))
-        square(3)
-        square(2, chunk(1))
-        for k in (0, 2, 1):
-            gather_h(k, 0)
         form_h(1, 4)
-        gather_h(0, 1)
-        form_h(3, 5)
-        gather_h(2, 1)
-        form_h(2, 6)
-        for k, j in ((3, 0), (1, 1), (3, 1), (1, 3), (0, 3), (1, 2), (0, 2), (3, 3), (2, 3)):
+        add_pairs(3, 0, 2)
+        root(3, 0, chunk(0))
+        form_h(2, 5)
+        add_pairs(3, 1, 0)
+        h_win[3] = sb([P, X], F32, "h3")
+        root(3, 1, chunk(1))
+        for h in halves:
+            square_last(h)
+        for k in range(3):
+            gather_h(k, 0)
+        form_h_last(0, 6)
+        form_h_last(1, 7)
+        gather_h(3, 0)
+        for k, j in ((0, 1), (1, 1), (0, 2), (1, 2), (0, 3), (1, 3)):
             gather_h(k, j)
-        weave(0)
-        weave(1)
-        gather_h(3, 2)
-        gather_h(2, 2)
-        weave(2)
-        quantize_g(0)
-        quantize_g(1)
-        weave(3)
-        quantize_g(2)
-        quantize_g(3)
+        for j in (1, 2, 3):
+            for k in (2, 3):
+                gather_h(k, j)
+        for pair in range(2):
+            for k in (2 * pair, 2 * pair + 1):
+                weave(k)
+            for k in (2 * pair, 2 * pair + 1):
+                quantize_g(k)
         zero_window(1, "g_grouped3")
         zero_window(3, "g_grouped2")
 
@@ -352,7 +359,7 @@ def tile_attend_gcolb_kernel(tc, qT, wT, us, ts, G, wt, offs, docoffs, slotoffs,
         put_dw(2, 0)
         form_dw(0, 1, True)
         form_dw(2, 1, False)
-        form_dw(1, 1, True)
+        form_dw(1, 1, False)
         form_dw(3, 1, False)
         put_dw(0, 1)
         put_dw(2, 1)

@@ -101,13 +101,9 @@ def tile_attend_gcolb_kernel(tc, qT, wT, us, ts, G, wt, offs, docoffs, slotoffs,
             nc.vector.tensor_copy(ts_all[h][:], bank[:].rearrange("p b c -> p (b c)"))
 
         qa = sb([P, R * PACK], BF16, "qa")
-        nc.gpsimd.tensor_scalar(
-            qa[:].rearrange("p (j s t) -> p s j t", j=PACK, t=PACK),
-            q_raw[:].rearrange("p t (s j) -> p s j t", j=PACK),
-            1.0,
-            0.0,
-            MULT,
-            ADD,
+        nc.vector.tensor_copy(
+            qa[:].rearrange("p (j s t) -> p s t j", j=PACK, t=PACK),
+            q_raw[:].rearrange("p t (s j) -> p s t j", j=PACK),
         )
         qa_codes = sb([P, R], U32, "qa_codes")
         qa_scales = sb([P, R], U8, "qa_scales")
@@ -271,9 +267,9 @@ def tile_attend_gcolb_kernel(tc, qT, wT, us, ts, G, wt, offs, docoffs, slotoffs,
         grouped = [sb([P, CHUNK * PACK], BF16, "g_grouped%d" % k) for k in chunks]
 
         def weave(k):
-            woven = grouped[k][:].rearrange("p (c i t) -> p c t i", i=4, t=PACK)
-            source = planes[k][:].rearrange("p t (c i) -> p c t i", i=4)
-            nc.vector.tensor_tensor(woven, source, x[:, :, chunk(k)].rearrange("p t (c i) -> p c t i", i=4), MULT)
+            woven = grouped[k][:].rearrange("p (c i t) -> p c t i", i=2, t=PACK)
+            source = planes[k][:].rearrange("p t (c i) -> p c t i", i=2)
+            nc.vector.tensor_tensor(woven, source, x[:, :, chunk(k)].rearrange("p t (c i) -> p c t i", i=2), MULT)
 
         def quantize_g(k):
             nc.vector.quantize_mx(g_codes[k // 2][:, chunk(k % 2)].bitcast(E5M2), g_scales[k // 2][:, chunk(k % 2)], grouped[k][:])

@@ -54,17 +54,16 @@ def tile_attend_gcolb_kernel(tc, qT, wT, us, ts, G, wt, offs, docoffs, slotoffs,
         nc.sync.dma_start(idx[:], offs)
         ts_win = sb([P, T], F32, "ts_win")
         nc.sync.dma_start(ts_win[P - 1 : P, :], ts[0:1, :])
+        us_col = sb([P, PACK], F32, "us_col")
+        nc.sync.dma_start(us_col[:], us.rearrange("(p j) o -> p (j o)", j=PACK))
+        wt_col = sb([P, PACK], F32, "wt_col")
+        nc.sync.dma_start(wt_col[:], wt.rearrange("(p j) o -> p (j o)", j=PACK))
         q_raw = sb([P, PACK, R], F32, "q_raw")
         nc.sync.dma_start(q_raw[:], qT.rearrange("(p j) r -> p j r", j=PACK))
         w_rows = wT.rearrange("(p j) t -> p j t", j=PACK)
         w_win = [sb([P, T], F32, "w_win%d" % t) for t in range(PACK)]
-        us_col = sb([P, PACK], F32, "us_col")
-        wt_col = sb([P, PACK], F32, "wt_col")
         for t in range(PACK):
             nc.sync.dma_start(w_win[t][:], w_rows[:, t, :])
-            if t == 0:
-                nc.sync.dma_start(us_col[:], us.rearrange("(p j) o -> p (j o)", j=PACK))
-                nc.sync.dma_start(wt_col[:], wt.rearrange("(p j) o -> p (j o)", j=PACK))
         slot = sb([P, C // 16], U16, "slot")
         nc.sync.dma_start(slot[:], slotoffs)
         doc = sb([P, C // 16], U16, "doc")
@@ -88,7 +87,7 @@ def tile_attend_gcolb_kernel(tc, qT, wT, us, ts, G, wt, offs, docoffs, slotoffs,
         for h in halves:
             nc.vector.tensor_copy(ts_row[h][:], ts_win[:].indirect(entries(idx, h * HALF, HALF)))
         ts_col = [sb([P, PACK], F32, "ts_col%d" % h) for h in halves]
-        ts_all = [sb([P, HALF], F32, "ts_all%d" % h) for h in halves]
+        ts_all = sb([P, C], F32, "ts_all")
         for h in halves:
             bank = bank_tile(4 + h, [P, PACK, P], "ts_turned")
             for b in range(PACK):
@@ -98,9 +97,9 @@ def tile_attend_gcolb_kernel(tc, qT, wT, us, ts, G, wt, offs, docoffs, slotoffs,
             bank = bank_tile(6 + h, [P, PACK, P], "ts_spread")
             for b in range(PACK):
                 nc.tensor.transpose(bank[:, b, :], ts_col[h][:, b : b + 1].to_broadcast([P, P]), ident[:])
-            nc.vector.tensor_copy(ts_all[h][:], bank[:].rearrange("p b c -> p (b c)"))
+            nc.vector.tensor_copy(ts_all[:, half(h)], bank[:].rearrange("p b c -> p (b c)"))
 
-        qa = sb([P, R * PACK], BF16, "qa")
+        qa = sb([P, R * PACK], BF16, "qa", "ts_row1")
         nc.vector.tensor_copy(
             qa[:].rearrange("p (j s t) -> p s t j", j=PACK, t=PACK),
             q_raw[:].rearrange("p t (s j) -> p s t j", j=PACK),
@@ -110,17 +109,16 @@ def tile_attend_gcolb_kernel(tc, qT, wT, us, ts, G, wt, offs, docoffs, slotoffs,
         nc.vector.quantize_mx(qa_codes[:].bitcast(E4M3), qa_scales[:], qa[:])
 
         q_pairs = sb([P, 2 * HALF], F32, "q_pairs")
-        for u in range(2):
-            nc.scalar.activation(
-                q_pairs[:].bitcast(BF16).rearrange("p (u j s e) -> p u j s e", u=2, j=PACK, e=2)[:, u],
-                q_raw[:].rearrange("p j (s u e) -> p u j s e", u=2, e=2)[:, u],
-                ACT.Copy,
-            )
+        nc.scalar.activation(
+            q_pairs[:].bitcast(BF16).rearrange("p (u n e) -> p n u e", u=2, e=2),
+            q_raw[:].rearrange("p j (s u e) -> p (j s) u e", u=2, e=2),
+            ACT.Copy,
+        )
         q_words = q_pairs[:].rearrange("p (u j s) -> p u j s", u=2, j=PACK)
         qb = sb([P, D * PACK], BF16, "qb")
         qb_words = qb[:].bitcast(F32).rearrange("s (j p u) -> s j p u", p=P, u=2)
         for pair in range(2):
-            bank = bank_tile(2 + pair, [P, 2, 2, P], "q_turned")
+            bank = bank_tile(5 - pair, [P, 2, 2, P], "q_turned")
             for b in range(2):
                 for u in range(2):
                     nc.tensor.transpose(bank[:, b, u, :], q_words[:, u, 2 * pair + b, :], ident[:])
@@ -130,19 +128,12 @@ def tile_attend_gcolb_kernel(tc, qT, wT, us, ts, G, wt, offs, docoffs, slotoffs,
         nc.vector.quantize_mx(qb_codes[:].bitcast(E4M3), qb_scales[:], qb[:])
 
         wtus = sb([P, PACK], F32, "wtus")
-        nc.vector.tensor_tensor(wtus[:], us_col[:], wt_col[:], MULT)
-        factor = {}
+        nc.gpsimd.tensor_tensor(wtus[:], us_col[:], wt_col[:], MULT)
+        factor = [sb([P, C], F32, "factor%d" % j) for j in r_tiles]
+        for j in r_tiles:
+            nc.gpsimd.tensor_scalar(factor[j][:], ts_all[:], wtus[:, j : j + 1], 0.0, MULT, ADD)
 
-        def form_factors(h, tag):
-            factor[h] = sb([P, PACK, HALF], F32, "factor%d" % h, tag)
-            for j in r_tiles:
-                nc.gpsimd.tensor_scalar(factor[h][:, j, :], ts_all[h][:], wtus[:, j : j + 1], 0.0, MULT, ADD)
-
-        form_factors(0, "factor0")
-        zero_window(2, "qb")
-        form_factors(1, "factor1")
-
-        w_grouped = [sb([P, CHUNK * PACK], BF16, "w_grouped%d" % k) for k in chunks]
+        w_grouped = [sb([P, CHUNK * PACK], BF16, "w_grouped%d" % k, ["ts_col1", "ts_col0", None, None][k]) for k in chunks]
         w_planes = [sb([P, 2, HALF], BF16, "w_planes%d" % u) for u in range(2)]
 
         def place(u, k):
@@ -186,12 +177,12 @@ def tile_attend_gcolb_kernel(tc, qT, wT, us, ts, G, wt, offs, docoffs, slotoffs,
                 stop=True,
             )
             z = sb([P, HALF], F32, "z", "z%d" % n)
-            nc.vector.tensor_tensor(z[:], a[:], ts_all[h][:], MULT)
+            nc.vector.tensor_tensor(z[:], a[:], ts_all[:, half(h)], MULT)
             nc.scalar.activation(e[j][:, half(h)], z[:], ACT.Exp, scale=us_col[:, j : j + 1])
 
         x = sb([P, PACK, C], F32, "x", "w_win0")
         for j, h in score_order:
-            nc.gpsimd.tensor_tensor(x[:, j, half(h)], e[j][:, half(h)], factor[h][:, j, :], MULT)
+            nc.gpsimd.tensor_tensor(x[:, j, half(h)], e[j][:, half(h)], factor[j][:, half(h)], MULT)
 
         es = {}
 
@@ -267,9 +258,9 @@ def tile_attend_gcolb_kernel(tc, qT, wT, us, ts, G, wt, offs, docoffs, slotoffs,
         grouped = [sb([P, CHUNK * PACK], BF16, "g_grouped%d" % k) for k in chunks]
 
         def weave(k):
-            woven = grouped[k][:].rearrange("p (c i t) -> p c t i", i=2, t=PACK)
-            source = planes[k][:].rearrange("p t (c i) -> p c t i", i=2)
-            nc.vector.tensor_tensor(woven, source, x[:, :, chunk(k)].rearrange("p t (c i) -> p c t i", i=2), MULT)
+            woven = grouped[k][:].rearrange("p (c i t) -> p c t i", i=4, t=PACK)
+            source = planes[k][:].rearrange("p t (c i) -> p c t i", i=4)
+            nc.vector.tensor_tensor(woven, source, x[:, :, chunk(k)].rearrange("p t (c i) -> p c t i", i=4), MULT)
 
         def quantize_g(k):
             nc.vector.quantize_mx(g_codes[k // 2][:, chunk(k % 2)].bitcast(E5M2), g_scales[k // 2][:, chunk(k % 2)], grouped[k][:])
@@ -294,6 +285,7 @@ def tile_attend_gcolb_kernel(tc, qT, wT, us, ts, G, wt, offs, docoffs, slotoffs,
         add_pairs(3, 0, 2)
         root(3, 0, chunk(0))
         form_h(2, 5)
+        zero_window(2, "qa")
         add_pairs(3, 1, 0)
         h_win[3] = sb([P, X], F32, "h3")
         root(3, 1, chunk(1))

@@ -22,6 +22,7 @@ P = 128
 PACK = 4
 HALF = 512
 CHUNK = 256
+PUT = 384
 C_TILES = C // P
 
 
@@ -309,7 +310,7 @@ def tile_attend_gcolb_kernel(tc, qT, wT, us, ts, G, wt, offs, docoffs, slotoffs,
         zero_window(1, "g_grouped3")
         zero_window(3, "g_grouped2")
 
-        dw = {}
+        dw = [sb([P, C], F32, "dw%d" % j, ["e0", "e1", "e2", "e3"][j]) for j in r_tiles]
 
         def form_dw(j, h, on_vector):
             bank = bank_tile((PACK * h + j + 7) % 8, [P, HALF], "dw_bank")
@@ -323,36 +324,36 @@ def tile_attend_gcolb_kernel(tc, qT, wT, us, ts, G, wt, offs, docoffs, slotoffs,
                 start=True,
                 stop=True,
             )
-            dw[j, h] = sb([P, HALF], F32, "dw", "z%d" % (PACK * h + j))
             if on_vector:
-                nc.vector.tensor_copy(dw[j, h][:], bank[:])
+                nc.vector.tensor_copy(dw[j][:, half(h)], bank[:])
             else:
-                nc.scalar.copy(dw[j, h][:], bank[:])
+                nc.scalar.copy(dw[j][:, half(h)], bank[:])
 
         out_rows = out.rearrange("(p j) t -> p j t", j=PACK)
 
-        def put_dw(j, h):
+        def put_dw(j, first, count):
+            window = out_win[j][:].indirect(entries(idx, first, count))
             if j < 2:
-                nc.vector.tensor_copy(out_win[j][:].indirect(entries(idx, h * HALF, HALF)), dw[j, h][:])
+                nc.vector.tensor_copy(window, dw[j][:, first : first + count])
             else:
-                for part in range(2):
-                    window = out_win[j][:].indirect(entries(idx, h * HALF + part * CHUNK, CHUNK))
-                    nc.scalar.activation(window, dw[j, h][:, chunk(part)], ACT.Copy)
-            if h == halves[-1]:
+                nc.scalar.activation(window, dw[j][:, first : first + count], ACT.Copy)
+            if first + count == C:
                 nc.sync.dma_start(out_rows[:, j, :], out_win[j][:])
 
         form_dw(2, 0, False)
         form_dw(0, 0, False)
-        put_dw(0, 0)
-        put_dw(2, 0)
+        put_dw(0, 0, HALF)
+        for k in range(2):
+            put_dw(2, k * CHUNK, CHUNK)
         form_dw(0, 1, True)
         form_dw(2, 1, False)
         form_dw(1, 1, False)
         form_dw(3, 1, False)
-        put_dw(0, 1)
-        put_dw(2, 1)
+        put_dw(0, HALF, HALF)
+        for k in range(2, 4):
+            put_dw(2, k * CHUNK, CHUNK)
         form_dw(1, 0, False)
         form_dw(3, 0, False)
-        for j in (1, 3):
-            for h in halves:
-                put_dw(j, h)
+        put_dw(1, 0, C)
+        for first in range(0, C, PUT):
+            put_dw(3, first, min(PUT, C - first))

@@ -187,13 +187,12 @@ def tile_attend_gcolb_kernel(tc, qT, wT, us, ts, G, wt, offs, docoffs, slotoffs,
 
         es = {}
 
-        def gather_e(j, h, tag=None):
-            es[j, h] = sb([P, HALF], F32, "es%d_%d" % (j, h), tag)
+        def gather_e(j, h):
             window = e[j][:].indirect(entries(slot, h * HALF, HALF))
             if (j, h) == (2, 0):
-                nc.scalar.activation(es[j, h][:], window, ACT.Copy)
+                nc.scalar.activation(es[j, h], window, ACT.Copy)
             else:
-                nc.vector.tensor_copy(es[j, h][:].rearrange("p (u x) -> p x u", u=2), window)
+                nc.vector.tensor_copy(es[j, h].rearrange("p (u x) -> p x u", u=2), window)
 
         s_turned = {}
 
@@ -266,12 +265,19 @@ def tile_attend_gcolb_kernel(tc, qT, wT, us, ts, G, wt, offs, docoffs, slotoffs,
         def quantize_g(k):
             nc.vector.quantize_mx(g_codes[k // 2][:, chunk(k % 2)].bitcast(E5M2), g_scales[k // 2][:, chunk(k % 2)], grouped[k][:])
 
+        for j, tag in enumerate(("z5", "z6")):
+            both = sb([P, C], F32, "es%d" % j, tag)
+            for h in halves:
+                es[j, h] = both[:, half(h)]
+        for j in (2, 3):
+            for h in halves:
+                es[j, h] = sb([P, HALF], F32, "es%d_%d" % (j, h))[:]
         for h in halves:
-            gather_e(0, h, "z5" if h == 0 else None)
+            gather_e(0, h)
         gather_e(2, 0)
-        add_pairs(2, 0, 1)
         for h in halves:
             add_pairs(0, h, 0)
+        add_pairs(2, 0, 1)
         for j, h in ((1, 0), (1, 1), (2, 1), (3, 0), (3, 1)):
             gather_e(j, h)
         for h in halves:
@@ -279,7 +285,7 @@ def tile_attend_gcolb_kernel(tc, qT, wT, us, ts, G, wt, offs, docoffs, slotoffs,
         root(0)
         root(2, 0, chunk(0))
         form_h(0, 3)
-        add_pairs(2, 1, 0)
+        add_pairs(2, 1, 1)
         root(1)
         root(2, 1, chunk(1))
         form_h(1, 4)
@@ -287,7 +293,7 @@ def tile_attend_gcolb_kernel(tc, qT, wT, us, ts, G, wt, offs, docoffs, slotoffs,
         root(3, 0, chunk(0))
         form_h(2, 5)
         zero_window(2, "qa")
-        add_pairs(3, 1, 0)
+        add_pairs(3, 1, 1)
         h_win[3] = sb([P, X], F32, "h3")
         root(3, 1, chunk(1))
         for h in halves:

@@ -83,6 +83,9 @@ def tile_attend_gcolb_kernel(tc, qT, wT, us, ts, G, wt, offs, docoffs, slotoffs,
             nc.gpsimd.memset(out_win[j][:].bitcast(I32), 0)
 
         zero_window(0, "out_win0")
+        out_win[1] = sb([P, T], F32, "out_win1")
+        nc.vector.memset(out_win[1][:, : T - 1].bitcast(I32), 0)
+        nc.vector.memset(out_win[1][:, T - 1 :].bitcast(I32), 0)
 
         ts_row = [sb([P, HALF], F32, "ts_row%d" % h) for h in halves]
         for h in halves:
@@ -108,6 +111,7 @@ def tile_attend_gcolb_kernel(tc, qT, wT, us, ts, G, wt, offs, docoffs, slotoffs,
         qa_codes = sb([P, R], U32, "qa_codes")
         qa_scales = sb([P, R], U8, "qa_scales")
         nc.vector.quantize_mx(qa_codes[:].bitcast(E4M3), qa_scales[:], qa[:])
+        zero_window(3, "ts_row1")
 
         q_pairs = sb([P, 2 * HALF], F32, "q_pairs")
         nc.scalar.activation(
@@ -217,7 +221,7 @@ def tile_attend_gcolb_kernel(tc, qT, wT, us, ts, G, wt, offs, docoffs, slotoffs,
                         is_transpose=True,
                     )
 
-        roots = [sb([P, X], F32, "roots%d" % j, ["ts_row0", "ts_row1", "w_planes0", "w_planes1"][j]) for j in r_tiles]
+        roots = [sb([P, X], F32, "roots%d" % j, ["ts_row0", "w_grouped2", "w_planes0", "w_planes1"][j]) for j in r_tiles]
         squares = [sb([P, X], F32, "squares%d" % j, ["q_raw", "ts_win", "qa", "q_pairs"][j]) for j in r_tiles]
         whole = slice(0, X)
 
@@ -244,26 +248,23 @@ def tile_attend_gcolb_kernel(tc, qT, wT, us, ts, G, wt, offs, docoffs, slotoffs,
             inv = turn(squares[3], n, range(2 * h, 2 * h + 2))
             nc.vector.tensor_tensor(h_win[3][:, chunk(h)], inv[:, chunk(h)], g_in[:, 3 * X : 4 * X][:, chunk(h)], MULT)
 
-        planes = [sb([P, PACK, CHUNK], F32, "planes%d" % k) for k in chunks]
+        planes = [sb([P, PACK, CHUNK], F32, "planes%d" % k, "planes%d" % (k % 3)) for k in chunks]
 
-        def gather_h(k, j):
+        def gather_h(k, j, on_vector):
             window = h_win[j][:].indirect(entries(doc, k * CHUNK, CHUNK))
-            if j == 0 or (k, j) == (0, 3):
+            if on_vector:
                 nc.vector.tensor_copy(planes[k][:, j, :], window)
             else:
                 nc.scalar.activation(planes[k][:, j, :], window, ACT.Copy)
 
         g_codes = [sb([P, HALF], U32, "g_codes%d" % h) for h in halves]
         g_scales = [sb([P, HALF], U8, "g_scales%d" % h) for h in halves]
-        grouped = [sb([P, CHUNK * PACK], BF16, "g_grouped%d" % k) for k in chunks]
+        early = [sb([P, CHUNK * PACK], BF16, "g_early%d" % k) for k in range(2)]
 
-        def weave(k):
-            woven = grouped[k][:].rearrange("p (c i t) -> p c t i", i=4, t=PACK)
+        def weave(engine, target, k):
+            woven = target.rearrange("p (c i t) -> p c t i", i=4, t=PACK)
             source = planes[k][:].rearrange("p t (c i) -> p c t i", i=4)
-            nc.vector.tensor_tensor(woven, source, x[:, :, chunk(k)].rearrange("p t (c i) -> p c t i", i=4), MULT)
-
-        def quantize_g(k):
-            nc.vector.quantize_mx(g_codes[k // 2][:, chunk(k % 2)].bitcast(E5M2), g_scales[k // 2][:, chunk(k % 2)], grouped[k][:])
+            engine.tensor_tensor(woven, source, x[:, :, chunk(k)].rearrange("p t (c i) -> p c t i", i=4), MULT)
 
         for j, tag in enumerate(("z5", "z6")):
             both = sb([P, C], F32, "es%d" % j, tag)
@@ -299,41 +300,42 @@ def tile_attend_gcolb_kernel(tc, qT, wT, us, ts, G, wt, offs, docoffs, slotoffs,
         for h in halves:
             square_last(h)
         for k in range(3):
-            gather_h(k, 0)
+            gather_h(k, 0, True)
         form_h_last(0, 6)
         form_h_last(1, 7)
-        gather_h(3, 0)
-        for k, j in ((0, 1), (1, 1), (0, 2), (1, 2), (0, 3), (1, 3)):
-            gather_h(k, j)
-        for j in (1, 2, 3):
-            for k in (2, 3):
-                gather_h(k, j)
-        for pair in range(2):
-            for k in (2 * pair, 2 * pair + 1):
-                weave(k)
-            for k in (2 * pair, 2 * pair + 1):
-                quantize_g(k)
-        zero_window(1, "g_grouped3")
-        zero_window(3, "g_grouped2")
+        gather_h(2, 1, True)
+        for k, j in ((0, 1), (1, 1), (0, 2), (1, 2), (0, 3), (1, 3), (2, 2), (2, 3)):
+            gather_h(k, j, (k, j) == (0, 3))
+        for k in range(2):
+            weave(nc.vector, early[k][:], k)
+        for k in range(2):
+            nc.vector.quantize_mx(g_codes[0][:, chunk(k)].bitcast(E5M2), g_scales[0][:, chunk(k)], early[k][:])
+        for j in r_tiles:
+            gather_h(3, j, j < 2)
+        late = sb([P, HALF * PACK], BF16, "g_late", "g_early1")
+        for k in range(2):
+            weave(nc.gpsimd, late[:, k * CHUNK * PACK : (k + 1) * CHUNK * PACK], 2 + k)
+        nc.vector.quantize_mx(g_codes[1][:].bitcast(E5M2), g_scales[1][:], late[:])
 
-        dw = [sb([P, C], F32, "dw%d" % j, ["e0", "e1", "e2", "e3"][j]) for j in r_tiles]
+        dw = [sb([P, C], F32, "dw%d" % j, ["e0", "planes0", "e2", "e3"][j]) for j in r_tiles]
 
-        def form_dw(j, h, on_vector):
-            bank = bank_tile((PACK * h + j + 7) % 8, [P, HALF], "dw_bank")
+        def form_dw(j, first, count, n, on_vector):
+            bank = bank_tile(n, [P, count], "dw_bank")
             rows = slice(j * P, (j + 1) * P)
+            h, cols = first // HALF, slice(first % HALF, first % HALF + count)
             nc.tensor.matmul_mx(
                 bank[:],
                 lhsT=qb_codes[:, rows].bitcast(E4M3),
                 lhsT_scale=qb_scales[:, rows],
-                rhs=g_codes[h][:].bitcast(E5M2),
-                rhs_scale=g_scales[h][:],
+                rhs=g_codes[h][:, cols].bitcast(E5M2),
+                rhs_scale=g_scales[h][:, cols],
                 start=True,
                 stop=True,
             )
             if on_vector:
-                nc.vector.tensor_copy(dw[j][:, half(h)], bank[:])
+                nc.vector.tensor_copy(dw[j][:, first : first + count], bank[:])
             else:
-                nc.scalar.copy(dw[j][:, half(h)], bank[:])
+                nc.scalar.copy(dw[j][:, first : first + count], bank[:])
 
         out_rows = out.rearrange("(p j) t -> p j t", j=PACK)
 
@@ -344,22 +346,24 @@ def tile_attend_gcolb_kernel(tc, qT, wT, us, ts, G, wt, offs, docoffs, slotoffs,
             else:
                 nc.scalar.activation(window, dw[j][:, first : first + count], ACT.Copy)
             if first + count == C:
-                nc.sync.dma_start(out_rows[:, j, :], out_win[j][:])
+                (nc.scalar if j == 3 else nc.sync).dma_start(out_rows[:, j, :], out_win[j][:])
 
-        form_dw(2, 0, False)
-        form_dw(0, 0, False)
+        form_dw(2, 0, CHUNK, 0, False)
+        put_dw(2, 0, CHUNK)
+        form_dw(0, 0, HALF, 1, True)
         put_dw(0, 0, HALF)
-        for k in range(2):
-            put_dw(2, k * CHUNK, CHUNK)
-        form_dw(0, 1, True)
-        form_dw(2, 1, False)
-        form_dw(1, 1, False)
-        form_dw(3, 1, False)
+        form_dw(2, CHUNK, CHUNK, 2, False)
+        form_dw(3, 0, HALF, 3, False)
+        put_dw(2, CHUNK, CHUNK)
+        put_dw(3, 0, CHUNK)
+        form_dw(1, 0, HALF, 4, True)
+        form_dw(0, HALF, HALF, 5, True)
+        form_dw(2, HALF, HALF, 6, False)
         put_dw(0, HALF, HALF)
-        for k in range(2, 4):
-            put_dw(2, k * CHUNK, CHUNK)
-        form_dw(1, 0, False)
-        form_dw(3, 0, False)
+        put_dw(2, 2 * CHUNK, CHUNK)
+        form_dw(3, HALF, HALF, 7, False)
+        put_dw(2, 3 * CHUNK, CHUNK)
+        form_dw(1, HALF, HALF, 0, True)
         put_dw(1, 0, C)
-        for first in range(0, C, PUT):
-            put_dw(3, first, min(PUT, C - first))
+        for first in range(CHUNK, C, PUT):
+            put_dw(3, first, PUT)

@@ -83,9 +83,9 @@ def tile_attend_gcolb_kernel(tc, qT, wT, us, ts, G, wt, offs, docoffs, slotoffs,
             nc.gpsimd.memset(out_win[j][:].bitcast(I32), 0)
 
         zero_window(0, "out_win0")
-        out_win[1] = sb([P, T], F32, "out_win1")
-        nc.vector.memset(out_win[1][:, : T - 1].bitcast(I32), 0)
-        nc.vector.memset(out_win[1][:, T - 1 :].bitcast(I32), 0)
+        out_win[3] = sb([P, T], F32, "out_win3")
+        nc.vector.memset(out_win[3][:, : T - 1].bitcast(I32), 0)
+        nc.vector.memset(out_win[3][:, T - 1 :].bitcast(I32), 0)
 
         ts_row = [sb([P, HALF], F32, "ts_row%d" % h) for h in halves]
         for h in halves:
@@ -111,7 +111,6 @@ def tile_attend_gcolb_kernel(tc, qT, wT, us, ts, G, wt, offs, docoffs, slotoffs,
         qa_codes = sb([P, R], U32, "qa_codes")
         qa_scales = sb([P, R], U8, "qa_scales")
         nc.vector.quantize_mx(qa_codes[:].bitcast(E4M3), qa_scales[:], qa[:])
-        zero_window(3, "ts_row1")
 
         q_pairs = sb([P, 2 * HALF], F32, "q_pairs")
         nc.scalar.activation(
@@ -221,7 +220,7 @@ def tile_attend_gcolb_kernel(tc, qT, wT, us, ts, G, wt, offs, docoffs, slotoffs,
                         is_transpose=True,
                     )
 
-        roots = [sb([P, X], F32, "roots%d" % j, ["ts_row0", "w_grouped2", "w_planes0", "w_planes1"][j]) for j in r_tiles]
+        roots = [sb([P, X], F32, "roots%d" % j, ["ts_row0", "ts_row1", "w_planes0", "w_planes1"][j]) for j in r_tiles]
         squares = [sb([P, X], F32, "squares%d" % j, ["q_raw", "ts_win", "qa", "q_pairs"][j]) for j in r_tiles]
         whole = slice(0, X)
 
@@ -316,6 +315,7 @@ def tile_attend_gcolb_kernel(tc, qT, wT, us, ts, G, wt, offs, docoffs, slotoffs,
         for k in range(2):
             weave(nc.gpsimd, late[:, k * CHUNK * PACK : (k + 1) * CHUNK * PACK], 2 + k)
         nc.vector.quantize_mx(g_codes[1][:].bitcast(E5M2), g_scales[1][:], late[:])
+        zero_window(1, "g_early1")
 
         dw = [sb([P, C], F32, "dw%d" % j, ["e0", "planes0", "e2", "e3"][j]) for j in r_tiles]
 

@@ -185,17 +185,27 @@ def tile_attend_gcolb_kernel(tc, qT, wT, us, ts, G, wt, offs, docoffs, slotoffs,
             nc.scalar.activation(e[j][:, half(h)], z[:], ACT.Exp, scale=us_col[:, j : j + 1])
 
         x = sb([P, PACK, C], F32, "x", "w_win0")
-        for j, h in score_order:
+
+        def form_x(j, h):
             nc.gpsimd.tensor_tensor(x[:, j, half(h)], e[j][:, half(h)], factor[j][:, half(h)], MULT)
+
+        for j, h in score_order[:-1]:
+            form_x(j, h)
 
         es = {}
 
-        def gather_e(j, h):
-            window = e[j][:].indirect(entries(slot, h * HALF, HALF))
-            if (j, h) == (2, 0):
-                nc.scalar.activation(es[j, h], window, ACT.Copy)
+        def gather_e(j, first, count, target, on_vector):
+            window = e[j][:].indirect(entries(slot, first * CHUNK, count * CHUNK))
+            if on_vector:
+                nc.vector.tensor_copy(target.rearrange("p (u x) -> p x u", u=2), window)
             else:
-                nc.vector.tensor_copy(es[j, h].rearrange("p (u x) -> p x u", u=2), window)
+                nc.scalar.activation(target, window, ACT.Copy)
+            for b in range(count):
+                for u in range(2):
+                    if on_vector:
+                        es[j, first + b, u] = target[:, (count * u + b) * P : (count * u + b + 1) * P]
+                    else:
+                        es[j, first + b, u] = target[:, 2 * P * b + u : 2 * P * (b + 1) : 2]
 
         s_turned = {}
 
@@ -207,29 +217,30 @@ def tile_attend_gcolb_kernel(tc, qT, wT, us, ts, G, wt, offs, docoffs, slotoffs,
                 s_turned[j, h] = bank
             for b in range(2):
                 for u in range(2):
-                    if (j, h) == (2, 0):
-                        members = slice(2 * P * b + u, 2 * P * (b + 1), 2)
-                    else:
-                        members = slice((2 * u + b) * P, (2 * u + b + 1) * P)
                     nc.tensor.matmul(
                         s_turned[j, h][:, (2 * h + b) * P : (2 * h + b + 1) * P],
-                        es[j, h][:, members],
+                        es[j, 2 * h + b, u],
                         ident[:],
                         start=(u == 0),
                         stop=(u == 1),
                         is_transpose=True,
                     )
 
-        roots = [sb([P, X], F32, "roots%d" % j, ["ts_row0", "ts_row1", "w_planes0", "w_planes1"][j]) for j in r_tiles]
-        squares = [sb([P, X], F32, "squares%d" % j, ["q_raw", "ts_win", "qa", "q_pairs"][j]) for j in r_tiles]
+        gathered = sb([P, 3 * PACK * CHUNK], F32, "gathered")
+        slots = gathered[:].rearrange("p (k t c) -> p k t c", t=PACK, c=CHUNK)
+        planes = [slots[:, k % 3] for k in chunks]
+
+        roots = [sb([P, X], F32, "roots%d" % j, ["ts_row0", "ts_row1", "w_planes0"][j])[:] for j in range(3)]
+        squares = [sb([P, X], F32, "squares%d" % j, ["q_raw", "ts_win"][j])[:] for j in range(2)]
+        squares.append(x[:, 3, half(1)])
         whole = slice(0, X)
 
         def root(j, h=0, cols=whole):
             nc.scalar.activation(roots[j][:, cols], s_turned[j, h][:, cols], ACT.Abs_reciprocal_sqrt)
 
-        def turn(source, n, blocks=range(X // P)):
+        def turn(source, n):
             bank = bank_tile(n, [P, X], "turned_back")
-            for b in blocks:
+            for b in range(X // P):
                 nc.tensor.transpose(bank[:, b * P : (b + 1) * P], source[:, b * P : (b + 1) * P], ident[:])
             return bank
 
@@ -237,17 +248,29 @@ def tile_attend_gcolb_kernel(tc, qT, wT, us, ts, G, wt, offs, docoffs, slotoffs,
 
         def form_h(j, n):
             h_win[j] = sb([P, X], F32, "h%d" % j)
-            nc.scalar.activation(squares[j][:], turn(roots[j], n)[:], ACT.Square)
-            nc.gpsimd.tensor_tensor(h_win[j][:], squares[j][:], g_in[:, j * X : (j + 1) * X], MULT)
+            nc.scalar.activation(squares[j], turn(roots[j], n)[:], ACT.Square)
+            nc.gpsimd.tensor_tensor(h_win[j][:], squares[j], g_in[:, j * X : (j + 1) * X], MULT)
+
+        def last_roots(h):
+            return slots[:, 0:2, 1:3, h * 64 : (h + 1) * 64]
+
+        def last_squares(h):
+            return planes[2][:, 3 - h, :]
+
+        def quarters(ap):
+            return ap.rearrange("p (a b c) -> p a b c", a=2, b=2)
+
+        def root_last(h):
+            nc.scalar.activation(last_roots(h), quarters(s_turned[3, h][:, chunk(h)]), ACT.Abs_reciprocal_sqrt)
 
         def square_last(h):
-            nc.scalar.activation(squares[3][:, chunk(h)], roots[3][:, chunk(h)], ACT.Square)
+            nc.scalar.activation(quarters(last_squares(h)), last_roots(h), ACT.Square)
 
         def form_h_last(h, n):
-            inv = turn(squares[3], n, range(2 * h, 2 * h + 2))
-            nc.vector.tensor_tensor(h_win[3][:, chunk(h)], inv[:, chunk(h)], g_in[:, 3 * X : 4 * X][:, chunk(h)], MULT)
-
-        planes = [sb([P, PACK, CHUNK], F32, "planes%d" % k, "planes%d" % (k % 3)) for k in chunks]
+            bank = bank_tile(n, [P, CHUNK], "turned_back")
+            for b in range(2):
+                nc.tensor.transpose(bank[:, b * P : (b + 1) * P], last_squares(h)[:, b * P : (b + 1) * P], ident[:])
+            nc.vector.tensor_tensor(h_win[3][:, chunk(h)], bank[:], g_in[:, 3 * X : 4 * X][:, chunk(h)], MULT)
 
         def gather_h(k, j, on_vector):
             window = h_win[j][:].indirect(entries(doc, k * CHUNK, CHUNK))
@@ -262,40 +285,39 @@ def tile_attend_gcolb_kernel(tc, qT, wT, us, ts, G, wt, offs, docoffs, slotoffs,
 
         def weave(engine, target, k):
             woven = target.rearrange("p (c i t) -> p c t i", i=4, t=PACK)
-            source = planes[k][:].rearrange("p t (c i) -> p c t i", i=4)
+            source = planes[k].rearrange("p t (c i) -> p c t i", i=4)
             engine.tensor_tensor(woven, source, x[:, :, chunk(k)].rearrange("p t (c i) -> p c t i", i=4), MULT)
 
-        for j, tag in enumerate(("z5", "z6")):
-            both = sb([P, C], F32, "es%d" % j, tag)
-            for h in halves:
-                es[j, h] = both[:, half(h)]
-        for j in (2, 3):
-            for h in halves:
-                es[j, h] = sb([P, HALF], F32, "es%d_%d" % (j, h))[:]
+        both = [sb([P, C], F32, "es%d" % j, tag) for j, tag in enumerate(("z5", "z6"))]
         for h in halves:
-            gather_e(0, h)
-        gather_e(2, 0)
+            gather_e(0, 2 * h, 2, both[0][:, half(h)], True)
+        gather_e(2, 0, 2, sb([P, HALF], F32, "es2_0")[:], False)
         for h in halves:
             add_pairs(0, h, 0)
         add_pairs(2, 0, 1)
-        for j, h in ((1, 0), (1, 1), (2, 1), (3, 0), (3, 1)):
-            gather_e(j, h)
+        for h in halves:
+            gather_e(1, 2 * h, 2, both[1][:, half(h)], True)
+        gather_e(2, 3, 1, sb([P, CHUNK], F32, "es2_3")[:], True)
+        for h in halves:
+            gather_e(3, 2 * h, 2, sb([P, HALF], F32, "es3_%d" % h)[:], True)
         for h in halves:
             add_pairs(1, h, 2)
         root(0)
         root(2, 0, chunk(0))
+        gather_e(2, 2, 1, sb([P, CHUNK], F32, "es2_2", "z5")[:], False)
         form_h(0, 3)
         add_pairs(2, 1, 1)
         root(1)
         root(2, 1, chunk(1))
         form_h(1, 4)
-        add_pairs(3, 0, 2)
-        root(3, 0, chunk(0))
         form_h(2, 5)
-        zero_window(2, "qa")
-        add_pairs(3, 1, 1)
+        form_x(3, 1)
+        zero_window(2, "factor3")
+        add_pairs(3, 0, 1)
+        root_last(0)
+        add_pairs(3, 1, 4)
         h_win[3] = sb([P, X], F32, "h3")
-        root(3, 1, chunk(1))
+        root_last(1)
         for h in halves:
             square_last(h)
         for k in range(3):
@@ -317,7 +339,7 @@ def tile_attend_gcolb_kernel(tc, qT, wT, us, ts, G, wt, offs, docoffs, slotoffs,
         nc.vector.quantize_mx(g_codes[1][:].bitcast(E5M2), g_scales[1][:], late[:])
         zero_window(1, "g_early1")
 
-        dw = [sb([P, C], F32, "dw%d" % j, ["e0", "planes0", "e2", "e3"][j]) for j in r_tiles]
+        dw = [gathered[:, :C] if j == 1 else sb([P, C], F32, "dw%d" % j, "e%d" % j)[:] for j in r_tiles]
 
         def form_dw(j, first, count, n, on_vector):
             bank = bank_tile(n, [P, count], "dw_bank")
@@ -351,19 +373,19 @@ def tile_attend_gcolb_kernel(tc, qT, wT, us, ts, G, wt, offs, docoffs, slotoffs,
         form_dw(2, 0, CHUNK, 0, False)
         put_dw(2, 0, CHUNK)
         form_dw(0, 0, HALF, 1, True)
-        put_dw(0, 0, HALF)
         form_dw(2, CHUNK, CHUNK, 2, False)
-        form_dw(3, 0, HALF, 3, False)
-        put_dw(2, CHUNK, CHUNK)
+        form_dw(3, 0, HALF, 3, True)
+        put_dw(0, 0, HALF)
         put_dw(3, 0, CHUNK)
-        form_dw(1, 0, HALF, 4, True)
-        form_dw(0, HALF, HALF, 5, True)
-        form_dw(2, HALF, HALF, 6, False)
+        put_dw(2, CHUNK, CHUNK)
+        put_dw(3, CHUNK, CHUNK)
+        for j, h, n in ((1, 0, 4), (0, 1, 5), (1, 1, 6)):
+            form_dw(j, h * HALF, HALF, n, True)
+        form_dw(2, HALF, HALF, 7, False)
         put_dw(0, HALF, HALF)
         put_dw(2, 2 * CHUNK, CHUNK)
-        form_dw(3, HALF, HALF, 7, False)
+        form_dw(3, HALF, HALF, 0, False)
         put_dw(2, 3 * CHUNK, CHUNK)
-        form_dw(1, HALF, HALF, 0, True)
         put_dw(1, 0, C)
-        for first in range(CHUNK, C, PUT):
-            put_dw(3, first, PUT)
+        for k in (2, 3):
+            put_dw(3, k * CHUNK, CHUNK)

from contextlib import ExitStack

import concourse.mybir as mybir
from concourse.masks import make_identity

D, R, C, T, X = 512, 512, 1024, 2048, 512
FLOPS = 2 * 2 * D * R * C

F32 = mybir.dt.float32
BF16 = mybir.dt.bfloat16
U32 = mybir.dt.uint32
U16 = mybir.dt.uint16
U8 = mybir.dt.uint8
I32 = mybir.dt.int32
E4M3 = mybir.dt.float8_e4m3fn_x4
E5M2 = mybir.dt.float8_e5m2_x4
ACT = mybir.ActivationFunctionType
MULT = mybir.AluOpType.mult
ADD = mybir.AluOpType.add

P = 128
PACK = 4
HALF = 512
CHUNK = 256
PUT = 384
C_TILES = C // P


def tile_attend_gcolb_kernel(tc, qT, wT, us, ts, G, wt, offs, docoffs, slotoffs, out):
    nc = tc.nc
    halves = range(C // HALF)
    chunks = range(C // CHUNK)
    r_tiles = range(PACK)

    def entries(tile, first, count):
        return tile[:, first // 16 : (first + count) // 16]

    def half(h):
        return slice(h * HALF, (h + 1) * HALF)

    def chunk(k):
        return slice(k * CHUNK, (k + 1) * CHUNK)

    with ExitStack() as ctx:
        keep = ctx.enter_context(tc.tile_pool(name="keep", bufs=1))
        psum = ctx.enter_context(tc.psum_pool(name="psum", bufs=1))

        def sb(shape, dtype, name, tag=None):
            return keep.tile(shape, dtype, name=name, tag=tag or name, align_bytes=64)

        def bank_tile(n, shape, name):
            return psum.tile(shape, F32, name=name, tag="bank%d" % n)

        idx = sb([P, C // 16], U16, "idx")
        nc.sync.dma_start(idx[:], offs)
        ts_win = sb([P, T], F32, "ts_win")
        nc.sync.dma_start(ts_win[P - 1 : P, :], ts[0:1, :])
        us_col = sb([P, PACK], F32, "us_col")
        nc.sync.dma_start(us_col[:], us.rearrange("(p j) o -> p (j o)", j=PACK))
        wt_col = sb([P, PACK], F32, "wt_col")
        nc.sync.dma_start(wt_col[:], wt.rearrange("(p j) o -> p (j o)", j=PACK))
        q_raw = sb([P, PACK, R], F32, "q_raw")
        nc.sync.dma_start(q_raw[:], qT.rearrange("(p j) r -> p j r", j=PACK))
        w_rows = wT.rearrange("(p j) t -> p j t", j=PACK)
        w_win = [sb([P, T], F32, "w_win%d" % t) for t in range(PACK)]
        for t in range(PACK):
            nc.sync.dma_start(w_win[t][:], w_rows[:, t, :])
        slot = sb([P, C // 16], U16, "slot")
        nc.sync.dma_start(slot[:], slotoffs)
        doc = sb([P, C // 16], U16, "doc")
        nc.sync.dma_start(doc[:], docoffs)
        g_in = sb([P, PACK * X], F32, "g_in")
        nc.sync.dma_start(g_in[:], G.rearrange("(p j) x -> p (j x)", j=PACK))

        ident = sb([P, P], F32, "ident")
        make_identity(nc, ident[:])
        nc.gpsimd.memset(ts_win[0 : P - 1, :].bitcast(I32), 0)

        out_win = {}

        def zero_window(j, tag):
            out_win[j] = sb([P, T], F32, "out_win%d" % j, tag)
            nc.gpsimd.memset(out_win[j][:].bitcast(I32), 0)

        zero_window(0, "out_win0")
        out_win[3] = sb([P, T], F32, "out_win3")
        nc.vector.memset(out_win[3][:, : T - 1].bitcast(I32), 0)
        nc.vector.memset(out_win[3][:, T - 1 :].bitcast(I32), 0)

        ts_row = [sb([P, HALF], F32, "ts_row%d" % h) for h in halves]
        for h in halves:
            nc.vector.tensor_copy(ts_row[h][:], ts_win[:].indirect(entries(idx, h * HALF, HALF)))
        ts_col = [sb([P, PACK], F32, "ts_col%d" % h) for h in halves]
        ts_all = sb([P, C], F32, "ts_all")
        for h in halves:
            bank = bank_tile(4 + h, [P, PACK, P], "ts_turned")
            for b in range(PACK):
                nc.tensor.transpose(bank[:, b, :], ts_row[h][:, b * P : (b + 1) * P], ident[:])
            nc.vector.tensor_copy(ts_col[h][:], bank[:, :, P - 1])
        for h in halves:
            bank = bank_tile(6 + h, [P, PACK, P], "ts_spread")
            for b in range(PACK):
                nc.tensor.transpose(bank[:, b, :], ts_col[h][:, b : b + 1].to_broadcast([P, P]), ident[:])
            nc.vector.tensor_copy(ts_all[:, half(h)], bank[:].rearrange("p b c -> p (b c)"))

        qa = sb([P, R * PACK], BF16, "qa", "ts_row1")
        nc.vector.tensor_copy(
            qa[:].rearrange("p (j s t) -> p s t j", j=PACK, t=PACK),
            q_raw[:].rearrange("p t (s j) -> p s t j", j=PACK),
        )
        qa_codes = sb([P, R], U32, "qa_codes")
        qa_scales = sb([P, R], U8, "qa_scales")
        nc.vector.quantize_mx(qa_codes[:].bitcast(E4M3), qa_scales[:], qa[:])

        q_pairs = sb([P, 2 * HALF], F32, "q_pairs")
        nc.scalar.activation(
            q_pairs[:].bitcast(BF16).rearrange("p (u n e) -> p n u e", u=2, e=2),
            q_raw[:].rearrange("p j (s u e) -> p (j s) u e", u=2, e=2),
            ACT.Copy,
        )
        q_words = q_pairs[:].rearrange("p (u j s) -> p u j s", u=2, j=PACK)
        qb = sb([P, D * PACK], BF16, "qb")
        qb_words = qb[:].bitcast(F32).rearrange("s (j p u) -> s j p u", p=P, u=2)
        for pair in range(2):
            bank = bank_tile(5 - pair, [P, 2, 2, P], "q_turned")
            for b in range(2):
                for u in range(2):
                    nc.tensor.transpose(bank[:, b, u, :], q_words[:, u, 2 * pair + b, :], ident[:])
            nc.scalar.copy(qb_words[:, 2 * pair : 2 * pair + 2], bank[:].rearrange("s b u p -> s b p u"))
        qb_codes = sb([P, D], U32, "qb_codes")
        qb_scales = sb([P, D], U8, "qb_scales")
        nc.vector.quantize_mx(qb_codes[:].bitcast(E4M3), qb_scales[:], qb[:])

        wtus = sb([P, PACK], F32, "wtus")
        nc.gpsimd.tensor_tensor(wtus[:], us_col[:], wt_col[:], MULT)
        factor = [sb([P, C], F32, "factor%d" % j) for j in r_tiles]
        for j in r_tiles:
            nc.gpsimd.tensor_scalar(factor[j][:], ts_all[:], wtus[:, j : j + 1], 0.0, MULT, ADD)

        w_grouped = [sb([P, CHUNK * PACK], BF16, "w_grouped%d" % k, ["ts_col1", "ts_col0", None, None][k]) for k in chunks]
        w_planes = [sb([P, 2, HALF], BF16, "w_planes%d" % u) for u in range(2)]

        def place(u, k):
            nc.scalar.copy(
                w_grouped[k][:].rearrange("p (c t) -> p c t", t=PACK)[:, :, 2 * u : 2 * u + 2],
                w_planes[u][:, :, chunk(k - 2)].rearrange("p t c -> p c t"),
            )

        for t in range(PACK):
            for k in range(2):
                nc.vector.tensor_copy(
                    w_grouped[k][:].rearrange("p (c t) -> p c t", t=PACK)[:, :, t],
                    w_win[t][:].indirect(entries(idx, k * CHUNK, CHUNK)),
                )
            width = CHUNK if t == PACK - 1 else HALF
            for first in range(0, HALF, width):
                nc.scalar.activation(
                    w_planes[t // 2][:, t % 2, first : first + width],
                    w_win[t][:].indirect(entries(idx, HALF + first, width)),
                    ACT.Copy,
                )
            if t % 2 == 1:
                for k in range(2, 4):
                    place(t // 2, k)
        w_codes = [sb([P, HALF], U32, "w_codes%d" % h) for h in halves]
        w_scales = [sb([P, HALF], U8, "w_scales%d" % h) for h in halves]
        for k in chunks:
            nc.vector.quantize_mx(w_codes[k // 2][:, chunk(k % 2)].bitcast(E4M3), w_scales[k // 2][:, chunk(k % 2)], w_grouped[k][:])

        e = [sb([P, C], F32, "e%d" % j) for j in r_tiles]
        score_order = [(j, h) for h in halves for j in r_tiles]
        for n, (j, h) in enumerate(score_order):
            a = bank_tile(n, [P, HALF], "a")
            nc.tensor.matmul_mx(
                a[:],
                lhsT=qa_codes[:, j * P : (j + 1) * P].bitcast(E4M3),
                lhsT_scale=qa_scales[:, j * P : (j + 1) * P],
                rhs=w_codes[h][:].bitcast(E4M3),
                rhs_scale=w_scales[h][:],
                start=True,
                stop=True,
            )
            z = sb([P, HALF], F32, "z", "z%d" % n)
            nc.vector.tensor_tensor(z[:], a[:], ts_all[:, half(h)], MULT)
            nc.scalar.activation(e[j][:, half(h)], z[:], ACT.Exp, scale=us_col[:, j : j + 1])

        x = sb([P, PACK, C], F32, "x", "w_win0")

        def form_x(j, h):
            nc.gpsimd.tensor_tensor(x[:, j, half(h)], e[j][:, half(h)], factor[j][:, half(h)], MULT)

        for j, h in score_order[:-1]:
            form_x(j, h)

        es = {}

        def gather_e(j, first, count, target, on_vector):
            window = e[j][:].indirect(entries(slot, first * CHUNK, count * CHUNK))
            if on_vector:
                nc.vector.tensor_copy(target.rearrange("p (u x) -> p x u", u=2), window)
            else:
                nc.scalar.activation(target, window, ACT.Copy)
            for b in range(count):
                for u in range(2):
                    if on_vector:
                        es[j, first + b, u] = target[:, (count * u + b) * P : (count * u + b + 1) * P]
                    else:
                        es[j, first + b, u] = target[:, 2 * P * b + u : 2 * P * (b + 1) : 2]

        s_turned = {}

        def add_pairs(j, h, n):
            if (j, h) not in s_turned:
                bank = bank_tile(n, [P, X], "s_turned")
                for part in range(h, 1 if j >= 2 else 2):
                    s_turned[j, part] = bank
                s_turned[j, h] = bank
            for b in range(2):
                for u in range(2):
                    nc.tensor.matmul(
                        s_turned[j, h][:, (2 * h + b) * P : (2 * h + b + 1) * P],
                        es[j, 2 * h + b, u],
                        ident[:],
                        start=(u == 0),
                        stop=(u == 1),
                        is_transpose=True,
                    )

        gathered = sb([P, 3 * PACK * CHUNK], F32, "gathered")
        slots = gathered[:].rearrange("p (k t c) -> p k t c", t=PACK, c=CHUNK)
        planes = [slots[:, k % 3] for k in chunks]

        roots = [sb([P, X], F32, "roots%d" % j, ["ts_row0", "ts_row1", "w_planes0"][j])[:] for j in range(3)]
        squares = [sb([P, X], F32, "squares%d" % j, ["q_raw", "ts_win"][j])[:] for j in range(2)]
        squares.append(x[:, 3, half(1)])
        whole = slice(0, X)

        def root(j, h=0, cols=whole):
            nc.scalar.activation(roots[j][:, cols], s_turned[j, h][:, cols], ACT.Abs_reciprocal_sqrt)

        def turn(source, n):
            bank = bank_tile(n, [P, X], "turned_back")
            for b in range(X // P):
                nc.tensor.transpose(bank[:, b * P : (b + 1) * P], source[:, b * P : (b + 1) * P], ident[:])
            return bank

        h_win = {}

        def form_h(j, n):
            h_win[j] = sb([P, X], F32, "h%d" % j)
            nc.scalar.activation(squares[j], turn(roots[j], n)[:], ACT.Square)
            nc.gpsimd.tensor_tensor(h_win[j][:], squares[j], g_in[:, j * X : (j + 1) * X], MULT)

        def last_roots(h):
            return slots[:, 0:2, 1:3, h * 64 : (h + 1) * 64]

        def last_squares(h):
            return planes[2][:, 3 - h, :]

        def quarters(ap):
            return ap.rearrange("p (a b c) -> p a b c", a=2, b=2)

        def root_last(h):
            nc.scalar.activation(last_roots(h), quarters(s_turned[3, h][:, chunk(h)]), ACT.Abs_reciprocal_sqrt)

        def square_last(h):
            nc.scalar.activation(quarters(last_squares(h)), last_roots(h), ACT.Square)

        def form_h_last(h, n):
            bank = bank_tile(n, [P, CHUNK], "turned_back")
            for b in range(2):
                nc.tensor.transpose(bank[:, b * P : (b + 1) * P], last_squares(h)[:, b * P : (b + 1) * P], ident[:])
            nc.vector.tensor_tensor(h_win[3][:, chunk(h)], bank[:], g_in[:, 3 * X : 4 * X][:, chunk(h)], MULT)

        def gather_h(k, j, on_vector):
            window = h_win[j][:].indirect(entries(doc, k * CHUNK, CHUNK))
            if on_vector:
                nc.vector.tensor_copy(planes[k][:, j, :], window)
            else:
                nc.scalar.activation(planes[k][:, j, :], window, ACT.Copy)

        g_codes = [sb([P, HALF], U32, "g_codes%d" % h) for h in halves]
        g_scales = [sb([P, HALF], U8, "g_scales%d" % h) for h in halves]
        early = [sb([P, CHUNK * PACK], BF16, "g_early%d" % k) for k in range(2)]

        def weave(engine, target, k):
            woven = target.rearrange("p (c i t) -> p c t i", i=4, t=PACK)
            source = planes[k].rearrange("p t (c i) -> p c t i", i=4)
            engine.tensor_tensor(woven, source, x[:, :, chunk(k)].rearrange("p t (c i) -> p c t i", i=4), MULT)

        both = [sb([P, C], F32, "es%d" % j, tag) for j, tag in enumerate(("z5", "z6"))]
        for h in halves:
            gather_e(0, 2 * h, 2, both[0][:, half(h)], True)
        gather_e(2, 0, 2, sb([P, HALF], F32, "es2_0")[:], False)
        for h in halves:
            add_pairs(0, h, 0)
        add_pairs(2, 0, 1)
        for h in halves:
            gather_e(1, 2 * h, 2, both[1][:, half(h)], True)
        gather_e(2, 3, 1, sb([P, CHUNK], F32, "es2_3")[:], True)
        for h in halves:
            gather_e(3, 2 * h, 2, sb([P, HALF], F32, "es3_%d" % h)[:], True)
        for h in halves:
            add_pairs(1, h, 2)
        root(0)
        root(2, 0, chunk(0))
        gather_e(2, 2, 1, sb([P, CHUNK], F32, "es2_2", "z5")[:], False)
        form_h(0, 3)
        add_pairs(2, 1, 1)
        root(1)
        root(2, 1, chunk(1))
        form_h(1, 4)
        form_h(2, 5)
        form_x(3, 1)
        zero_window(2, "factor3")
        add_pairs(3, 0, 1)
        root_last(0)
        add_pairs(3, 1, 4)
        h_win[3] = sb([P, X], F32, "h3")
        root_last(1)
        for h in halves:
            square_last(h)
        for k in range(3):
            gather_h(k, 0, True)
        form_h_last(0, 6)
        form_h_last(1, 7)
        gather_h(2, 1, True)
        for k, j in ((0, 1), (1, 1), (0, 2), (1, 2), (0, 3), (1, 3), (2, 2), (2, 3)):
            gather_h(k, j, (k, j) == (0, 3))
        for k in range(2):
            weave(nc.vector, early[k][:], k)
        for k in range(2):
            nc.vector.quantize_mx(g_codes[0][:, chunk(k)].bitcast(E5M2), g_scales[0][:, chunk(k)], early[k][:])
        for j in r_tiles:
            gather_h(3, j, j < 2)
        late = sb([P, HALF * PACK], BF16, "g_late", "g_early1")
        for k in range(2):
            weave(nc.gpsimd, late[:, k * CHUNK * PACK : (k + 1) * CHUNK * PACK], 2 + k)
        nc.vector.quantize_mx(g_codes[1][:].bitcast(E5M2), g_scales[1][:], late[:])
        zero_window(1, "g_early1")

        dw = [gathered[:, :C] if j == 1 else sb([P, C], F32, "dw%d" % j, "e%d" % j)[:] for j in r_tiles]

        def form_dw(j, first, count, n, on_vector):
            bank = bank_tile(n, [P, count], "dw_bank")
            rows = slice(j * P, (j + 1) * P)
            h, cols = first // HALF, slice(first % HALF, first % HALF + count)
            nc.tensor.matmul_mx(
                bank[:],
                lhsT=qb_codes[:, rows].bitcast(E4M3),
                lhsT_scale=qb_scales[:, rows],
                rhs=g_codes[h][:, cols].bitcast(E5M2),
                rhs_scale=g_scales[h][:, cols],
                start=True,
                stop=True,
            )
            if on_vector:
                nc.vector.tensor_copy(dw[j][:, first : first + count], bank[:])
            else:
                nc.scalar.copy(dw[j][:, first : first + count], bank[:])

        out_rows = out.rearrange("(p j) t -> p j t", j=PACK)

        def put_dw(j, first, count):
            window = out_win[j][:].indirect(entries(idx, first, count))
            if j < 2:
                nc.vector.tensor_copy(window, dw[j][:, first : first + count])
            else:
                nc.scalar.activation(window, dw[j][:, first : first + count], ACT.Copy)
            if first + count == C:
                (nc.scalar if j == 3 else nc.sync).dma_start(out_rows[:, j, :], out_win[j][:])

        form_dw(2, 0, CHUNK, 0, False)
        put_dw(2, 0, CHUNK)
        form_dw(0, 0, HALF, 1, True)
        form_dw(2, CHUNK, CHUNK, 2, False)
        form_dw(3, 0, HALF, 3, True)
        put_dw(0, 0, HALF)
        put_dw(3, 0, CHUNK)
        put_dw(2, CHUNK, CHUNK)
        put_dw(3, CHUNK, CHUNK)
        for j, h, n in ((1, 0, 4), (0, 1, 5), (1, 1, 6)):
            form_dw(j, h * HALF, HALF, n, True)
        form_dw(2, HALF, HALF, 7, False)
        put_dw(0, HALF, HALF)
        put_dw(2, 2 * CHUNK, CHUNK)
        form_dw(3, HALF, HALF, 0, False)
        put_dw(2, 3 * CHUNK, CHUNK)
        put_dw(1, 0, C)
        for k in (2, 3):
            put_dw(3, k * CHUNK, CHUNK)
